import numpy as np
import ml_dtypes


def mxq(x, axis, fmt="e4m3"):
    dtype, down = {"e4m3": (ml_dtypes.float8_e4m3fn, 7), "e5m2": (ml_dtypes.float8_e5m2, 14)}[fmt]
    v = np.moveaxis(np.asarray(x, np.float32).astype(ml_dtypes.bfloat16).astype(np.float64), axis, -1)
    blocks = v.reshape(v.shape[:-1] + (-1, 32))
    amax = np.abs(blocks).max(-1, keepdims=True)
    byte = np.maximum(np.where(amax > 0, np.frexp(amax)[1] - 1 + 127, 0) - down, 1)
    scale = np.exp2(byte - 127.0)
    codes = (blocks / scale).astype(np.float32).astype(dtype).astype(np.float64)
    return np.moveaxis((codes * scale).reshape(v.shape), -1, axis)


WIDE = False


def mx_kscale(k):
    if not WIDE:
        return np.ones(k)
    levels = np.array([30, -30])
    if k % 512:
        return np.exp2(np.random.permutation(np.resize(levels, k // 32))).repeat(32)
    a = np.empty((k // 512, 16))
    for p in range(k // 512):
        a[p, :8] = np.random.permutation(np.resize(levels, 8))
        for g in range(8):
            far = levels[np.abs(levels - a[p, g]) >= 10]
            a[p, g + 8] = far[np.random.randint(len(far))]
    return np.exp2(a.ravel()).repeat(32)


BF16 = ml_dtypes.bfloat16


def bf(x):
    return np.asarray(x, np.float32).astype(BF16)


def f64(x):
    return np.asarray(x).astype(np.float64)


E2M1 = np.array([0.0, 0.5, 1.0, 1.5, 2.0, 3.0, 4.0, 6.0, -0.0, -0.5, -1.0, -1.5, -2.0, -3.0, -4.0, -6.0])


def pack_weight(w, fmt):
    k, n = w.shape
    w = f64(bf(w)).reshape(k // 32, 32, n)
    amax = np.abs(w).max(1)
    if fmt in ("e4m3", "e5m2"):
        byte = np.frexp(amax)[1] - 1 + 127 - (7 if fmt == "e4m3" else 14)
    else:
        mant, ex = np.frexp(amax / 6.0)
        byte = np.where(mant > 0.5, ex, ex - 1) + 127
    byte = np.clip(np.where(amax > 0, byte, 1), 1, 254)
    scaled = (w * np.exp2(127.0 - byte)[:, None, :]).reshape(k, n).astype(np.float32)
    by_word = np.ascontiguousarray(scaled.reshape(k // 512, 128, 4, n).transpose(0, 1, 3, 2))
    if fmt in ("e4m3", "e5m2"):
        words = by_word.astype(ml_dtypes.float8_e4m3fn if fmt == "e4m3" else ml_dtypes.float8_e5m2).view(np.uint8)
    else:
        c = by_word.astype(ml_dtypes.float4_e2m1fn).view(np.uint8) & 0xF
        words = c[..., 0::2] | (c[..., 1::2] << 4)
    return np.ascontiguousarray(words), np.ascontiguousarray(byte.astype(np.uint8).reshape(k // 512, 16, n))


def unpack_weight(words, scales, fmt):
    g, p, n, _ = words.shape
    if fmt in ("e4m3", "e5m2"):
        vals = np.ascontiguousarray(words).view(ml_dtypes.float8_e4m3fn if fmt == "e4m3" else ml_dtypes.float8_e5m2).astype(np.float64)
    else:
        nib = np.empty((g, p, n, 4), np.uint8)
        nib[..., 0::2] = words & 0xF
        nib[..., 1::2] = words >> 4
        vals = E2M1[nib]
    vals = vals * np.repeat(np.exp2(scales.astype(np.float64) - 127.0), 8, axis=1)[..., None]
    return vals.transpose(0, 1, 3, 2).reshape(g * 512, n)


K, N, R, S = 2048, 1024, 1024, 2048


def setup_inputs():
    s = mx_kscale(K)
    t = mx_kscale(R)
    G = np.random.standard_normal((K, N)) * np.exp(0.5 * np.random.standard_normal((K, N)))
    innov_words, innov_scales = pack_weight(G * s[:, None], "e5m2")
    return {
        "innov_words": innov_words,
        "innov_scales": innov_scales,
        "obs_modes": bf(np.random.standard_normal((K, R)) / np.sqrt(K) / s[:, None] * t),
        "mode_ratio": bf(np.random.uniform(0.2, 4.0, R)),
        "state_modes": bf(np.random.standard_normal((S, R)) / np.sqrt(R) / t),
    }


def reference(innov_words, innov_scales, obs_modes, mode_ratio, state_modes):
    G = unpack_weight(innov_words, innov_scales, "e5m2")
    U = mxq(f64(obs_modes), 0, "e4m3")
    z = U.T @ G
    r = f64(mode_ratio)
    gain = r / (1.0 + r * r)
    h = mxq(z * gain[:, None], 0, "e5m2")
    V = mxq(f64(state_modes), 1, "e4m3")
    return V @ h

@@ -1,0 +1,358 @@
+from contextlib import ExitStack
+
+import concourse.mybir as mybir
+from concourse.masks import make_identity
+
+K, N, R, S = 2048, 1024, 1024, 2048
+FLOPS = 2 * K * R * N + 2 * S * R * N
+
+F32 = mybir.dt.float32
+BF16 = mybir.dt.bfloat16
+U32 = mybir.dt.uint32
+I32 = mybir.dt.int32
+U8 = mybir.dt.uint8
+E4 = mybir.dt.float8_e4m3fn_x4
+E5 = mybir.dt.float8_e5m2_x4
+COPY = mybir.ActivationFunctionType.Copy
+MULT = mybir.AluOpType.mult
+
+P = 128
+KG = K // 512
+ST = S // P
+SP = ST // 2
+U_CUT = 88
+H_CUT = 256
+WARM = 12
+
+
+def tile_factored_gain_correction_e3_kernel(tc, innov_words, innov_scales, obs_modes, mode_ratio, state_modes, out):
+    nc = tc.nc
+    v_rows = state_modes.rearrange("(p a) r -> p a r", a=ST)
+    out_rows = out.rearrange("(p a) n -> p a n", a=ST)
+
+    with ExitStack() as ctx:
+        keep = ctx.enter_context(tc.tile_pool(name="keep", bufs=1))
+        work = ctx.enter_context(tc.tile_pool(name="work", bufs=2))
+        psum = ctx.enter_context(tc.psum_pool(name="psum", bufs=1))
+        ctx.enter_context(tc.manual_schedule())
+
+        def bank(b):
+            return psum.tile([P, 512], F32, name="bank%d" % b, tag="bank%d" % b)
+
+        ident = keep.tile([P, P], F32, name="ident", align_bytes=64)
+        ratio = keep.tile([P, 2, 4], BF16, name="ratio")
+        square = keep.tile([P, 8], F32, name="square")
+        gain = keep.tile([P, 8], F32, name="gain")
+        g_words = [keep.tile([P, N], U32, name="g_words%d" % g, align_bytes=64) for g in range(KG)]
+        g_scales = keep.tile([P, KG, N], U8, name="g_scales", align_bytes=64)
+        u_raw = {(g, r): keep.tile([P, 4, 512], BF16, name="u_raw%d_%d" % (g, r), align_bytes=64) for g in range(KG) for r in range(2)}
+        u_codes = {k: keep.tile([P, 512], U32, name="u_codes%d_%d" % k, align_bytes=64) for k in u_raw}
+        u_scales = {k: keep.tile([P, 512], U8, name="u_scales%d_%d" % k, align_bytes=64) for k in u_raw}
+        v_raw = [keep.tile([P, 2, R], BF16, name="v_raw%d" % q, align_bytes=64) for q in range(SP)]
+        v_codes = [keep.tile([P, 512], U32, name="v_codes%d" % q, align_bytes=64) for q in range(SP)]
+        v_scales = [keep.tile([P, 512], U8, name="v_scales%d" % q, align_bytes=64) for q in range(SP)]
+        h_codes = {(r, n): keep.tile([P, 512], U32, name="h_codes%d_%d" % (r, n), align_bytes=64) for r in range(2) for n in range(2)}
+        h_scales = {k: keep.tile([P, 512], U8, name="h_scales%d_%d" % k, align_bytes=64) for k in h_codes}
+
+        nc.vector.memset(g_scales[:].rearrange("p g n -> p (g n)").bitcast(I32), 0)
+        nc.scalar.dma_start(out=ratio[:], in_=mode_ratio.rearrange("(g p t) -> p g t", g=2, t=4))
+        for q in range(4):
+            nc.scalar.dma_start(
+                out=g_scales[32 * q : 32 * q + 4, :, :].bitcast(I32),
+                in_=innov_scales[:, 4 * q : 4 * q + 4, :].rearrange("g q n -> q g n").bitcast(I32),
+            )
+
+        def load_u(g, r):
+            rows = obs_modes[512 * g : 512 * (g + 1), 512 * r : 512 * (r + 1)]
+            nc.sync.dma_start(out=u_raw[g, r][:], in_=rows.rearrange("(p j) w -> p j w", j=4))
+
+        def load_w(g):
+            nc.sync.dma_start(out=g_words[g][:].bitcast(I32), in_=innov_words[g].rearrange("p n t -> p (n t)").bitcast(I32))
+
+        def load_v(q):
+            nc.sync.dma_start(out=v_raw[q][:], in_=v_rows[:, 2 * q : 2 * q + 2, :])
+
+        load_u(0, 0)
+        load_w(0)
+        for g in range(1, KG):
+            load_u(g, 0)
+            if g > 1:
+                load_w(g - 1)
+        load_u(0, 1)
+        load_w(KG - 1)
+        for g in range(1, KG):
+            load_u(g, 1)
+        for q in range(SP):
+            load_v(q)
+
+        zeros = keep.tile([P, 2048], BF16, name="zeros", align_bytes=64)
+        warm_moving = keep.tile([P, 512], U32, name="warm_moving", align_bytes=64)
+        warm_moving_scales = keep.tile([P, 512], U8, name="warm_moving_scales", align_bytes=64)
+        warm_stationary = keep.tile([P, P], U32, name="warm_stationary", align_bytes=64)
+        warm_stationary_scales = keep.tile([P, P], U8, name="warm_stationary_scales", align_bytes=64)
+        nc.gpsimd.memset(zeros[:].bitcast(U32), 0)
+        make_identity(nc, ident[:])
+        nc.vector.quantize_mx(out=warm_moving[:].bitcast(E5), scales=warm_moving_scales[:], in_=zeros[:])
+        nc.vector.quantize_mx(out=warm_stationary[:].bitcast(E4), scales=warm_stationary_scales[:], in_=zeros[:, 0:512])
+        idle = bank(7)
+        for i in range(WARM):
+            nc.tensor.matmul_mx(
+                out=idle[:],
+                lhsT=warm_stationary[:].bitcast(E4),
+                lhsT_scale=warm_stationary_scales[:],
+                rhs=warm_moving[:].bitcast(E5),
+                rhs_scale=warm_moving_scales[:],
+                start=True,
+                stop=True,
+            )
+
+        def make_gain():
+            flat = ratio[:].rearrange("p g t -> p (g t)")
+            nc.vector.tensor_tensor(out=square[:], in0=flat, in1=flat, op=MULT)
+            nc.vector.tensor_scalar_add(square[:], square[:], 1.0)
+            nc.vector.reciprocal(square[:], square[:])
+            nc.vector.tensor_tensor(out=gain[:], in0=flat, in1=square[:], op=MULT)
+
+        v_group = {}
+
+        v_words = {}
+
+        def order_v(q, engine):
+            v_words[q] = work.tile([P, 2, 2, 2, P], F32, name="v_words", tag="v_words", bufs=2, align_bytes=64)
+            src = v_raw[q][:].rearrange("p i r -> p (i r)").bitcast(F32).rearrange("p (x m u) -> p x u m", x=4, u=2)
+            dst = v_words[q][:].rearrange("p i g u m -> p (i g) u m")
+            if engine == "s":
+                nc.scalar.copy(out=dst, in_=src)
+            else:
+                nc.vector.tensor_copy(out=dst, in_=src)
+
+        def transpose_v(a, b):
+            t = bank(b)
+            if a // 2 in v_words:
+                ordered = v_words[a // 2][:, a % 2].rearrange("p g u m -> p (g u m)")
+                for c in range(4):
+                    cols = slice(128 * c, 128 * (c + 1))
+                    nc.tensor.transpose(t[:, cols], ordered[:, cols], ident[:])
+                return t
+            words = v_raw[a // 2][:, a % 2, :].bitcast(F32)
+            for g in range(2):
+                for u in range(2):
+                    c = 2 * g + u
+                    nc.tensor.transpose(t[:, 128 * c : 128 * (c + 1)], words[:, 256 * g + u : 256 * (g + 1) : 2], ident[:])
+            return t
+
+        def empty_v(a, t, engine):
+            q = a // 2
+            if q not in v_group:
+                v_group[q] = work.tile([P, 2, 2, P, 4], BF16, name="v_group", tag="v_group", bufs=3, align_bytes=64)
+            dst = v_group[q][:, a % 2].rearrange("p g s t -> p g (s t)").bitcast(F32).rearrange("p g (s u) -> p g s u", u=2)
+            src = t[:].rearrange("p (g u s) -> p g s u", g=2, u=2)
+            if engine == "s":
+                nc.scalar.copy(out=dst, in_=src)
+            else:
+                nc.vector.tensor_copy(out=dst, in_=src)
+
+        def quantize_v(q):
+            nc.vector.quantize_mx(out=v_codes[q][:].bitcast(E4), scales=v_scales[q][:], in_=v_group[q][:].rearrange("p i g s t -> p (i g s t)"))
+
+        u_group = {}
+
+        def group_u(g, r):
+            u_group[g, r] = work.tile([P, 4, P, 4], BF16, name="u_group", tag="u_group", bufs=4, align_bytes=64)
+            src = u_raw[g, r][:].rearrange("p j (m t) -> p m j t", t=4)
+            dst = u_group[g, r][:].rearrange("p t m j -> p m j t")
+            nc.vector.tensor_copy(out=dst[:, 0:U_CUT], in_=src[:, 0:U_CUT])
+            nc.scalar.copy(out=dst[:, U_CUT:P], in_=src[:, U_CUT:P])
+
+        def quantize_u(g, r):
+            nc.vector.quantize_mx(out=u_codes[g, r][:].bitcast(E4), scales=u_scales[g, r][:], in_=u_group[g, r][:].rearrange("p t m j -> p (t m j)"))
+
+        z = {}
+
+        def stage1(g, r, n, base, tiles=range(4)):
+            cols = slice(512 * n, 512 * (n + 1))
+            for t in tiles:
+                if g == 0:
+                    z[r, n, t] = bank(base + t)
+                m = slice(128 * t, 128 * (t + 1))
+                nc.tensor.matmul_mx(
+                    out=z[r, n, t][:],
+                    lhsT=u_codes[g, r][:, m].bitcast(E4),
+                    lhsT_scale=u_scales[g, r][:, m],
+                    rhs=g_words[g][:, cols].bitcast(E5),
+                    rhs_scale=g_scales[:, g, cols],
+                    start=(g == 0),
+                    stop=(g == KG - 1),
+                )
+
+        h_rows = {}
+        h_group = {}
+
+        def empty_z(r, n, t, engine):
+            if (r, n) not in h_rows:
+                h_rows[r, n] = work.tile([P, 4, 512], BF16, name="h_rows", tag="h_rows", bufs=3, align_bytes=64)
+            scale = gain[:, 4 * r + t : 4 * r + t + 1]
+            if engine == "s":
+                nc.scalar.activation(out=h_rows[r, n][:, t, :], in_=z[r, n, t][:], func=COPY, scale=scale)
+            else:
+                nc.vector.tensor_scalar_mul(h_rows[r, n][:, t, :], z[r, n, t][:], scale)
+
+        def group_h(r, n):
+            h_group[r, n] = work.tile([P, 512, 4], BF16, name="h_group", tag="h_group", bufs=2, align_bytes=64)
+            src = h_rows[r, n][:].rearrange("p t (c i) -> p c t i", i=4)
+            dst = h_group[r, n][:].rearrange("p (c i) t -> p c t i", i=4)
+            cut = H_CUT // 4
+            nc.vector.tensor_copy(out=dst[:, 0:cut], in_=src[:, 0:cut])
+            nc.scalar.copy(out=dst[:, cut:P], in_=src[:, cut:P])
+
+        def quantize_h(r, n):
+            nc.vector.quantize_mx(out=h_codes[r, n][:].bitcast(E5), scales=h_scales[r, n][:], in_=h_group[r, n][:].rearrange("p n t -> p (n t)"))
+
+        def stage2(a, n, b):
+            q, i = a // 2, a % 2
+            acc = bank(b)
+            for r in range(2):
+                m = slice(256 * i + 128 * r, 256 * i + 128 * (r + 1))
+                nc.tensor.matmul_mx(
+                    out=acc[:],
+                    lhsT=v_codes[q][:, m].bitcast(E4),
+                    lhsT_scale=v_scales[q][:, m],
+                    rhs=h_codes[r, n][:].bitcast(E5),
+                    rhs_scale=h_scales[r, n][:],
+                    start=(r == 0),
+                    stop=(r == 1),
+                )
+            return acc
+
+        results = {}
+
+        def empty_out(a, n, acc, engine, lo=0, hi=512):
+            if a not in results:
+                results[a] = work.tile([P, 1, N], F32, name="result", tag="result", bufs=6, align_bytes=64)
+            dst = results[a][:, 0, 512 * n + lo : 512 * n + hi]
+            if engine == "s":
+                nc.scalar.copy(out=dst, in_=acc[:, lo:hi])
+            else:
+                nc.vector.tensor_copy(out=dst, in_=acc[:, lo:hi])
+
+        def store(a):
+            nc.sync.dma_start(out=out_rows[:, a : a + 1, :], in_=results[a][:])
+
+        t = {}
+
+        def stage1_pair(g, r):
+            stage1(g, r, 0, 0)
+            stage1(g, r, 1, 4)
+
+        u_group[0, 0] = work.tile([P, 4, P, 4], BF16, name="u_group", tag="u_group", bufs=4, align_bytes=64)
+        src = u_raw[0, 0][:].rearrange("p j (m t) -> p m j t", t=4)
+        dst = u_group[0, 0][:].rearrange("p t m j -> p m j t")
+        nc.vector.tensor_copy(out=dst[:, :, :, 0:2], in_=src[:, :, :, 0:2])
+        nc.scalar.copy(out=dst[:, :, :, 2:4], in_=src[:, :, :, 2:4])
+        for half in range(2):
+            cols = slice(256 * half, 256 * (half + 1))
+            nc.vector.quantize_mx(
+                out=u_codes[0, 0][:, cols].bitcast(E4),
+                scales=u_scales[0, 0][:, cols],
+                in_=u_group[0, 0][:, 2 * half : 2 * half + 2].rearrange("p t m j -> p (t m j)"),
+            )
+            for n in range(2):
+                stage1(0, 0, n, 4 * n, (2 * half, 2 * half + 1))
+        for g in range(1, KG):
+            group_u(g, 0)
+            if g > 1:
+                stage1_pair(g - 1, 0)
+            if g == 2:
+                make_gain()
+            quantize_u(g, 0)
+        group_u(0, 1)
+        stage1(3, 0, 1, 4)
+        stage1(3, 0, 0, 0)
+        empty_z(0, 1, 0, "s")
+        quantize_u(0, 1)
+        empty_z(0, 1, 2, "s")
+        empty_z(0, 1, 1, "v")
+        group_u(1, 1)
+        empty_z(0, 1, 3, "s")
+        quantize_u(1, 1)
+        stage1(0, 1, 1, 4)
+        stage1(1, 1, 1, 4)
+        empty_z(0, 0, 0, "s")
+        empty_z(0, 0, 1, "v")
+        empty_z(0, 0, 2, "s")
+        group_u(2, 1)
+        empty_z(0, 0, 3, "s")
+        quantize_u(2, 1)
+        group_u(3, 1)
+        quantize_u(3, 1)
+        for g in range(KG):
+            stage1(g, 1, 0, 0)
+        group_h(0, 0)
+        group_h(0, 1)
+        for g in range(2, KG):
+            stage1(g, 1, 1, 4)
+        quantize_h(0, 0)
+        order_v(0, "v")
+        for j in range(3):
+            empty_z(1, 0, j, "s")
+        empty_z(1, 0, 3, "v")
+        order_v(1, "v")
+        quantize_h(0, 1)
+        group_h(1, 0)
+        for j in range(4):
+            empty_z(1, 1, j, "svsv"[j])
+        for a in range(4):
+            t[a] = transpose_v(a, a)
+        quantize_h(1, 0)
+        for a in range(4, 8):
+            t[a] = transpose_v(a, a)
+        empty_v(0, t[0], "s")
+        empty_v(1, t[1], "s")
+        group_h(1, 1)
+        quantize_v(0)
+        empty_v(2, t[2], "v")
+        empty_v(3, t[3], "s")
+        quantize_h(1, 1)
+        quantize_v(1)
+        empty_v(4, t[4], "s")
+        empty_v(5, t[5], "v")
+
+        def finish(a, n, engine, b):
+            acc = stage2(a, n, b)
+            empty_out(a, n, acc, engine)
+
+        for i in range(4):
+            for n in range(2):
+                finish(i, n, "sv"[n], (2 * i + n) % 4)
+            store(i)
+            if i == 0:
+                quantize_v(2)
+                empty_v(6, t[6], "s")
+            if i == 1:
+                empty_v(7, t[7], "s")
+                order_v(4, "v")
+            if i == 2:
+                quantize_v(3)
+        for q in range(4, SP):
+            ts = (2 * q, 2 * q + 1)
+            for a in ts:
+                t[a] = transpose_v(a, 4 + a % 4)
+                empty_v(a, t[a], "s")
+            for i in range(2):
+                a = 2 * q - 4 + i
+                for n in range(2):
+                    finish(a, n, "vs"[n], (2 * a + n) % 4)
+                store(a)
+                if i == 0 and q + 1 < SP:
+                    order_v(q + 1, "v")
+            quantize_v(q)
+        for a in range(ST - 4, ST - 1):
+            for n in range(2):
+                finish(a, n, "sv"[n], (2 * a + n) % 8)
+            store(a)
+        last = ST - 1
+        for n in range(2):
+            acc = stage2(last, n, 6 + n)
+            empty_out(last, n, acc, "s", 0, 256)
+            empty_out(last, n, acc, "v", 256, 512)
+            nc.sync.dma_start(out=out_rows[:, last : ST, 512 * n : 512 * (n + 1)], in_=results[last][:, 0:1, 512 * n : 512 * (n + 1)])

@@ -20,9 +20,7 @@ P = 128
 KG = K // 512
 ST = S // P
 SP = ST // 2
-U_CUT = 88
-H_CUT = 256
-WARM = 12
+RESULT_BUFS = 8
 
 
 def tile_factored_gain_correction_e3_kernel(tc, innov_words, innov_scales, obs_modes, mode_ratio, state_modes, out):
@@ -39,15 +37,22 @@ def tile_factored_gain_correction_e3_kernel(tc, innov_words, innov_scales, obs_m
         def bank(b):
             return psum.tile([P, 512], F32, name="bank%d" % b, tag="bank%d" % b)
 
+        used = []
+
+        def next_bank():
+            used.append(len(used) % 8)
+            return bank(used[-1])
+
         ident = keep.tile([P, P], F32, name="ident", align_bytes=64)
         ratio = keep.tile([P, 2, 4], BF16, name="ratio")
+        ratio32 = keep.tile([P, 8], F32, name="ratio32")
         square = keep.tile([P, 8], F32, name="square")
         gain = keep.tile([P, 8], F32, name="gain")
-        g_words = [keep.tile([P, N], U32, name="g_words%d" % g, align_bytes=64) for g in range(KG)]
+        g_words = {(g, n): keep.tile([P, 512], U32, name="g_words%d_%d" % (g, n), align_bytes=64) for g in range(KG) for n in range(2)}
         g_scales = keep.tile([P, KG, N], U8, name="g_scales", align_bytes=64)
-        u_raw = {(g, r): keep.tile([P, 4, 512], BF16, name="u_raw%d_%d" % (g, r), align_bytes=64) for g in range(KG) for r in range(2)}
-        u_codes = {k: keep.tile([P, 512], U32, name="u_codes%d_%d" % k, align_bytes=64) for k in u_raw}
-        u_scales = {k: keep.tile([P, 512], U8, name="u_scales%d_%d" % k, align_bytes=64) for k in u_raw}
+        u_raw = [keep.tile([P, 4, R], BF16, name="u_raw%d" % g, align_bytes=64) for g in range(KG)]
+        u_codes = {(g, r): keep.tile([P, 512], U32, name="u_codes%d_%d" % (g, r), align_bytes=64) for g in range(KG) for r in range(2)}
+        u_scales = {k: keep.tile([P, 512], U8, name="u_scales%d_%d" % k, align_bytes=64) for k in u_codes}
         v_raw = [keep.tile([P, 2, R], BF16, name="v_raw%d" % q, align_bytes=64) for q in range(SP)]
         v_codes = [keep.tile([P, 512], U32, name="v_codes%d" % q, align_bytes=64) for q in range(SP)]
         v_scales = [keep.tile([P, 512], U8, name="v_scales%d" % q, align_bytes=64) for q in range(SP)]
@@ -56,134 +61,104 @@ def tile_factored_gain_correction_e3_kernel(tc, innov_words, innov_scales, obs_m
 
         nc.vector.memset(g_scales[:].rearrange("p g n -> p (g n)").bitcast(I32), 0)
         nc.scalar.dma_start(out=ratio[:], in_=mode_ratio.rearrange("(g p t) -> p g t", g=2, t=4))
-        for q in range(4):
-            nc.scalar.dma_start(
-                out=g_scales[32 * q : 32 * q + 4, :, :].bitcast(I32),
-                in_=innov_scales[:, 4 * q : 4 * q + 4, :].rearrange("g q n -> q g n").bitcast(I32),
-            )
 
-        def load_u(g, r):
-            rows = obs_modes[512 * g : 512 * (g + 1), 512 * r : 512 * (r + 1)]
-            nc.sync.dma_start(out=u_raw[g, r][:], in_=rows.rearrange("(p j) w -> p j w", j=4))
+        def load_scales():
+            scale_rows = innov_scales.rearrange("g (q j) n -> j q g n", j=4)
+            for j in range(4):
+                nc.sync.dma_start(out=g_scales[j:P:32, :, :].bitcast(I32), in_=scale_rows[j].bitcast(I32))
 
-        def load_w(g):
-            nc.sync.dma_start(out=g_words[g][:].bitcast(I32), in_=innov_words[g].rearrange("p n t -> p (n t)").bitcast(I32))
+        def load_u(g):
+            nc.sync.dma_start(out=u_raw[g][:], in_=obs_modes[512 * g : 512 * (g + 1), :].rearrange("(p j) w -> p j w", j=4))
+
+        def load_w(g, n):
+            words = innov_words[g][:, 512 * n : 512 * (n + 1), :].rearrange("p n t -> p (n t)")
+            nc.sync.dma_start(out=g_words[g, n][:].bitcast(I32), in_=words.bitcast(I32))
 
         def load_v(q):
             nc.sync.dma_start(out=v_raw[q][:], in_=v_rows[:, 2 * q : 2 * q + 2, :])
 
-        load_u(0, 0)
-        load_w(0)
-        for g in range(1, KG):
-            load_u(g, 0)
-            if g > 1:
-                load_w(g - 1)
-        load_u(0, 1)
-        load_w(KG - 1)
-        for g in range(1, KG):
-            load_u(g, 1)
+        for g in range(KG):
+            load_u(g)
+            load_w(g, 0)
+            if g == 0:
+                load_scales()
+        for g in range(KG):
+            load_w(g, 1)
         for q in range(SP):
             load_v(q)
 
-        zeros = keep.tile([P, 2048], BF16, name="zeros", align_bytes=64)
-        warm_moving = keep.tile([P, 512], U32, name="warm_moving", align_bytes=64)
-        warm_moving_scales = keep.tile([P, 512], U8, name="warm_moving_scales", align_bytes=64)
-        warm_stationary = keep.tile([P, P], U32, name="warm_stationary", align_bytes=64)
-        warm_stationary_scales = keep.tile([P, P], U8, name="warm_stationary_scales", align_bytes=64)
-        nc.gpsimd.memset(zeros[:].bitcast(U32), 0)
         make_identity(nc, ident[:])
-        nc.vector.quantize_mx(out=warm_moving[:].bitcast(E5), scales=warm_moving_scales[:], in_=zeros[:])
-        nc.vector.quantize_mx(out=warm_stationary[:].bitcast(E4), scales=warm_stationary_scales[:], in_=zeros[:, 0:512])
-        idle = bank(7)
-        for i in range(WARM):
-            nc.tensor.matmul_mx(
-                out=idle[:],
-                lhsT=warm_stationary[:].bitcast(E4),
-                lhsT_scale=warm_stationary_scales[:],
-                rhs=warm_moving[:].bitcast(E5),
-                rhs_scale=warm_moving_scales[:],
-                start=True,
-                stop=True,
-            )
 
-        def make_gain():
-            flat = ratio[:].rearrange("p g t -> p (g t)")
-            nc.vector.tensor_tensor(out=square[:], in0=flat, in1=flat, op=MULT)
-            nc.vector.tensor_scalar_add(square[:], square[:], 1.0)
-            nc.vector.reciprocal(square[:], square[:])
-            nc.vector.tensor_tensor(out=gain[:], in0=flat, in1=square[:], op=MULT)
+        nc.scalar.activation(out=ratio32[:], in_=ratio[:].rearrange("p g t -> p (g t)"), func=COPY)
+        nc.vector.tensor_tensor(out=square[:], in0=ratio32[:], in1=ratio32[:], op=MULT)
+        nc.vector.tensor_scalar_add(square[:], square[:], 1.0)
+        nc.vector.reciprocal(square[:], square[:])
+        nc.vector.tensor_tensor(out=gain[:], in0=ratio32[:], in1=square[:], op=MULT)
 
-        v_group = {}
+        def copy(engine, out, in_):
+            if engine == "s":
+                nc.scalar.copy(out=out, in_=in_)
+            else:
+                nc.vector.tensor_copy(out=out, in_=in_)
 
         v_words = {}
+        v_group = {}
+        v_bank = {}
 
-        def order_v(q, engine):
-            v_words[q] = work.tile([P, 2, 2, 2, P], F32, name="v_words", tag="v_words", bufs=2, align_bytes=64)
+        def order_v(q):
+            v_words[q] = work.tile([P, 2, 2, 2, P], F32, name="v_words", tag="v_words", bufs=3, align_bytes=64)
             src = v_raw[q][:].rearrange("p i r -> p (i r)").bitcast(F32).rearrange("p (x m u) -> p x u m", x=4, u=2)
-            dst = v_words[q][:].rearrange("p i g u m -> p (i g) u m")
-            if engine == "s":
-                nc.scalar.copy(out=dst, in_=src)
-            else:
-                nc.vector.tensor_copy(out=dst, in_=src)
+            copy("v", v_words[q][:].rearrange("p i g u m -> p (i g) u m"), src)
 
-        def transpose_v(a, b):
-            t = bank(b)
-            if a // 2 in v_words:
-                ordered = v_words[a // 2][:, a % 2].rearrange("p g u m -> p (g u m)")
-                for c in range(4):
-                    cols = slice(128 * c, 128 * (c + 1))
-                    nc.tensor.transpose(t[:, cols], ordered[:, cols], ident[:])
-                return t
-            words = v_raw[a // 2][:, a % 2, :].bitcast(F32)
-            for g in range(2):
-                for u in range(2):
-                    c = 2 * g + u
-                    nc.tensor.transpose(t[:, 128 * c : 128 * (c + 1)], words[:, 256 * g + u : 256 * (g + 1) : 2], ident[:])
-            return t
+        def transpose_v(a):
+            v_bank[a] = next_bank()
+            ordered = v_words[a // 2][:, a % 2].rearrange("p g u m -> p (g u m)")
+            for c in range(4):
+                cols = slice(128 * c, 128 * (c + 1))
+                nc.tensor.transpose(v_bank[a][:, cols], ordered[:, cols], ident[:])
 
-        def empty_v(a, t, engine):
+        def empty_v(a, engine):
             q = a // 2
             if q not in v_group:
                 v_group[q] = work.tile([P, 2, 2, P, 4], BF16, name="v_group", tag="v_group", bufs=3, align_bytes=64)
             dst = v_group[q][:, a % 2].rearrange("p g s t -> p g (s t)").bitcast(F32).rearrange("p g (s u) -> p g s u", u=2)
-            src = t[:].rearrange("p (g u s) -> p g s u", g=2, u=2)
-            if engine == "s":
-                nc.scalar.copy(out=dst, in_=src)
-            else:
-                nc.vector.tensor_copy(out=dst, in_=src)
+            copy(engine, dst, v_bank[a][:].rearrange("p (g u s) -> p g s u", g=2, u=2))
 
         def quantize_v(q):
             nc.vector.quantize_mx(out=v_codes[q][:].bitcast(E4), scales=v_scales[q][:], in_=v_group[q][:].rearrange("p i g s t -> p (i g s t)"))
 
         u_group = {}
 
-        def group_u(g, r):
-            u_group[g, r] = work.tile([P, 4, P, 4], BF16, name="u_group", tag="u_group", bufs=4, align_bytes=64)
-            src = u_raw[g, r][:].rearrange("p j (m t) -> p m j t", t=4)
+        def group_u(g, r, engine, rows, slots=slice(0, 4)):
+            if (g, r) not in u_group:
+                u_group[g, r] = work.tile([P, 4, P, 4], BF16, name="u_group", tag="u_group", bufs=3, align_bytes=64)
+            src = u_raw[g][:, :, 512 * r : 512 * (r + 1)].rearrange("p j (m t) -> p m j t", t=4)
             dst = u_group[g, r][:].rearrange("p t m j -> p m j t")
-            nc.vector.tensor_copy(out=dst[:, 0:U_CUT], in_=src[:, 0:U_CUT])
-            nc.scalar.copy(out=dst[:, U_CUT:P], in_=src[:, U_CUT:P])
+            copy(engine, dst[:, rows, :, slots], src[:, rows, :, slots])
 
-        def quantize_u(g, r):
-            nc.vector.quantize_mx(out=u_codes[g, r][:].bitcast(E4), scales=u_scales[g, r][:], in_=u_group[g, r][:].rearrange("p t m j -> p (t m j)"))
+        def quantize_u(g, r, lo=0, hi=4):
+            cols = slice(128 * lo, 128 * hi)
+            nc.vector.quantize_mx(
+                out=u_codes[g, r][:, cols].bitcast(E4),
+                scales=u_scales[g, r][:, cols],
+                in_=u_group[g, r][:, lo:hi].rearrange("p t m j -> p (t m j)"),
+            )
 
         z = {}
 
-        def stage1(g, r, n, base, tiles=range(4)):
-            cols = slice(512 * n, 512 * (n + 1))
-            for t in tiles:
-                if g == 0:
-                    z[r, n, t] = bank(base + t)
-                m = slice(128 * t, 128 * (t + 1))
-                nc.tensor.matmul_mx(
-                    out=z[r, n, t][:],
-                    lhsT=u_codes[g, r][:, m].bitcast(E4),
-                    lhsT_scale=u_scales[g, r][:, m],
-                    rhs=g_words[g][:, cols].bitcast(E5),
-                    rhs_scale=g_scales[:, g, cols],
-                    start=(g == 0),
-                    stop=(g == KG - 1),
-                )
+        def stage1(g, r, n, t):
+            if g == 0:
+                z[r, n, t] = next_bank()
+            m = slice(128 * t, 128 * (t + 1))
+            nc.tensor.matmul_mx(
+                out=z[r, n, t][:],
+                lhsT=u_codes[g, r][:, m].bitcast(E4),
+                lhsT_scale=u_scales[g, r][:, m],
+                rhs=g_words[g, n][:].bitcast(E5),
+                rhs_scale=g_scales[:, g, 512 * n : 512 * (n + 1)],
+                start=(g == 0),
+                stop=(g == KG - 1),
+            )
 
         h_rows = {}
         h_group = {}
@@ -200,21 +175,20 @@ def tile_factored_gain_correction_e3_kernel(tc, innov_words, innov_scales, obs_m
         def group_h(r, n):
             h_group[r, n] = work.tile([P, 512, 4], BF16, name="h_group", tag="h_group", bufs=2, align_bytes=64)
             src = h_rows[r, n][:].rearrange("p t (c i) -> p c t i", i=4)
-            dst = h_group[r, n][:].rearrange("p (c i) t -> p c t i", i=4)
-            cut = H_CUT // 4
-            nc.vector.tensor_copy(out=dst[:, 0:cut], in_=src[:, 0:cut])
-            nc.scalar.copy(out=dst[:, cut:P], in_=src[:, cut:P])
+            copy("v", h_group[r, n][:].rearrange("p (c i) t -> p c t i", i=4), src)
 
         def quantize_h(r, n):
             nc.vector.quantize_mx(out=h_codes[r, n][:].bitcast(E5), scales=h_scales[r, n][:], in_=h_group[r, n][:].rearrange("p n t -> p (n t)"))
 
-        def stage2(a, n, b):
+        acc = {}
+
+        def stage2(a, n):
             q, i = a // 2, a % 2
-            acc = bank(b)
+            acc[a, n] = next_bank()
             for r in range(2):
                 m = slice(256 * i + 128 * r, 256 * i + 128 * (r + 1))
                 nc.tensor.matmul_mx(
-                    out=acc[:],
+                    out=acc[a, n][:],
                     lhsT=v_codes[q][:, m].bitcast(E4),
                     lhsT_scale=v_scales[q][:, m],
                     rhs=h_codes[r, n][:].bitcast(E5),
@@ -222,137 +196,100 @@ def tile_factored_gain_correction_e3_kernel(tc, innov_words, innov_scales, obs_m
                     start=(r == 0),
                     stop=(r == 1),
                 )
-            return acc
 
         results = {}
 
-        def empty_out(a, n, acc, engine, lo=0, hi=512):
+        def empty_out(a, n, engine, lo=0, hi=512):
             if a not in results:
-                results[a] = work.tile([P, 1, N], F32, name="result", tag="result", bufs=6, align_bytes=64)
-            dst = results[a][:, 0, 512 * n + lo : 512 * n + hi]
-            if engine == "s":
-                nc.scalar.copy(out=dst, in_=acc[:, lo:hi])
-            else:
-                nc.vector.tensor_copy(out=dst, in_=acc[:, lo:hi])
+                results[a] = work.tile([P, 1, N], F32, name="result", tag="result", bufs=RESULT_BUFS, align_bytes=64)
+            copy(engine, results[a][:, 0, 512 * n + lo : 512 * n + hi], acc[a, n][:, lo:hi])
 
-        def store(a):
-            nc.sync.dma_start(out=out_rows[:, a : a + 1, :], in_=results[a][:])
+        def store(a, lo=0, hi=N):
+            nc.sync.dma_start(out=out_rows[:, a : a + 1, lo:hi], in_=results[a][:, :, lo:hi])
 
-        t = {}
+        whole = slice(0, P)
 
-        def stage1_pair(g, r):
-            stage1(g, r, 0, 0)
-            stage1(g, r, 1, 4)
-
-        u_group[0, 0] = work.tile([P, 4, P, 4], BF16, name="u_group", tag="u_group", bufs=4, align_bytes=64)
-        src = u_raw[0, 0][:].rearrange("p j (m t) -> p m j t", t=4)
-        dst = u_group[0, 0][:].rearrange("p t m j -> p m j t")
-        nc.vector.tensor_copy(out=dst[:, :, :, 0:2], in_=src[:, :, :, 0:2])
-        nc.scalar.copy(out=dst[:, :, :, 2:4], in_=src[:, :, :, 2:4])
-        for half in range(2):
-            cols = slice(256 * half, 256 * (half + 1))
-            nc.vector.quantize_mx(
-                out=u_codes[0, 0][:, cols].bitcast(E4),
-                scales=u_scales[0, 0][:, cols],
-                in_=u_group[0, 0][:, 2 * half : 2 * half + 2].rearrange("p t m j -> p (t m j)"),
-            )
-            for n in range(2):
-                stage1(0, 0, n, 4 * n, (2 * half, 2 * half + 1))
-        for g in range(1, KG):
-            group_u(g, 0)
-            if g > 1:
-                stage1_pair(g - 1, 0)
-            if g == 2:
-                make_gain()
-            quantize_u(g, 0)
-        group_u(0, 1)
-        stage1(3, 0, 1, 4)
-        stage1(3, 0, 0, 0)
-        empty_z(0, 1, 0, "s")
-        quantize_u(0, 1)
-        empty_z(0, 1, 2, "s")
-        empty_z(0, 1, 1, "v")
-        group_u(1, 1)
-        empty_z(0, 1, 3, "s")
-        quantize_u(1, 1)
-        stage1(0, 1, 1, 4)
-        stage1(1, 1, 1, 4)
-        empty_z(0, 0, 0, "s")
-        empty_z(0, 0, 1, "v")
-        empty_z(0, 0, 2, "s")
-        group_u(2, 1)
-        empty_z(0, 0, 3, "s")
-        quantize_u(2, 1)
-        group_u(3, 1)
-        quantize_u(3, 1)
         for g in range(KG):
-            stage1(g, 1, 0, 0)
+            for r in range(2):
+                group_u(g, r, "v", whole, slice(0, 2))
+                group_u(g, r, "s", whole, slice(2, 4))
+            for r in range(2):
+                for lo in (0, 2):
+                    quantize_u(g, r, lo, lo + 2)
+                    for t in (lo, lo + 1):
+                        stage1(g, r, 0, t)
+        for r in range(2):
+            for t in range(4):
+                empty_z(r, 0, t, "ssvv"[t] if r == 0 else "ssvs"[t])
+
+        def sweep(r, t):
+            for g in range(KG):
+                stage1(g, r, 1, t)
+            empty_z(r, 1, t, "s")
+
         group_h(0, 0)
-        group_h(0, 1)
-        for g in range(2, KG):
-            stage1(g, 1, 1, 4)
+        order_v(0)
         quantize_h(0, 0)
-        order_v(0, "v")
-        for j in range(3):
-            empty_z(1, 0, j, "s")
-        empty_z(1, 0, 3, "v")
-        order_v(1, "v")
-        quantize_h(0, 1)
         group_h(1, 0)
-        for j in range(4):
-            empty_z(1, 1, j, "svsv"[j])
-        for a in range(4):
-            t[a] = transpose_v(a, a)
+        order_v(1)
         quantize_h(1, 0)
-        for a in range(4, 8):
-            t[a] = transpose_v(a, a)
-        empty_v(0, t[0], "s")
-        empty_v(1, t[1], "s")
-        group_h(1, 1)
+        for t in range(4):
+            sweep(0, t)
+        for a in range(4):
+            transpose_v(a)
+        group_h(0, 1)
+        empty_v(0, "s")
+        empty_v(1, "v")
+        empty_v(2, "s")
+        quantize_h(0, 1)
+        empty_v(3, "s")
         quantize_v(0)
-        empty_v(2, t[2], "v")
-        empty_v(3, t[3], "s")
-        quantize_h(1, 1)
+        order_v(2)
         quantize_v(1)
-        empty_v(4, t[4], "s")
-        empty_v(5, t[5], "v")
+        order_v(3)
+        for t in range(4):
+            sweep(1, t)
+        group_h(1, 1)
+        for a in range(4):
+            stage2(a, 0)
+            empty_out(a, 0, "s")
+            store(a, 0, 512)
+        quantize_h(1, 1)
+        for a in range(4, 8):
+            transpose_v(a)
+            empty_v(a, "vs"[a % 2])
+        quantize_v(2)
+        order_v(4)
+        quantize_v(3)
+        order_v(5)
+        for a in range(4):
+            stage2(a, 1)
+            empty_out(a, 1, "s")
+            store(a, 512, N)
 
-        def finish(a, n, engine, b):
-            acc = stage2(a, n, b)
-            empty_out(a, n, acc, engine)
-
-        for i in range(4):
+        def finish(a, engines):
             for n in range(2):
-                finish(i, n, "sv"[n], (2 * i + n) % 4)
-            store(i)
-            if i == 0:
-                quantize_v(2)
-                empty_v(6, t[6], "s")
-            if i == 1:
-                empty_v(7, t[7], "s")
-                order_v(4, "v")
-            if i == 2:
-                quantize_v(3)
-        for q in range(4, SP):
-            ts = (2 * q, 2 * q + 1)
-            for a in ts:
-                t[a] = transpose_v(a, 4 + a % 4)
-                empty_v(a, t[a], "s")
-            for i in range(2):
-                a = 2 * q - 4 + i
-                for n in range(2):
-                    finish(a, n, "vs"[n], (2 * a + n) % 4)
-                store(a)
-                if i == 0 and q + 1 < SP:
-                    order_v(q + 1, "v")
-            quantize_v(q)
-        for a in range(ST - 4, ST - 1):
-            for n in range(2):
-                finish(a, n, "sv"[n], (2 * a + n) % 8)
+                stage2(a, n)
+                empty_out(a, n, engines[n])
             store(a)
+
+        for q in (4, 6):
+            finish(2 * q - 4, "ss")
+            finish(2 * q - 3, "sv")
+            for a in range(2 * q, 2 * q + 4):
+                transpose_v(a)
+                empty_v(a, "sv"[a % 2])
+            quantize_v(q)
+            quantize_v(q + 1)
+            finish(2 * q - 2, "ss")
+            finish(2 * q - 1, "sv")
+            if q == 4:
+                order_v(6)
+                order_v(7)
+        for a in range(ST - 4, ST - 1):
+            finish(a, "sv")
         last = ST - 1
         for n in range(2):
-            acc = stage2(last, n, 6 + n)
-            empty_out(last, n, acc, "s", 0, 256)
-            empty_out(last, n, acc, "v", 256, 512)
-            nc.sync.dma_start(out=out_rows[:, last : ST, 512 * n : 512 * (n + 1)], in_=results[last][:, 0:1, 512 * n : 512 * (n + 1)])
+            stage2(last, n)
+            empty_out(last, n, "sv"[n])
+            store(last, 512 * n, 512 * (n + 1))

@@ -21,6 +21,7 @@ KG = K // 512
 ST = S // P
 SP = ST // 2
 RESULT_BUFS = 8
+U_CUTS = (84, 60)
 
 
 def tile_factored_gain_correction_e3_kernel(tc, innov_words, innov_scales, obs_modes, mode_ratio, state_modes, out):
@@ -37,20 +38,21 @@ def tile_factored_gain_correction_e3_kernel(tc, innov_words, innov_scales, obs_m
         def bank(b):
             return psum.tile([P, 512], F32, name="bank%d" % b, tag="bank%d" % b)
 
-        used = []
+        turn = [0]
 
         def next_bank():
-            used.append(len(used) % 8)
-            return bank(used[-1])
+            b = turn[0]
+            turn[0] = (b + 1) % 8
+            return bank(b)
 
         ident = keep.tile([P, P], F32, name="ident", align_bytes=64)
         ratio = keep.tile([P, 2, 4], BF16, name="ratio")
         ratio32 = keep.tile([P, 8], F32, name="ratio32")
         square = keep.tile([P, 8], F32, name="square")
         gain = keep.tile([P, 8], F32, name="gain")
-        g_words = {(g, n): keep.tile([P, 512], U32, name="g_words%d_%d" % (g, n), align_bytes=64) for g in range(KG) for n in range(2)}
-        g_scales = keep.tile([P, KG, N], U8, name="g_scales", align_bytes=64)
-        u_raw = [keep.tile([P, 4, R], BF16, name="u_raw%d" % g, align_bytes=64) for g in range(KG)]
+        g_words = {}
+        g_scales = [keep.tile([P, KG, 512], U8, name="g_scales%d" % n, align_bytes=64) for n in range(2)]
+        u_raw = {}
         u_codes = {(g, r): keep.tile([P, 512], U32, name="u_codes%d_%d" % (g, r), align_bytes=64) for g in range(KG) for r in range(2)}
         u_scales = {k: keep.tile([P, 512], U8, name="u_scales%d_%d" % k, align_bytes=64) for k in u_codes}
         v_raw = [keep.tile([P, 2, R], BF16, name="v_raw%d" % q, align_bytes=64) for q in range(SP)]
@@ -59,31 +61,40 @@ def tile_factored_gain_correction_e3_kernel(tc, innov_words, innov_scales, obs_m
         h_codes = {(r, n): keep.tile([P, 512], U32, name="h_codes%d_%d" % (r, n), align_bytes=64) for r in range(2) for n in range(2)}
         h_scales = {k: keep.tile([P, 512], U8, name="h_scales%d_%d" % k, align_bytes=64) for k in h_codes}
 
-        nc.vector.memset(g_scales[:].rearrange("p g n -> p (g n)").bitcast(I32), 0)
+        for n in range(2):
+            nc.vector.memset(g_scales[n][:].rearrange("p g n -> p (g n)").bitcast(I32), 0)
         nc.scalar.dma_start(out=ratio[:], in_=mode_ratio.rearrange("(g p t) -> p g t", g=2, t=4))
 
-        def load_scales():
-            scale_rows = innov_scales.rearrange("g (q j) n -> j q g n", j=4)
+        def load_scales(n):
+            scale_rows = innov_scales[:, :, 512 * n : 512 * (n + 1)].rearrange("g (q j) n -> j q g n", j=4)
             for j in range(4):
-                nc.sync.dma_start(out=g_scales[j:P:32, :, :].bitcast(I32), in_=scale_rows[j].bitcast(I32))
+                nc.sync.dma_start(out=g_scales[n][j:P:32, :, :].bitcast(I32), in_=scale_rows[j].bitcast(I32))
 
-        def load_u(g):
-            nc.sync.dma_start(out=u_raw[g][:], in_=obs_modes[512 * g : 512 * (g + 1), :].rearrange("(p j) w -> p j w", j=4))
+        def load_u(g, halves):
+            lo, hi = 512 * halves[0], 512 * (halves[-1] + 1)
+            raw = keep.tile([P, 4, hi - lo], BF16, name="u_raw%d_%d" % (g, lo), align_bytes=64)
+            nc.sync.dma_start(out=raw[:], in_=obs_modes[512 * g : 512 * (g + 1), lo:hi].rearrange("(p j) w -> p j w", j=4))
+            for r in halves:
+                u_raw[g, r] = raw[:, :, 512 * r - lo : 512 * (r + 1) - lo]
 
-        def load_w(g, n):
-            words = innov_words[g][:, 512 * n : 512 * (n + 1), :].rearrange("p n t -> p (n t)")
-            nc.sync.dma_start(out=g_words[g, n][:].bitcast(I32), in_=words.bitcast(I32))
+        def load_w(lo, hi, n):
+            tile = keep.tile([P, hi - lo, 512], U32, name="g_words%d_%d" % (lo, n), align_bytes=64)
+            words = innov_words[lo:hi, :, 512 * n : 512 * (n + 1), :].rearrange("g p n t -> p g (n t)")
+            nc.sync.dma_start(out=tile[:].bitcast(I32), in_=words.bitcast(I32))
+            for g in range(lo, hi):
+                g_words[g, n] = tile[:, g - lo, :]
 
         def load_v(q):
             nc.sync.dma_start(out=v_raw[q][:], in_=v_rows[:, 2 * q : 2 * q + 2, :])
 
         for g in range(KG):
-            load_u(g)
-            load_w(g, 0)
+            load_u(g, (0, 1))
+            load_w(g, g + 1, 0)
             if g == 0:
-                load_scales()
-        for g in range(KG):
-            load_w(g, 1)
+                load_scales(0)
+        load_scales(1)
+        load_w(0, 2, 1)
+        load_w(2, 4, 1)
         for q in range(SP):
             load_v(q)
 
@@ -112,10 +123,12 @@ def tile_factored_gain_correction_e3_kernel(tc, innov_words, innov_scales, obs_m
 
         def transpose_v(a):
             v_bank[a] = next_bank()
-            ordered = v_words[a // 2][:, a % 2].rearrange("p g u m -> p (g u m)")
             for c in range(4):
-                cols = slice(128 * c, 128 * (c + 1))
-                nc.tensor.transpose(v_bank[a][:, cols], ordered[:, cols], ident[:])
+                if a // 2 in v_words:
+                    words = v_words[a // 2][:, a % 2, c // 2, c % 2, :]
+                else:
+                    words = v_raw[a // 2][:, a % 2, :].bitcast(F32)[:, 256 * (c // 2) + c % 2 : 256 * (c // 2 + 1) : 2]
+                nc.tensor.transpose(v_bank[a][:, 128 * c : 128 * (c + 1)], words, ident[:])
 
         def empty_v(a, engine):
             q = a // 2
@@ -131,8 +144,8 @@ def tile_factored_gain_correction_e3_kernel(tc, innov_words, innov_scales, obs_m
 
         def group_u(g, r, engine, rows, slots=slice(0, 4)):
             if (g, r) not in u_group:
-                u_group[g, r] = work.tile([P, 4, P, 4], BF16, name="u_group", tag="u_group", bufs=3, align_bytes=64)
-            src = u_raw[g][:, :, 512 * r : 512 * (r + 1)].rearrange("p j (m t) -> p m j t", t=4)
+                u_group[g, r] = work.tile([P, 4, P, 4], BF16, name="u_group", tag="u_group", bufs=4, align_bytes=64)
+            src = u_raw[g, r].rearrange("p j (m t) -> p m j t", t=4)
             dst = u_group[g, r][:].rearrange("p t m j -> p m j t")
             copy(engine, dst[:, rows, :, slots], src[:, rows, :, slots])
 
@@ -154,8 +167,8 @@ def tile_factored_gain_correction_e3_kernel(tc, innov_words, innov_scales, obs_m
                 out=z[r, n, t][:],
                 lhsT=u_codes[g, r][:, m].bitcast(E4),
                 lhsT_scale=u_scales[g, r][:, m],
-                rhs=g_words[g, n][:].bitcast(E5),
-                rhs_scale=g_scales[:, g, 512 * n : 512 * (n + 1)],
+                rhs=g_words[g, n].bitcast(E5),
+                rhs_scale=g_scales[n][:, g, :],
                 start=(g == 0),
                 stop=(g == KG - 1),
             )
@@ -172,20 +185,22 @@ def tile_factored_gain_correction_e3_kernel(tc, innov_words, innov_scales, obs_m
             else:
                 nc.vector.tensor_scalar_mul(h_rows[r, n][:, t, :], z[r, n, t][:], scale)
 
-        def group_h(r, n):
-            h_group[r, n] = work.tile([P, 512, 4], BF16, name="h_group", tag="h_group", bufs=2, align_bytes=64)
+        def group_h(r, n, engine="v", lo=0, hi=P):
+            if (r, n) not in h_group:
+                h_group[r, n] = work.tile([P, 512, 4], BF16, name="h_group", tag="h_group", bufs=2, align_bytes=64)
             src = h_rows[r, n][:].rearrange("p t (c i) -> p c t i", i=4)
-            copy("v", h_group[r, n][:].rearrange("p (c i) t -> p c t i", i=4), src)
+            copy(engine, h_group[r, n][:].rearrange("p (c i) t -> p c t i", i=4)[:, lo:hi], src[:, lo:hi])
 
         def quantize_h(r, n):
             nc.vector.quantize_mx(out=h_codes[r, n][:].bitcast(E5), scales=h_scales[r, n][:], in_=h_group[r, n][:].rearrange("p n t -> p (n t)"))
 
         acc = {}
 
-        def stage2(a, n):
+        def stage2(a, n, mode_halves=(0, 1)):
             q, i = a // 2, a % 2
-            acc[a, n] = next_bank()
-            for r in range(2):
+            if (a, n) not in acc:
+                acc[a, n] = next_bank()
+            for r in mode_halves:
                 m = slice(256 * i + 128 * r, 256 * i + 128 * (r + 1))
                 nc.tensor.matmul_mx(
                     out=acc[a, n][:],
@@ -207,46 +222,52 @@ def tile_factored_gain_correction_e3_kernel(tc, innov_words, innov_scales, obs_m
         def store(a, lo=0, hi=N):
             nc.sync.dma_start(out=out_rows[:, a : a + 1, lo:hi], in_=results[a][:, :, lo:hi])
 
-        whole = slice(0, P)
+        def group_half(g, r, cut):
+            group_u(g, r, "v", slice(0, cut))
+            group_u(g, r, "s", slice(cut, P))
 
-        for g in range(KG):
-            for r in range(2):
-                group_u(g, r, "v", whole, slice(0, 2))
-                group_u(g, r, "s", whole, slice(2, 4))
-            for r in range(2):
-                for lo in (0, 2):
-                    quantize_u(g, r, lo, lo + 2)
-                    for t in (lo, lo + 1):
-                        stage1(g, r, 0, t)
-        for r in range(2):
+        def quantize_pairs(g, r):
+            quantize_u(g, r, 0, 2)
+            quantize_u(g, r, 2, 4)
+
+        def passes(g, r, n):
             for t in range(4):
-                empty_z(r, 0, t, "ssvv"[t] if r == 0 else "ssvs"[t])
+                stage1(g, r, n, t)
 
         def sweep(r, t):
             for g in range(KG):
                 stage1(g, r, 1, t)
             empty_z(r, 1, t, "s")
 
+        for g in range(KG):
+            for r in range(2):
+                group_half(g, r, U_CUTS[r])
+            for r in range(2):
+                quantize_pairs(g, r)
+                passes(g, r, 0)
+        for r in range(2):
+            for t in range(4):
+                empty_z(r, 0, t, "ssvs"[t] if r == 0 else "vsvs"[t])
         group_h(0, 0)
         order_v(0)
         quantize_h(0, 0)
-        group_h(1, 0)
         order_v(1)
-        quantize_h(1, 0)
+        group_h(1, 0)
         for t in range(4):
             sweep(0, t)
         for a in range(4):
             transpose_v(a)
-        group_h(0, 1)
-        empty_v(0, "s")
-        empty_v(1, "v")
+        empty_v(0, "v")
+        quantize_h(1, 0)
+        empty_v(1, "s")
         empty_v(2, "s")
-        quantize_h(0, 1)
         empty_v(3, "s")
-        quantize_v(0)
         order_v(2)
+        quantize_v(0)
+        group_h(0, 1)
         quantize_v(1)
         order_v(3)
+        quantize_h(0, 1)
         for t in range(4):
             sweep(1, t)
         group_h(1, 1)
@@ -262,8 +283,10 @@ def tile_factored_gain_correction_e3_kernel(tc, innov_words, innov_scales, obs_m
         order_v(4)
         quantize_v(3)
         order_v(5)
+        for a in range(2):
+            stage2(a, 1, (0,))
         for a in range(4):
-            stage2(a, 1)
+            stage2(a, 1, (1,) if a < 2 else (0, 1))
             empty_out(a, 1, "s")
             store(a, 512, N)
 

@@ -26,8 +26,8 @@ U_CUTS = (84, 60)
 
 def tile_factored_gain_correction_e3_kernel(tc, innov_words, innov_scales, obs_modes, mode_ratio, state_modes, out):
     nc = tc.nc
-    v_rows = state_modes.rearrange("(p a) r -> p a r", a=ST)
-    out_rows = out.rearrange("(p a) n -> p a n", a=ST)
+    v_rows = state_modes.rearrange("(q p i) r -> q p i r", p=P, i=2)
+    out_rows = out.rearrange("(q p i) n -> q p i n", p=P, i=2)
 
     with ExitStack() as ctx:
         keep = ctx.enter_context(tc.tile_pool(name="keep", bufs=1))
@@ -85,7 +85,7 @@ def tile_factored_gain_correction_e3_kernel(tc, innov_words, innov_scales, obs_m
                 g_words[g, n] = tile[:, g - lo, :]
 
         def load_v(q):
-            nc.sync.dma_start(out=v_raw[q][:], in_=v_rows[:, 2 * q : 2 * q + 2, :])
+            nc.sync.dma_start(out=v_raw[q][:], in_=v_rows[q])
 
         for g in range(KG):
             load_u(g, (0, 1))
@@ -220,7 +220,7 @@ def tile_factored_gain_correction_e3_kernel(tc, innov_words, innov_scales, obs_m
             copy(engine, results[a][:, 0, 512 * n + lo : 512 * n + hi], acc[a, n][:, lo:hi])
 
         def store(a, lo=0, hi=N):
-            nc.sync.dma_start(out=out_rows[:, a : a + 1, lo:hi], in_=results[a][:, :, lo:hi])
+            nc.sync.dma_start(out=out_rows[a // 2][:, a % 2 : a % 2 + 1, lo:hi], in_=results[a][:, :, lo:hi])
 
         def group_half(g, r, cut):
             group_u(g, r, "v", slice(0, cut))
@@ -309,10 +309,5 @@ def tile_factored_gain_correction_e3_kernel(tc, innov_words, innov_scales, obs_m
             if q == 4:
                 order_v(6)
                 order_v(7)
-        for a in range(ST - 4, ST - 1):
+        for a in range(ST - 4, ST):
             finish(a, "sv")
-        last = ST - 1
-        for n in range(2):
-            stage2(last, n)
-            empty_out(last, n, "sv"[n])
-            store(last, 512 * n, 512 * (n + 1))

@@ -20,7 +20,7 @@ P = 128
 KG = K // 512
 ST = S // P
 SP = ST // 2
-RESULT_BUFS = 8
+RESULT_BUFS = 7
 U_CUTS = (84, 60)
 
 
@@ -45,25 +45,27 @@ def tile_factored_gain_correction_e3_kernel(tc, innov_words, innov_scales, obs_m
             turn[0] = (b + 1) % 8
             return bank(b)
 
-        ident = keep.tile([P, P], F32, name="ident", align_bytes=64)
-        ratio = keep.tile([P, 2, 4], BF16, name="ratio")
+        ident = keep.tile([P, P], F32, name="ident", align_bytes=256)
+        ratio_rows = keep.tile([P, 256], F32, name="ratio_rows", align_bytes=256)
         ratio32 = keep.tile([P, 8], F32, name="ratio32")
         square = keep.tile([P, 8], F32, name="square")
         gain = keep.tile([P, 8], F32, name="gain")
         g_words = {}
-        g_scales = [keep.tile([P, KG, 512], U8, name="g_scales%d" % n, align_bytes=64) for n in range(2)]
+        g_scales = [keep.tile([P, KG, 512], U8, name="g_scales%d" % n, align_bytes=256) for n in range(2)]
         u_raw = {}
-        u_codes = {(g, r): keep.tile([P, 512], U32, name="u_codes%d_%d" % (g, r), align_bytes=64) for g in range(KG) for r in range(2)}
-        u_scales = {k: keep.tile([P, 512], U8, name="u_scales%d_%d" % k, align_bytes=64) for k in u_codes}
-        v_raw = [keep.tile([P, 2, R], BF16, name="v_raw%d" % q, align_bytes=64) for q in range(SP)]
-        v_codes = [keep.tile([P, 512], U32, name="v_codes%d" % q, align_bytes=64) for q in range(SP)]
-        v_scales = [keep.tile([P, 512], U8, name="v_scales%d" % q, align_bytes=64) for q in range(SP)]
-        h_codes = {(r, n): keep.tile([P, 512], U32, name="h_codes%d_%d" % (r, n), align_bytes=64) for r in range(2) for n in range(2)}
-        h_scales = {k: keep.tile([P, 512], U8, name="h_scales%d_%d" % k, align_bytes=64) for k in h_codes}
+        u_codes = {(g, r): keep.tile([P, 512], U32, name="u_codes%d_%d" % (g, r), align_bytes=256) for g in range(KG) for r in range(2)}
+        u_scales = {k: keep.tile([P, 512], U8, name="u_scales%d_%d" % k, align_bytes=256) for k in u_codes}
+        v_raw = [keep.tile([P, 2, R], BF16, name="v_raw%d" % q, align_bytes=256) for q in range(SP)]
+        v_codes = [keep.tile([P, 512], U32, name="v_codes%d" % q, align_bytes=256) for q in range(SP)]
+        v_scales = [keep.tile([P, 512], U8, name="v_scales%d" % q, align_bytes=256) for q in range(SP)]
+        h_codes = {(r, n): keep.tile([P, 512], U32, name="h_codes%d_%d" % (r, n), align_bytes=256) for r in range(2) for n in range(2)}
+        h_scales = {k: keep.tile([P, 512], U8, name="h_scales%d_%d" % k, align_bytes=256) for k in h_codes}
 
         for n in range(2):
             nc.vector.memset(g_scales[n][:].rearrange("p g n -> p (g n)").bitcast(I32), 0)
-        nc.scalar.dma_start(out=ratio[:], in_=mode_ratio.rearrange("(g p t) -> p g t", g=2, t=4))
+        make_identity(nc, ident[:])
+        for half in range(2):
+            nc.scalar.activation(out=ratio_rows[:, P * half : P * (half + 1)], in_=ident[:], func=COPY, scale=0.0)
 
         def load_scales(n):
             scale_rows = innov_scales[:, :, 512 * n : 512 * (n + 1)].rearrange("g (q j) n -> j q g n", j=4)
@@ -72,13 +74,13 @@ def tile_factored_gain_correction_e3_kernel(tc, innov_words, innov_scales, obs_m
 
         def load_u(g, halves):
             lo, hi = 512 * halves[0], 512 * (halves[-1] + 1)
-            raw = keep.tile([P, 4, hi - lo], BF16, name="u_raw%d_%d" % (g, lo), align_bytes=64)
+            raw = keep.tile([P, 4, hi - lo], BF16, name="u_raw%d_%d" % (g, lo), align_bytes=256)
             nc.sync.dma_start(out=raw[:], in_=obs_modes[512 * g : 512 * (g + 1), lo:hi].rearrange("(p j) w -> p j w", j=4))
             for r in halves:
                 u_raw[g, r] = raw[:, :, 512 * r - lo : 512 * (r + 1) - lo]
 
         def load_w(lo, hi, n):
-            tile = keep.tile([P, hi - lo, 512], U32, name="g_words%d_%d" % (lo, n), align_bytes=64)
+            tile = keep.tile([P, hi - lo, 512], U32, name="g_words%d_%d" % (lo, n), align_bytes=256)
             words = innov_words[lo:hi, :, 512 * n : 512 * (n + 1), :].rearrange("g p n t -> p g (n t)")
             nc.sync.dma_start(out=tile[:].bitcast(I32), in_=words.bitcast(I32))
             for g in range(lo, hi):
@@ -92,19 +94,24 @@ def tile_factored_gain_correction_e3_kernel(tc, innov_words, innov_scales, obs_m
             load_w(g, g + 1, 0)
             if g == 0:
                 load_scales(0)
+                nc.sync.dma_start(out=ratio_rows[0:2, :].bitcast(BF16), in_=mode_ratio.rearrange("(r c) -> r c", r=2))
         load_scales(1)
         load_w(0, 2, 1)
         load_w(2, 4, 1)
         for q in range(SP):
             load_v(q)
 
-        make_identity(nc, ident[:])
-
-        nc.scalar.activation(out=ratio32[:], in_=ratio[:].rearrange("p g t -> p (g t)"), func=COPY)
-        nc.vector.tensor_tensor(out=square[:], in0=ratio32[:], in1=ratio32[:], op=MULT)
-        nc.vector.tensor_scalar_add(square[:], square[:], 1.0)
-        nc.vector.reciprocal(square[:], square[:])
-        nc.vector.tensor_tensor(out=gain[:], in0=ratio32[:], in1=square[:], op=MULT)
+        ratio_bank = bank(7)
+        for u in range(2):
+            nc.tensor.transpose(ratio_bank[:, P * u : P * (u + 1)], ratio_rows[:, u:256:2], ident[:])
+        ratio_turned = ratio_bank[:, : 2 * P].bitcast(BF16).rearrange("p (u k e) -> p k u e", u=2, e=2)[:, 0:2]
+        gain_steps = [
+            lambda: nc.vector.tensor_copy(out=ratio32[:].rearrange("p (r u e) -> p r u e", r=2, u=2), in_=ratio_turned),
+            lambda: nc.vector.tensor_tensor(out=square[:], in0=ratio32[:], in1=ratio32[:], op=MULT),
+            lambda: nc.vector.tensor_scalar_add(square[:], square[:], 1.0),
+            lambda: nc.vector.reciprocal(square[:], square[:]),
+            lambda: nc.vector.tensor_tensor(out=gain[:], in0=ratio32[:], in1=square[:], op=MULT),
+        ]
 
         def copy(engine, out, in_):
             if engine == "s":
@@ -117,7 +124,7 @@ def tile_factored_gain_correction_e3_kernel(tc, innov_words, innov_scales, obs_m
         v_bank = {}
 
         def order_v(q):
-            v_words[q] = work.tile([P, 2, 2, 2, P], F32, name="v_words", tag="v_words", bufs=3, align_bytes=64)
+            v_words[q] = work.tile([P, 2, 2, 2, P], F32, name="v_words", tag="v_words", bufs=3, align_bytes=256)
             src = v_raw[q][:].rearrange("p i r -> p (i r)").bitcast(F32).rearrange("p (x m u) -> p x u m", x=4, u=2)
             copy("v", v_words[q][:].rearrange("p i g u m -> p (i g) u m"), src)
 
@@ -133,7 +140,7 @@ def tile_factored_gain_correction_e3_kernel(tc, innov_words, innov_scales, obs_m
         def empty_v(a, engine):
             q = a // 2
             if q not in v_group:
-                v_group[q] = work.tile([P, 2, 2, P, 4], BF16, name="v_group", tag="v_group", bufs=3, align_bytes=64)
+                v_group[q] = work.tile([P, 2, 2, P, 4], BF16, name="v_group", tag="v_group", bufs=3, align_bytes=256)
             dst = v_group[q][:, a % 2].rearrange("p g s t -> p g (s t)").bitcast(F32).rearrange("p g (s u) -> p g s u", u=2)
             copy(engine, dst, v_bank[a][:].rearrange("p (g u s) -> p g s u", g=2, u=2))
 
@@ -144,7 +151,7 @@ def tile_factored_gain_correction_e3_kernel(tc, innov_words, innov_scales, obs_m
 
         def group_u(g, r, engine, rows, slots=slice(0, 4)):
             if (g, r) not in u_group:
-                u_group[g, r] = work.tile([P, 4, P, 4], BF16, name="u_group", tag="u_group", bufs=4, align_bytes=64)
+                u_group[g, r] = work.tile([P, 4, P, 4], BF16, name="u_group", tag="u_group", bufs=4, align_bytes=256)
             src = u_raw[g, r].rearrange("p j (m t) -> p m j t", t=4)
             dst = u_group[g, r][:].rearrange("p t m j -> p m j t")
             copy(engine, dst[:, rows, :, slots], src[:, rows, :, slots])
@@ -178,7 +185,7 @@ def tile_factored_gain_correction_e3_kernel(tc, innov_words, innov_scales, obs_m
 
         def empty_z(r, n, t, engine):
             if (r, n) not in h_rows:
-                h_rows[r, n] = work.tile([P, 4, 512], BF16, name="h_rows", tag="h_rows", bufs=3, align_bytes=64)
+                h_rows[r, n] = work.tile([P, 4, 512], BF16, name="h_rows", tag="h_rows", bufs=3, align_bytes=256)
             scale = gain[:, 4 * r + t : 4 * r + t + 1]
             if engine == "s":
                 nc.scalar.activation(out=h_rows[r, n][:, t, :], in_=z[r, n, t][:], func=COPY, scale=scale)
@@ -187,7 +194,7 @@ def tile_factored_gain_correction_e3_kernel(tc, innov_words, innov_scales, obs_m
 
         def group_h(r, n, engine="v", lo=0, hi=P):
             if (r, n) not in h_group:
-                h_group[r, n] = work.tile([P, 512, 4], BF16, name="h_group", tag="h_group", bufs=2, align_bytes=64)
+                h_group[r, n] = work.tile([P, 512, 4], BF16, name="h_group", tag="h_group", bufs=2, align_bytes=256)
             src = h_rows[r, n][:].rearrange("p t (c i) -> p c t i", i=4)
             copy(engine, h_group[r, n][:].rearrange("p (c i) t -> p c t i", i=4)[:, lo:hi], src[:, lo:hi])
 
@@ -216,7 +223,7 @@ def tile_factored_gain_correction_e3_kernel(tc, innov_words, innov_scales, obs_m
 
         def empty_out(a, n, engine, lo=0, hi=512):
             if a not in results:
-                results[a] = work.tile([P, 1, N], F32, name="result", tag="result", bufs=RESULT_BUFS, align_bytes=64)
+                results[a] = work.tile([P, 1, N], F32, name="result", tag="result", bufs=RESULT_BUFS, align_bytes=256)
             copy(engine, results[a][:, 0, 512 * n + lo : 512 * n + hi], acc[a, n][:, lo:hi])
 
         def store(a, lo=0, hi=N):
@@ -244,6 +251,8 @@ def tile_factored_gain_correction_e3_kernel(tc, innov_words, innov_scales, obs_m
                 group_half(g, r, U_CUTS[r])
             for r in range(2):
                 quantize_pairs(g, r)
+                if gain_steps:
+                    gain_steps.pop(0)()
                 passes(g, r, 0)
         for r in range(2):
             for t in range(4):
@@ -294,7 +303,10 @@ def tile_factored_gain_correction_e3_kernel(tc, innov_words, innov_scales, obs_m
             for n in range(2):
                 stage2(a, n)
                 empty_out(a, n, engines[n])
-            store(a)
+                if a == ST - 6:
+                    store(a, 512 * n, 512 * (n + 1))
+            if a != ST - 6:
+                store(a)
 
         for q in (4, 6):
             finish(2 * q - 4, "ss")

@@ -15,13 +15,16 @@ E4 = mybir.dt.float8_e4m3fn_x4
 E5 = mybir.dt.float8_e5m2_x4
 COPY = mybir.ActivationFunctionType.Copy
 MULT = mybir.AluOpType.mult
+ADD = mybir.AluOpType.add
 
 P = 128
 KG = K // 512
 ST = S // P
 SP = ST // 2
 RESULT_BUFS = 7
+HALVES = (8, 12)
 U_CUTS = (84, 60)
+EDGE_CUTS = (32, 64)
 
 
 def tile_factored_gain_correction_e3_kernel(tc, innov_words, innov_scales, obs_modes, mode_ratio, state_modes, out):
@@ -48,6 +51,7 @@ def tile_factored_gain_correction_e3_kernel(tc, innov_words, innov_scales, obs_m
         ident = keep.tile([P, P], F32, name="ident", align_bytes=256)
         ratio_rows = keep.tile([P, 256], F32, name="ratio_rows", align_bytes=256)
         ratio32 = keep.tile([P, 8], F32, name="ratio32")
+        ones = keep.tile([P, 8], F32, name="ones")
         square = keep.tile([P, 8], F32, name="square")
         gain = keep.tile([P, 8], F32, name="gain")
         g_words = {}
@@ -61,11 +65,11 @@ def tile_factored_gain_correction_e3_kernel(tc, innov_words, innov_scales, obs_m
         h_codes = {(r, n): keep.tile([P, 512], U32, name="h_codes%d_%d" % (r, n), align_bytes=256) for r in range(2) for n in range(2)}
         h_scales = {k: keep.tile([P, 512], U8, name="h_scales%d_%d" % k, align_bytes=256) for k in h_codes}
 
-        for n in range(2):
-            nc.vector.memset(g_scales[n][:].rearrange("p g n -> p (g n)").bitcast(I32), 0)
+        nc.vector.memset(ratio_rows[:], 0.0)
+        nc.vector.memset(g_scales[0][:].rearrange("p g n -> p (g n)").bitcast(I32), 0)
+        nc.vector.memset(g_scales[1][:].rearrange("p g n -> p (g n)").bitcast(I32), 0)
         make_identity(nc, ident[:])
-        for half in range(2):
-            nc.scalar.activation(out=ratio_rows[:, P * half : P * (half + 1)], in_=ident[:], func=COPY, scale=0.0)
+        nc.scalar.activation(out=ones[:], in_=ident[:, :8], func=COPY, scale=0.0, bias=1.0)
 
         def load_scales(n):
             scale_rows = innov_scales[:, :, 512 * n : 512 * (n + 1)].rearrange("g (q j) n -> j q g n", j=4)
@@ -91,10 +95,11 @@ def tile_factored_gain_correction_e3_kernel(tc, innov_words, innov_scales, obs_m
 
         for g in range(KG):
             load_u(g, (0, 1))
+            if g == 0:
+                nc.sync.dma_start(out=ratio_rows[0:2, :].bitcast(BF16), in_=mode_ratio.rearrange("(r c) -> r c", r=2))
             load_w(g, g + 1, 0)
             if g == 0:
                 load_scales(0)
-                nc.sync.dma_start(out=ratio_rows[0:2, :].bitcast(BF16), in_=mode_ratio.rearrange("(r c) -> r c", r=2))
         load_scales(1)
         load_w(0, 2, 1)
         load_w(2, 4, 1)
@@ -108,7 +113,7 @@ def tile_factored_gain_correction_e3_kernel(tc, innov_words, innov_scales, obs_m
         gain_steps = [
             lambda: nc.vector.tensor_copy(out=ratio32[:].rearrange("p (r u e) -> p r u e", r=2, u=2), in_=ratio_turned),
             lambda: nc.vector.tensor_tensor(out=square[:], in0=ratio32[:], in1=ratio32[:], op=MULT),
-            lambda: nc.vector.tensor_scalar_add(square[:], square[:], 1.0),
+            lambda: nc.vector.tensor_tensor(out=square[:], in0=square[:], in1=ones[:], op=ADD),
             lambda: nc.vector.reciprocal(square[:], square[:]),
             lambda: nc.vector.tensor_tensor(out=gain[:], in0=ratio32[:], in1=square[:], op=MULT),
         ]
@@ -246,14 +251,30 @@ def tile_factored_gain_correction_e3_kernel(tc, innov_words, innov_scales, obs_m
                 stage1(g, r, 1, t)
             empty_z(r, 1, t, "s")
 
+        def gain_step():
+            if gain_steps:
+                gain_steps.pop(0)()
+
         for g in range(KG):
-            for r in range(2):
-                group_half(g, r, U_CUTS[r])
-            for r in range(2):
-                quantize_pairs(g, r)
-                if gain_steps:
-                    gain_steps.pop(0)()
-                passes(g, r, 0)
+            if g in (0, KG - 1):
+                group_half(g, 0, U_CUTS[0])
+                group_u(g, 1, "v", slice(0, EDGE_CUTS[0]))
+                group_u(g, 1, "s", slice(EDGE_CUTS[1], P))
+                for lo, hi in ((0, 1), (1, 2), (2, 4)):
+                    quantize_u(g, 0, lo, hi)
+                group_u(g, 1, "v", slice(EDGE_CUTS[0], EDGE_CUTS[1]))
+                passes(g, 0, 0)
+                gain_step()
+                for lo, hi in ((0, 1), (1, 2), (2, 4)):
+                    quantize_u(g, 1, lo, hi)
+                passes(g, 1, 0)
+            else:
+                for r in range(2):
+                    group_half(g, r, U_CUTS[r])
+                for r in range(2):
+                    quantize_pairs(g, r)
+                    gain_step()
+                    passes(g, r, 0)
         for r in range(2):
             for t in range(4):
                 empty_z(r, 0, t, "ssvs"[t] if r == 0 else "vsvs"[t])
@@ -279,19 +300,21 @@ def tile_factored_gain_correction_e3_kernel(tc, innov_words, innov_scales, obs_m
         quantize_h(0, 1)
         for t in range(4):
             sweep(1, t)
+        order_v(4)
         group_h(1, 1)
         for a in range(4):
             stage2(a, 0)
             empty_out(a, 0, "s")
             store(a, 0, 512)
         quantize_h(1, 1)
-        for a in range(4, 8):
+        for a in range(4, 10):
             transpose_v(a)
             empty_v(a, "vs"[a % 2])
         quantize_v(2)
-        order_v(4)
         quantize_v(3)
         order_v(5)
+        quantize_v(4)
+        order_v(6)
         for a in range(2):
             stage2(a, 1, (0,))
         for a in range(4):
@@ -303,23 +326,25 @@ def tile_factored_gain_correction_e3_kernel(tc, innov_words, innov_scales, obs_m
             for n in range(2):
                 stage2(a, n)
                 empty_out(a, n, engines[n])
-                if a == ST - 6:
+                if a in HALVES:
                     store(a, 512 * n, 512 * (n + 1))
-            if a != ST - 6:
+            if a not in HALVES:
                 store(a)
 
-        for q in (4, 6):
-            finish(2 * q - 4, "ss")
-            finish(2 * q - 3, "sv")
-            for a in range(2 * q, 2 * q + 4):
+        def turn_v(lo, hi):
+            for a in range(lo, hi):
                 transpose_v(a)
                 empty_v(a, "sv"[a % 2])
-            quantize_v(q)
-            quantize_v(q + 1)
-            finish(2 * q - 2, "ss")
-            finish(2 * q - 1, "sv")
-            if q == 4:
-                order_v(6)
-                order_v(7)
-        for a in range(ST - 4, ST):
+            for q in range(lo // 2, hi // 2):
+                quantize_v(q)
+
+        for a in range(4, 8):
+            finish(a, "sv" if a % 2 else "ss")
+        turn_v(10, 14)
+        order_v(7)
+        for a in range(8, 12):
+            finish(a, "sv" if a % 2 else "ss")
+        turn_v(14, 16)
+        finish(12, "ss")
+        for a in range(13, ST):
             finish(a, "sv")

@@ -15,16 +15,14 @@ E4 = mybir.dt.float8_e4m3fn_x4
 E5 = mybir.dt.float8_e5m2_x4
 COPY = mybir.ActivationFunctionType.Copy
 MULT = mybir.AluOpType.mult
-ADD = mybir.AluOpType.add
 
 P = 128
 KG = K // 512
 ST = S // P
 SP = ST // 2
 RESULT_BUFS = 7
-HALVES = (8, 12)
+BY_VECTOR = (5, 7)
 U_CUTS = (84, 60)
-EDGE_CUTS = (32, 64)
 
 
 def tile_factored_gain_correction_e3_kernel(tc, innov_words, innov_scales, obs_modes, mode_ratio, state_modes, out):
@@ -51,7 +49,6 @@ def tile_factored_gain_correction_e3_kernel(tc, innov_words, innov_scales, obs_m
         ident = keep.tile([P, P], F32, name="ident", align_bytes=256)
         ratio_rows = keep.tile([P, 256], F32, name="ratio_rows", align_bytes=256)
         ratio32 = keep.tile([P, 8], F32, name="ratio32")
-        ones = keep.tile([P, 8], F32, name="ones")
         square = keep.tile([P, 8], F32, name="square")
         gain = keep.tile([P, 8], F32, name="gain")
         g_words = {}
@@ -65,11 +62,11 @@ def tile_factored_gain_correction_e3_kernel(tc, innov_words, innov_scales, obs_m
         h_codes = {(r, n): keep.tile([P, 512], U32, name="h_codes%d_%d" % (r, n), align_bytes=256) for r in range(2) for n in range(2)}
         h_scales = {k: keep.tile([P, 512], U8, name="h_scales%d_%d" % k, align_bytes=256) for k in h_codes}
 
-        nc.vector.memset(ratio_rows[:], 0.0)
-        nc.vector.memset(g_scales[0][:].rearrange("p g n -> p (g n)").bitcast(I32), 0)
-        nc.vector.memset(g_scales[1][:].rearrange("p g n -> p (g n)").bitcast(I32), 0)
+        for n in range(2):
+            nc.vector.memset(g_scales[n][:].rearrange("p g n -> p (g n)").bitcast(I32), 0)
         make_identity(nc, ident[:])
-        nc.scalar.activation(out=ones[:], in_=ident[:, :8], func=COPY, scale=0.0, bias=1.0)
+        for half in range(2):
+            nc.scalar.activation(out=ratio_rows[:, P * half : P * (half + 1)], in_=ident[:], func=COPY, scale=0.0)
 
         def load_scales(n):
             scale_rows = innov_scales[:, :, 512 * n : 512 * (n + 1)].rearrange("g (q j) n -> j q g n", j=4)
@@ -91,19 +88,24 @@ def tile_factored_gain_correction_e3_kernel(tc, innov_words, innov_scales, obs_m
                 g_words[g, n] = tile[:, g - lo, :]
 
         def load_v(q):
-            nc.sync.dma_start(out=v_raw[q][:], in_=v_rows[q])
+            if q not in BY_VECTOR:
+                nc.sync.dma_start(out=v_raw[q][:], in_=v_rows[q])
+            else:
+                quarters = state_modes[256 * q : 256 * (q + 1), :].rearrange("(j x) (r c w) -> c j (x r) w", x=8, r=2, c=4)
+                for c in range(4):
+                    rows = v_raw[q][32 * c : 32 * (c + 1)].rearrange("p i (y w) -> p (i y) w", w=128)
+                    nc.sync.dma_start(out=rows, in_=quarters[c])
 
         for g in range(KG):
             load_u(g, (0, 1))
-            if g == 0:
-                nc.sync.dma_start(out=ratio_rows[0:2, :].bitcast(BF16), in_=mode_ratio.rearrange("(r c) -> r c", r=2))
             load_w(g, g + 1, 0)
             if g == 0:
                 load_scales(0)
+                nc.sync.dma_start(out=ratio_rows[0:2, :].bitcast(BF16), in_=mode_ratio.rearrange("(r c) -> r c", r=2))
         load_scales(1)
         load_w(0, 2, 1)
         load_w(2, 4, 1)
-        for q in range(SP):
+        for q in (0, 1, 2, 3, 4, 6, 5, 7):
             load_v(q)
 
         ratio_bank = bank(7)
@@ -113,7 +115,7 @@ def tile_factored_gain_correction_e3_kernel(tc, innov_words, innov_scales, obs_m
         gain_steps = [
             lambda: nc.vector.tensor_copy(out=ratio32[:].rearrange("p (r u e) -> p r u e", r=2, u=2), in_=ratio_turned),
             lambda: nc.vector.tensor_tensor(out=square[:], in0=ratio32[:], in1=ratio32[:], op=MULT),
-            lambda: nc.vector.tensor_tensor(out=square[:], in0=square[:], in1=ones[:], op=ADD),
+            lambda: nc.vector.tensor_scalar_add(square[:], square[:], 1.0),
             lambda: nc.vector.reciprocal(square[:], square[:]),
             lambda: nc.vector.tensor_tensor(out=gain[:], in0=ratio32[:], in1=square[:], op=MULT),
         ]
@@ -148,6 +150,21 @@ def tile_factored_gain_correction_e3_kernel(tc, innov_words, innov_scales, obs_m
                 v_group[q] = work.tile([P, 2, 2, P, 4], BF16, name="v_group", tag="v_group", bufs=3, align_bytes=256)
             dst = v_group[q][:, a % 2].rearrange("p g s t -> p g (s t)").bitcast(F32).rearrange("p g (s u) -> p g s u", u=2)
             copy(engine, dst, v_bank[a][:].rearrange("p (g u s) -> p g s u", g=2, u=2))
+
+        def order_blocks(q):
+            v_words[q] = work.tile([P, 2, 2, 2, P], F32, name="v_words", tag="v_words", bufs=3, align_bytes=256)
+            src = v_raw[q][:].rearrange("p i r -> p (i r)").bitcast(F32).rearrange("p (y m u) -> p y u m", y=16, u=2)
+            copy("v", v_words[q][:].rearrange("p i g u (y m) -> p (i g u y) m", m=32).rearrange("p (y u) m -> p y u m", u=2), src)
+
+        def turn_blocks(q):
+            nc.vector.transpose(v_raw[q][:].rearrange("p i r -> p (i r)").bitcast(F32), v_words[q][:].rearrange("p i g u m -> p (i g u m)"))
+
+        def group_blocks(q, half):
+            if q not in v_group:
+                v_group[q] = work.tile([P, 2, 2, P, 4], BF16, name="v_group", tag="v_group", bufs=3, align_bytes=256)
+            dst = v_group[q][:].rearrange("p i g s t -> p (i g s t)").bitcast(F32).rearrange("p (y j b u) -> p y j b u", y=4, b=4, u=2)
+            src = v_raw[q][:].rearrange("p i r -> p (i r)").bitcast(F32).rearrange("p (b y u j) -> p y j b u", b=4, y=4, u=2)
+            copy("v", dst[:, :, :, 2 * half : 2 * half + 2], src[:, :, :, 2 * half : 2 * half + 2])
 
         def quantize_v(q):
             nc.vector.quantize_mx(out=v_codes[q][:].bitcast(E4), scales=v_scales[q][:], in_=v_group[q][:].rearrange("p i g s t -> p (i g s t)"))
@@ -251,30 +268,14 @@ def tile_factored_gain_correction_e3_kernel(tc, innov_words, innov_scales, obs_m
                 stage1(g, r, 1, t)
             empty_z(r, 1, t, "s")
 
-        def gain_step():
-            if gain_steps:
-                gain_steps.pop(0)()
-
         for g in range(KG):
-            if g in (0, KG - 1):
-                group_half(g, 0, U_CUTS[0])
-                group_u(g, 1, "v", slice(0, EDGE_CUTS[0]))
-                group_u(g, 1, "s", slice(EDGE_CUTS[1], P))
-                for lo, hi in ((0, 1), (1, 2), (2, 4)):
-                    quantize_u(g, 0, lo, hi)
-                group_u(g, 1, "v", slice(EDGE_CUTS[0], EDGE_CUTS[1]))
-                passes(g, 0, 0)
-                gain_step()
-                for lo, hi in ((0, 1), (1, 2), (2, 4)):
-                    quantize_u(g, 1, lo, hi)
-                passes(g, 1, 0)
-            else:
-                for r in range(2):
-                    group_half(g, r, U_CUTS[r])
-                for r in range(2):
-                    quantize_pairs(g, r)
-                    gain_step()
-                    passes(g, r, 0)
+            for r in range(2):
+                group_half(g, r, U_CUTS[r])
+            for r in range(2):
+                quantize_pairs(g, r)
+                if gain_steps:
+                    gain_steps.pop(0)()
+                passes(g, r, 0)
         for r in range(2):
             for t in range(4):
                 empty_z(r, 0, t, "ssvs"[t] if r == 0 else "vsvs"[t])
@@ -300,21 +301,19 @@ def tile_factored_gain_correction_e3_kernel(tc, innov_words, innov_scales, obs_m
         quantize_h(0, 1)
         for t in range(4):
             sweep(1, t)
-        order_v(4)
         group_h(1, 1)
         for a in range(4):
             stage2(a, 0)
             empty_out(a, 0, "s")
             store(a, 0, 512)
         quantize_h(1, 1)
-        for a in range(4, 10):
+        for a in range(4, 8):
             transpose_v(a)
             empty_v(a, "vs"[a % 2])
         quantize_v(2)
+        order_v(4)
         quantize_v(3)
-        order_v(5)
-        quantize_v(4)
-        order_v(6)
+        order_blocks(5)
         for a in range(2):
             stage2(a, 1, (0,))
         for a in range(4):
@@ -326,25 +325,36 @@ def tile_factored_gain_correction_e3_kernel(tc, innov_words, innov_scales, obs_m
             for n in range(2):
                 stage2(a, n)
                 empty_out(a, n, engines[n])
-                if a in HALVES:
+                if a == ST - 6:
                     store(a, 512 * n, 512 * (n + 1))
-            if a not in HALVES:
+            if a != ST - 6:
                 store(a)
 
-        def turn_v(lo, hi):
-            for a in range(lo, hi):
-                transpose_v(a)
-                empty_v(a, "sv"[a % 2])
-            for q in range(lo // 2, hi // 2):
-                quantize_v(q)
-
-        for a in range(4, 8):
-            finish(a, "sv" if a % 2 else "ss")
-        turn_v(10, 14)
-        order_v(7)
-        for a in range(8, 12):
-            finish(a, "sv" if a % 2 else "ss")
-        turn_v(14, 16)
-        finish(12, "ss")
-        for a in range(13, ST):
+        turn_blocks(5)
+        finish(4, "ss")
+        finish(5, "ss")
+        order_blocks(7)
+        for a in range(8, 10):
+            transpose_v(a)
+            empty_v(a, "sv"[a % 2])
+        order_v(6)
+        quantize_v(4)
+        finish(6, "ss")
+        group_blocks(5, 0)
+        group_blocks(5, 1)
+        finish(7, "sv")
+        quantize_v(5)
+        turn_blocks(7)
+        finish(8, "ss")
+        finish(9, "sv")
+        for a in range(12, 14):
+            transpose_v(a)
+            empty_v(a, "sv"[a % 2])
+        group_blocks(7, 0)
+        quantize_v(6)
+        group_blocks(7, 1)
+        finish(10, "ss")
+        finish(11, "sv")
+        quantize_v(7)
+        for a in range(12, ST):
             finish(a, "sv")

@@ -22,7 +22,7 @@ ST = S // P
 SP = ST // 2
 RESULT_BUFS = 7
 BY_VECTOR = (5, 7)
-U_CUTS = (84, 60)
+U_CUTS = (90, 68)
 
 
 def tile_factored_gain_correction_e3_kernel(tc, innov_words, innov_scales, obs_modes, mode_ratio, state_modes, out):

@@ -20,9 +20,14 @@ P = 128
 KG = K // 512
 ST = S // P
 SP = ST // 2
+BY_VECTOR = (4, 5, 6, 7)
+NARROW = ((0, 0),)
 RESULT_BUFS = 7
-BY_VECTOR = (5, 7)
-U_CUTS = (90, 68)
+WORD_BUFS = 4
+GROUP_BUFS = 3
+H_BUFS = 2
+ROW_BUFS = 2
+U_CUT = 32
 
 
 def tile_factored_gain_correction_e3_kernel(tc, innov_words, innov_scales, obs_modes, mode_ratio, state_modes, out):
@@ -36,15 +41,12 @@ def tile_factored_gain_correction_e3_kernel(tc, innov_words, innov_scales, obs_m
         psum = ctx.enter_context(tc.psum_pool(name="psum", bufs=1))
         ctx.enter_context(tc.manual_schedule())
 
-        def bank(b):
-            return psum.tile([P, 512], F32, name="bank%d" % b, tag="bank%d" % b)
-
         turn = [0]
 
         def next_bank():
             b = turn[0]
             turn[0] = (b + 1) % 8
-            return bank(b)
+            return psum.tile([P, 512], F32, name="bank%d" % b, tag="bank%d" % b)
 
         ident = keep.tile([P, P], F32, name="ident", align_bytes=256)
         ratio_rows = keep.tile([P, 256], F32, name="ratio_rows", align_bytes=256)
@@ -73,12 +75,11 @@ def tile_factored_gain_correction_e3_kernel(tc, innov_words, innov_scales, obs_m
             for j in range(4):
                 nc.sync.dma_start(out=g_scales[n][j:P:32, :, :].bitcast(I32), in_=scale_rows[j].bitcast(I32))
 
-        def load_u(g, halves):
-            lo, hi = 512 * halves[0], 512 * (halves[-1] + 1)
-            raw = keep.tile([P, 4, hi - lo], BF16, name="u_raw%d_%d" % (g, lo), align_bytes=256)
-            nc.sync.dma_start(out=raw[:], in_=obs_modes[512 * g : 512 * (g + 1), lo:hi].rearrange("(p j) w -> p j w", j=4))
-            for r in halves:
-                u_raw[g, r] = raw[:, :, 512 * r - lo : 512 * (r + 1) - lo]
+        def load_u(g):
+            raw = keep.tile([P, 4, R], BF16, name="u_raw%d" % g, align_bytes=256)
+            nc.sync.dma_start(out=raw[:], in_=obs_modes[512 * g : 512 * (g + 1), :].rearrange("(p j) w -> p j w", j=4))
+            for r in range(2):
+                u_raw[g, r] = raw[:, :, 512 * r : 512 * (r + 1)]
 
         def load_w(lo, hi, n):
             tile = keep.tile([P, hi - lo, 512], U32, name="g_words%d_%d" % (lo, n), align_bytes=256)
@@ -97,7 +98,7 @@ def tile_factored_gain_correction_e3_kernel(tc, innov_words, innov_scales, obs_m
                     nc.sync.dma_start(out=rows, in_=quarters[c])
 
         for g in range(KG):
-            load_u(g, (0, 1))
+            load_u(g)
             load_w(g, g + 1, 0)
             if g == 0:
                 load_scales(0)
@@ -105,10 +106,10 @@ def tile_factored_gain_correction_e3_kernel(tc, innov_words, innov_scales, obs_m
         load_scales(1)
         load_w(0, 2, 1)
         load_w(2, 4, 1)
-        for q in (0, 1, 2, 3, 4, 6, 5, 7):
+        for q in range(SP):
             load_v(q)
 
-        ratio_bank = bank(7)
+        ratio_bank = psum.tile([P, 512], F32, name="ratio_bank", tag="bank7")
         for u in range(2):
             nc.tensor.transpose(ratio_bank[:, P * u : P * (u + 1)], ratio_rows[:, u:256:2], ident[:])
         ratio_turned = ratio_bank[:, : 2 * P].bitcast(BF16).rearrange("p (u k e) -> p k u e", u=2, e=2)[:, 0:2]
@@ -130,53 +131,52 @@ def tile_factored_gain_correction_e3_kernel(tc, innov_words, innov_scales, obs_m
         v_group = {}
         v_bank = {}
 
-        def order_v(q):
-            v_words[q] = work.tile([P, 2, 2, 2, P], F32, name="v_words", tag="v_words", bufs=3, align_bytes=256)
-            src = v_raw[q][:].rearrange("p i r -> p (i r)").bitcast(F32).rearrange("p (x m u) -> p x u m", x=4, u=2)
-            copy("v", v_words[q][:].rearrange("p i g u m -> p (i g) u m"), src)
+        def words_tile(q):
+            v_words[q] = work.tile([P, 1024], F32, name="v_words", tag="v_words", bufs=WORD_BUFS, align_bytes=256)
+            return v_words[q]
+
+        def group_tile(q):
+            if q not in v_group:
+                v_group[q] = work.tile([P, 2048], BF16, name="v_group", tag="v_group", bufs=GROUP_BUFS, align_bytes=256)
+            return v_group[q]
+
+        def raw_words(q):
+            return v_raw[q][:].rearrange("p i r -> p (i r)").bitcast(F32)
+
+        def order_v(q, engine="v"):
+            run = 32 if q in BY_VECTOR else P
+            src = raw_words(q).rearrange("p (x m u) -> p x u m", m=run, u=2)
+            copy(engine, words_tile(q)[:].rearrange("p (x u m) -> p x u m", m=run, u=2), src)
 
         def transpose_v(a):
             v_bank[a] = next_bank()
             for c in range(4):
-                if a // 2 in v_words:
-                    words = v_words[a // 2][:, a % 2, c // 2, c % 2, :]
-                else:
-                    words = v_raw[a // 2][:, a % 2, :].bitcast(F32)[:, 256 * (c // 2) + c % 2 : 256 * (c // 2 + 1) : 2]
-                nc.tensor.transpose(v_bank[a][:, 128 * c : 128 * (c + 1)], words, ident[:])
+                first = 512 * (a % 2) + P * c
+                nc.tensor.transpose(v_bank[a][:, P * c : P * (c + 1)], v_words[a // 2][:, first : first + P], ident[:])
 
         def empty_v(a, engine):
-            q = a // 2
-            if q not in v_group:
-                v_group[q] = work.tile([P, 2, 2, P, 4], BF16, name="v_group", tag="v_group", bufs=3, align_bytes=256)
-            dst = v_group[q][:, a % 2].rearrange("p g s t -> p g (s t)").bitcast(F32).rearrange("p g (s u) -> p g s u", u=2)
+            dst = group_tile(a // 2)[:, 1024 * (a % 2) : 1024 * (a % 2 + 1)].bitcast(F32).rearrange("p (g s u) -> p g s u", g=2, u=2)
             copy(engine, dst, v_bank[a][:].rearrange("p (g u s) -> p g s u", g=2, u=2))
 
-        def order_blocks(q):
-            v_words[q] = work.tile([P, 2, 2, 2, P], F32, name="v_words", tag="v_words", bufs=3, align_bytes=256)
-            src = v_raw[q][:].rearrange("p i r -> p (i r)").bitcast(F32).rearrange("p (y m u) -> p y u m", y=16, u=2)
-            copy("v", v_words[q][:].rearrange("p i g u (y m) -> p (i g u y) m", m=32).rearrange("p (y u) m -> p y u m", u=2), src)
-
         def turn_blocks(q):
-            nc.vector.transpose(v_raw[q][:].rearrange("p i r -> p (i r)").bitcast(F32), v_words[q][:].rearrange("p i g u m -> p (i g u m)"))
+            nc.vector.transpose(raw_words(q), v_words[q][:])
 
         def group_blocks(q, half):
-            if q not in v_group:
-                v_group[q] = work.tile([P, 2, 2, P, 4], BF16, name="v_group", tag="v_group", bufs=3, align_bytes=256)
-            dst = v_group[q][:].rearrange("p i g s t -> p (i g s t)").bitcast(F32).rearrange("p (y j b u) -> p y j b u", y=4, b=4, u=2)
-            src = v_raw[q][:].rearrange("p i r -> p (i r)").bitcast(F32).rearrange("p (b y u j) -> p y j b u", b=4, y=4, u=2)
+            dst = group_tile(q)[:].bitcast(F32).rearrange("p (y j b u) -> p y j b u", y=4, b=4, u=2)
+            src = raw_words(q).rearrange("p (b y u j) -> p y j b u", b=4, y=4, u=2)
             copy("v", dst[:, :, :, 2 * half : 2 * half + 2], src[:, :, :, 2 * half : 2 * half + 2])
 
         def quantize_v(q):
-            nc.vector.quantize_mx(out=v_codes[q][:].bitcast(E4), scales=v_scales[q][:], in_=v_group[q][:].rearrange("p i g s t -> p (i g s t)"))
+            nc.vector.quantize_mx(out=v_codes[q][:].bitcast(E4), scales=v_scales[q][:], in_=v_group[q][:])
 
         u_group = {}
 
-        def group_u(g, r, engine, rows, slots=slice(0, 4)):
+        def group_u(g, r, engine, lo, hi):
             if (g, r) not in u_group:
                 u_group[g, r] = work.tile([P, 4, P, 4], BF16, name="u_group", tag="u_group", bufs=4, align_bytes=256)
             src = u_raw[g, r].rearrange("p j (m t) -> p m j t", t=4)
             dst = u_group[g, r][:].rearrange("p t m j -> p m j t")
-            copy(engine, dst[:, rows, :, slots], src[:, rows, :, slots])
+            copy(engine, dst[:, lo:hi], src[:, lo:hi])
 
         def quantize_u(g, r, lo=0, hi=4):
             cols = slice(128 * lo, 128 * hi)
@@ -188,40 +188,76 @@ def tile_factored_gain_correction_e3_kernel(tc, innov_words, innov_scales, obs_m
 
         z = {}
 
-        def stage1(g, r, n, t):
-            if g == 0:
-                z[r, n, t] = next_bank()
+        def stage1(out_ap, g, r, n, t, members, start, stop):
             m = slice(128 * t, 128 * (t + 1))
             nc.tensor.matmul_mx(
-                out=z[r, n, t][:],
+                out=out_ap,
                 lhsT=u_codes[g, r][:, m].bitcast(E4),
                 lhsT_scale=u_scales[g, r][:, m],
-                rhs=g_words[g, n].bitcast(E5),
-                rhs_scale=g_scales[n][:, g, :],
-                start=(g == 0),
-                stop=(g == KG - 1),
+                rhs=g_words[g, n][:, members].bitcast(E5),
+                rhs_scale=g_scales[n][:, g, members],
+                start=start,
+                stop=stop,
             )
+
+        def wide_pass(g, r, n, t):
+            if g == 0:
+                z[r, n, t] = next_bank()
+            stage1(z[r, n, t][:], g, r, n, t, slice(0, 512), g == 0, g == KG - 1)
+
+        def narrow_pass(g, r, n, t, b):
+            if g == 0 and t == 0:
+                z[r, n, b] = next_bank()
+            stage1(z[r, n, b][:, P * t : P * (t + 1)], g, r, n, t, slice(P * b, P * (b + 1)), g == 0 and t == 0, g == KG - 1 and t == 3)
+
+        def passes(g, r, n):
+            for t in range(4):
+                if (r, n) in NARROW:
+                    for b in range(4):
+                        narrow_pass(g, r, n, t, b)
+                else:
+                    wide_pass(g, r, n, t)
+
+        def sweep_bank(r, n, b):
+            for g in range(KG):
+                if (r, n) in NARROW:
+                    for t in range(4):
+                        narrow_pass(g, r, n, t, b)
+                else:
+                    wide_pass(g, r, n, b)
 
         h_rows = {}
         h_group = {}
 
-        def empty_z(r, n, t, engine):
+        def h_tile(r, n):
+            if (r, n) not in h_group:
+                h_group[r, n] = work.tile([P, 512, 4], BF16, name="h_group", tag="h_group", bufs=H_BUFS, align_bytes=256)
+            return h_group[r, n]
+
+        def empty_z(r, n, b, engine="v"):
+            if (r, n) in NARROW:
+                gains = gain[:, 4 * r : 4 * r + 4].rearrange("p (o t) -> p o t", o=1).to_broadcast([P, P, 4])
+                sums = z[r, n, b][:].rearrange("p (t c) -> p c t", t=4)
+                nc.vector.tensor_tensor(out=h_tile(r, n)[:, P * b : P * (b + 1), :], in0=sums, in1=gains, op=MULT)
+                return
             if (r, n) not in h_rows:
-                h_rows[r, n] = work.tile([P, 4, 512], BF16, name="h_rows", tag="h_rows", bufs=3, align_bytes=256)
-            scale = gain[:, 4 * r + t : 4 * r + t + 1]
+                h_rows[r, n] = work.tile([P, 4, 512], BF16, name="h_rows", tag="h_rows", bufs=ROW_BUFS, align_bytes=256)
+            scale = gain[:, 4 * r + b : 4 * r + b + 1]
             if engine == "s":
-                nc.scalar.activation(out=h_rows[r, n][:, t, :], in_=z[r, n, t][:], func=COPY, scale=scale)
+                nc.scalar.activation(out=h_rows[r, n][:, b, :], in_=z[r, n, b][:], func=COPY, scale=scale)
             else:
-                nc.vector.tensor_scalar_mul(h_rows[r, n][:, t, :], z[r, n, t][:], scale)
+                nc.vector.tensor_scalar_mul(h_rows[r, n][:, b, :], z[r, n, b][:], scale)
 
         def group_h(r, n, engine="v", lo=0, hi=P):
-            if (r, n) not in h_group:
-                h_group[r, n] = work.tile([P, 512, 4], BF16, name="h_group", tag="h_group", bufs=2, align_bytes=256)
             src = h_rows[r, n][:].rearrange("p t (c i) -> p c t i", i=4)
-            copy(engine, h_group[r, n][:].rearrange("p (c i) t -> p c t i", i=4)[:, lo:hi], src[:, lo:hi])
+            copy(engine, h_tile(r, n)[:].rearrange("p (c i) t -> p c t i", i=4)[:, lo:hi], src[:, lo:hi])
 
-        def quantize_h(r, n):
-            nc.vector.quantize_mx(out=h_codes[r, n][:].bitcast(E5), scales=h_scales[r, n][:], in_=h_group[r, n][:].rearrange("p n t -> p (n t)"))
+        def quantize_h(r, n, lo=0, hi=512):
+            nc.vector.quantize_mx(
+                out=h_codes[r, n][:, lo:hi].bitcast(E5),
+                scales=h_scales[r, n][:, lo:hi],
+                in_=h_group[r, n][:, lo:hi].rearrange("p n t -> p (n t)"),
+            )
 
         acc = {}
 
@@ -243,81 +279,79 @@ def tile_factored_gain_correction_e3_kernel(tc, innov_words, innov_scales, obs_m
 
         results = {}
 
-        def empty_out(a, n, engine, lo=0, hi=512):
+        def empty_out(a, n, engine):
             if a not in results:
                 results[a] = work.tile([P, 1, N], F32, name="result", tag="result", bufs=RESULT_BUFS, align_bytes=256)
-            copy(engine, results[a][:, 0, 512 * n + lo : 512 * n + hi], acc[a, n][:, lo:hi])
+            copy(engine, results[a][:, 0, 512 * n : 512 * (n + 1)], acc[a, n][:])
 
         def store(a, lo=0, hi=N):
             nc.sync.dma_start(out=out_rows[a // 2][:, a % 2 : a % 2 + 1, lo:hi], in_=results[a][:, :, lo:hi])
 
-        def group_half(g, r, cut):
-            group_u(g, r, "v", slice(0, cut))
-            group_u(g, r, "s", slice(cut, P))
-
-        def quantize_pairs(g, r):
-            quantize_u(g, r, 0, 2)
-            quantize_u(g, r, 2, 4)
-
-        def passes(g, r, n):
-            for t in range(4):
-                stage1(g, r, n, t)
-
-        def sweep(r, t):
-            for g in range(KG):
-                stage1(g, r, 1, t)
-            empty_z(r, 1, t, "s")
-
-        for g in range(KG):
+        for g in range(KG - 1):
+            group_u(g, 1, "s", U_CUT, P)
+            group_u(g, 0, "v", 0, P)
+            group_u(g, 1, "v", 0, U_CUT)
             for r in range(2):
-                group_half(g, r, U_CUTS[r])
-            for r in range(2):
-                quantize_pairs(g, r)
+                quantize_u(g, r)
                 if gain_steps:
                     gain_steps.pop(0)()
                 passes(g, r, 0)
-        for r in range(2):
-            for t in range(4):
-                empty_z(r, 0, t, "ssvs"[t] if r == 0 else "vsvs"[t])
-        group_h(0, 0)
+        g = KG - 1
+        group_u(g, 0, "v", 0, 88)
+        group_u(g, 0, "s", 88, P)
+        group_u(g, 1, "s", 64, P)
+        group_u(g, 1, "v", 0, 24)
+        quantize_u(g, 0, 0, 2)
+        quantize_u(g, 0, 2, 4)
+        group_u(g, 1, "v", 24, 64)
+        passes(g, 0, 0)
+        quantize_u(g, 1, 0, 2)
+        quantize_u(g, 1, 2, 4)
+        passes(g, 1, 0)
+
+        for b in range(4):
+            empty_z(0, 0, b)
+            empty_z(1, 0, b, "s")
         order_v(0)
         quantize_h(0, 0)
         order_v(1)
-        group_h(1, 0)
         for t in range(4):
-            sweep(0, t)
+            sweep_bank(0, 1, t)
+            empty_z(0, 1, t, "s")
+            if t < 2:
+                group_h(1, 0, "s", 32 * t, 32 * (t + 1))
+        group_h(1, 0, "v", 64, P)
+        order_v(2)
+        quantize_h(1, 0)
+        order_v(3)
         for a in range(4):
             transpose_v(a)
-        empty_v(0, "v")
-        quantize_h(1, 0)
-        empty_v(1, "s")
-        empty_v(2, "s")
-        empty_v(3, "s")
-        order_v(2)
-        quantize_v(0)
+            empty_v(a, "vsvs"[a])
         group_h(0, 1)
-        quantize_v(1)
-        order_v(3)
+        quantize_v(0)
         quantize_h(0, 1)
+        quantize_v(1)
+        order_v(4)
         for t in range(4):
-            sweep(1, t)
+            sweep_bank(1, 1, t)
+            empty_z(1, 1, t, "s")
+        turn_blocks(4)
         group_h(1, 1)
         for a in range(4):
             stage2(a, 0)
             empty_out(a, 0, "s")
             store(a, 0, 512)
+        group_blocks(4, 0)
         quantize_h(1, 1)
         for a in range(4, 8):
             transpose_v(a)
-            empty_v(a, "vs"[a % 2])
+            empty_v(a, "svss"[a % 4])
+        group_blocks(4, 1)
         quantize_v(2)
-        order_v(4)
+        order_v(5)
         quantize_v(3)
-        order_blocks(5)
-        for a in range(2):
-            stage2(a, 1, (0,))
         for a in range(4):
-            stage2(a, 1, (1,) if a < 2 else (0, 1))
+            stage2(a, 1)
             empty_out(a, 1, "s")
             store(a, 512, N)
 
@@ -325,36 +359,18 @@ def tile_factored_gain_correction_e3_kernel(tc, innov_words, innov_scales, obs_m
             for n in range(2):
                 stage2(a, n)
                 empty_out(a, n, engines[n])
-                if a == ST - 6:
-                    store(a, 512 * n, 512 * (n + 1))
-            if a != ST - 6:
-                store(a)
+            store(a)
 
-        turn_blocks(5)
-        finish(4, "ss")
-        finish(5, "ss")
-        order_blocks(7)
-        for a in range(8, 10):
-            transpose_v(a)
-            empty_v(a, "sv"[a % 2])
-        order_v(6)
-        quantize_v(4)
-        finish(6, "ss")
-        group_blocks(5, 0)
-        group_blocks(5, 1)
-        finish(7, "sv")
-        quantize_v(5)
-        turn_blocks(7)
-        finish(8, "ss")
-        finish(9, "sv")
-        for a in range(12, 14):
-            transpose_v(a)
-            empty_v(a, "sv"[a % 2])
-        group_blocks(7, 0)
-        quantize_v(6)
-        group_blocks(7, 1)
-        finish(10, "ss")
-        finish(11, "sv")
-        quantize_v(7)
-        for a in range(12, ST):
+        for q in range(5, SP):
+            turn_blocks(q)
+            quantize_v(q - 1)
+            group_blocks(q, 0)
+            group_blocks(q, 1)
+            if q + 1 < SP:
+                order_v(q + 1)
+            finish(2 * q - 6, "ss")
+            finish(2 * q - 5, "ss")
+        finish(10, "sv")
+        quantize_v(SP - 1)
+        for a in range(11, ST):
             finish(a, "sv")

@@ -20,14 +20,15 @@ P = 128
 KG = K // 512
 ST = S // P
 SP = ST // 2
-BY_VECTOR = (4, 5, 6, 7)
+BY_VECTOR = (4, 5, 6)
 NARROW = ((0, 0),)
-RESULT_BUFS = 7
+WIDE_BUFS = 7
 WORD_BUFS = 4
 GROUP_BUFS = 3
 H_BUFS = 2
 ROW_BUFS = 2
 U_CUT = 32
+SINGLE_FROM = 10
 
 
 def tile_factored_gain_correction_e3_kernel(tc, innov_words, innov_scales, obs_modes, mode_ratio, state_modes, out):
@@ -76,7 +77,7 @@ def tile_factored_gain_correction_e3_kernel(tc, innov_words, innov_scales, obs_m
                 nc.sync.dma_start(out=g_scales[n][j:P:32, :, :].bitcast(I32), in_=scale_rows[j].bitcast(I32))
 
         def load_u(g):
-            raw = keep.tile([P, 4, R], BF16, name="u_raw%d" % g, align_bytes=256)
+            raw = work.tile([P, 4, R], BF16, name="u_raw", tag="wide", bufs=WIDE_BUFS, align_bytes=256)
             nc.sync.dma_start(out=raw[:], in_=obs_modes[512 * g : 512 * (g + 1), :].rearrange("(p j) w -> p j w", j=4))
             for r in range(2):
                 u_raw[g, r] = raw[:, :, 512 * r : 512 * (r + 1)]
@@ -280,12 +281,15 @@ def tile_factored_gain_correction_e3_kernel(tc, innov_words, innov_scales, obs_m
         results = {}
 
         def empty_out(a, n, engine):
-            if a not in results:
-                results[a] = work.tile([P, 1, N], F32, name="result", tag="result", bufs=RESULT_BUFS, align_bytes=256)
-            copy(engine, results[a][:, 0, 512 * n : 512 * (n + 1)], acc[a, n][:])
+            if a // 2 not in results:
+                results[a // 2] = work.tile([P, 2, N], F32, name="result", tag="wide", bufs=WIDE_BUFS, align_bytes=256)
+            copy(engine, results[a // 2][:, a % 2, 512 * n : 512 * (n + 1)], acc[a, n][:])
 
         def store(a, lo=0, hi=N):
-            nc.sync.dma_start(out=out_rows[a // 2][:, a % 2 : a % 2 + 1, lo:hi], in_=results[a][:, :, lo:hi])
+            nc.sync.dma_start(out=out_rows[a // 2][:, a % 2 : a % 2 + 1, lo:hi], in_=results[a // 2][:, a % 2 : a % 2 + 1, lo:hi])
+
+        def store_pair(q, lo=0, hi=N):
+            nc.sync.dma_start(out=out_rows[q][:, :, lo:hi], in_=results[q][:, :, lo:hi])
 
         for g in range(KG - 1):
             group_u(g, 1, "s", U_CUT, P)
@@ -331,16 +335,18 @@ def tile_factored_gain_correction_e3_kernel(tc, innov_words, innov_scales, obs_m
         quantize_v(0)
         quantize_h(0, 1)
         quantize_v(1)
-        order_v(4)
         for t in range(4):
             sweep_bank(1, 1, t)
             empty_z(1, 1, t, "s")
+            if t == 0:
+                order_v(4, "s")
         turn_blocks(4)
         group_h(1, 1)
         for a in range(4):
             stage2(a, 0)
             empty_out(a, 0, "s")
-            store(a, 0, 512)
+            if a % 2:
+                store_pair(a // 2, 0, 512)
         group_blocks(4, 0)
         quantize_h(1, 1)
         for a in range(4, 8):
@@ -353,24 +359,38 @@ def tile_factored_gain_correction_e3_kernel(tc, innov_words, innov_scales, obs_m
         for a in range(4):
             stage2(a, 1)
             empty_out(a, 1, "s")
-            store(a, 512, N)
+            if a % 2:
+                store_pair(a // 2, 512, N)
 
         def finish(a, engines):
             for n in range(2):
                 stage2(a, n)
                 empty_out(a, n, engines[n])
-            store(a)
+            if a >= SINGLE_FROM:
+                store(a)
+            elif a % 2:
+                store_pair(a // 2)
 
-        for q in range(5, SP):
-            turn_blocks(q)
-            quantize_v(q - 1)
+
+        turn_blocks(5)
+        quantize_v(4)
+        for q in (5, 6):
             group_blocks(q, 0)
             group_blocks(q, 1)
-            if q + 1 < SP:
-                order_v(q + 1)
+            if q == 5:
+                order_v(6)
             finish(2 * q - 6, "ss")
+            quantize_v(q)
+            if q == 5:
+                turn_blocks(6)
+                order_v(7)
             finish(2 * q - 5, "ss")
-        finish(10, "sv")
-        quantize_v(SP - 1)
-        for a in range(11, ST):
+        for a in range(8, 11):
+            finish(a, "ss")
+        for a in (14, 15):
+            transpose_v(a)
+            empty_v(a, "v")
+        finish(11, "ss")
+        quantize_v(7)
+        for a in range(12, ST):
             finish(a, "sv")

@@ -21,14 +21,13 @@ KG = K // 512
 ST = S // P
 SP = ST // 2
 BY_VECTOR = (4, 5, 6)
-NARROW = ((0, 0),)
+NARROW = ()
 WIDE_BUFS = 7
 WORD_BUFS = 4
 GROUP_BUFS = 3
 H_BUFS = 2
-ROW_BUFS = 2
+ROW_BUFS = 3
 U_CUT = 32
-SINGLE_FROM = 10
 
 
 def tile_factored_gain_correction_e3_kernel(tc, innov_words, innov_scales, obs_modes, mode_ratio, state_modes, out):
@@ -288,8 +287,6 @@ def tile_factored_gain_correction_e3_kernel(tc, innov_words, innov_scales, obs_m
         def store(a, lo=0, hi=N):
             nc.sync.dma_start(out=out_rows[a // 2][:, a % 2 : a % 2 + 1, lo:hi], in_=results[a // 2][:, a % 2 : a % 2 + 1, lo:hi])
 
-        def store_pair(q, lo=0, hi=N):
-            nc.sync.dma_start(out=out_rows[q][:, :, lo:hi], in_=results[q][:, :, lo:hi])
 
         for g in range(KG - 1):
             group_u(g, 1, "s", U_CUT, P)
@@ -313,9 +310,10 @@ def tile_factored_gain_correction_e3_kernel(tc, innov_words, innov_scales, obs_m
         quantize_u(g, 1, 2, 4)
         passes(g, 1, 0)
 
-        for b in range(4):
-            empty_z(0, 0, b)
-            empty_z(1, 0, b, "s")
+        for r in range(2):
+            for t in range(4):
+                empty_z(r, 0, t, "ssvs"[t] if r == 0 else "vsvs"[t])
+        group_h(0, 0)
         order_v(0)
         quantize_h(0, 0)
         order_v(1)
@@ -345,8 +343,7 @@ def tile_factored_gain_correction_e3_kernel(tc, innov_words, innov_scales, obs_m
         for a in range(4):
             stage2(a, 0)
             empty_out(a, 0, "s")
-            if a % 2:
-                store_pair(a // 2, 0, 512)
+            store(a, 0, 512)
         group_blocks(4, 0)
         quantize_h(1, 1)
         for a in range(4, 8):
@@ -356,20 +353,18 @@ def tile_factored_gain_correction_e3_kernel(tc, innov_words, innov_scales, obs_m
         quantize_v(2)
         order_v(5)
         quantize_v(3)
+        for a in range(2):
+            stage2(a, 1, (0,))
         for a in range(4):
-            stage2(a, 1)
+            stage2(a, 1, (1,) if a < 2 else (0, 1))
             empty_out(a, 1, "s")
-            if a % 2:
-                store_pair(a // 2, 512, N)
+            store(a, 512, N)
 
         def finish(a, engines):
             for n in range(2):
                 stage2(a, n)
                 empty_out(a, n, engines[n])
-            if a >= SINGLE_FROM:
-                store(a)
-            elif a % 2:
-                store_pair(a // 2)
+            store(a)
 
 
         turn_blocks(5)
@@ -385,12 +380,13 @@ def tile_factored_gain_correction_e3_kernel(tc, innov_words, innov_scales, obs_m
                 turn_blocks(6)
                 order_v(7)
             finish(2 * q - 5, "ss")
-        for a in range(8, 11):
-            finish(a, "ss")
+        finish(8, "ss")
+        finish(9, "sv")
+        finish(10, "sv")
         for a in (14, 15):
             transpose_v(a)
-            empty_v(a, "v")
-        finish(11, "ss")
+            empty_v(a, "vs"[a % 2])
+        finish(11, "sv")
         quantize_v(7)
         for a in range(12, ST):
             finish(a, "sv")

@@ -20,14 +20,16 @@ P = 128
 KG = K // 512
 ST = S // P
 SP = ST // 2
+L = 32
 BY_VECTOR = (4, 5, 6)
-NARROW = ()
 WIDE_BUFS = 7
 WORD_BUFS = 4
 GROUP_BUFS = 3
 H_BUFS = 2
 ROW_BUFS = 3
-U_CUT = 32
+U_CUT = 8
+FIRST_CUT = 22
+LAST_CUT = 12
 
 
 def tile_factored_gain_correction_e3_kernel(tc, innov_words, innov_scales, obs_modes, mode_ratio, state_modes, out):
@@ -49,7 +51,8 @@ def tile_factored_gain_correction_e3_kernel(tc, innov_words, innov_scales, obs_m
             return psum.tile([P, 512], F32, name="bank%d" % b, tag="bank%d" % b)
 
         ident = keep.tile([P, P], F32, name="ident", align_bytes=256)
-        ratio_rows = keep.tile([P, 256], F32, name="ratio_rows", align_bytes=256)
+        ratio_rows = keep.tile([2, 256], F32, name="ratio_rows", align_bytes=256)
+        ratio_runs = keep.tile([P, 256], F32, name="ratio_runs", align_bytes=256)
         ratio32 = keep.tile([P, 8], F32, name="ratio32")
         square = keep.tile([P, 8], F32, name="square")
         gain = keep.tile([P, 8], F32, name="gain")
@@ -64,11 +67,14 @@ def tile_factored_gain_correction_e3_kernel(tc, innov_words, innov_scales, obs_m
         h_codes = {(r, n): keep.tile([P, 512], U32, name="h_codes%d_%d" % (r, n), align_bytes=256) for r in range(2) for n in range(2)}
         h_scales = {k: keep.tile([P, 512], U8, name="h_scales%d_%d" % k, align_bytes=256) for k in h_codes}
 
-        for n in range(2):
-            nc.vector.memset(g_scales[n][:].rearrange("p g n -> p (g n)").bitcast(I32), 0)
-        make_identity(nc, ident[:])
-        for half in range(2):
-            nc.scalar.activation(out=ratio_rows[:, P * half : P * (half + 1)], in_=ident[:], func=COPY, scale=0.0)
+        def copy(engine, out, in_):
+            if engine == "s":
+                nc.scalar.copy(out=out, in_=in_)
+            else:
+                nc.vector.tensor_copy(out=out, in_=in_)
+
+        def order_words(engine, dst, src, runs):
+            copy(engine, dst.rearrange("p (x u l w) -> p x u l w", u=2, l=runs, w=4), src.rearrange("p (x l u w) -> p x u l w", u=2, l=runs, w=4))
 
         def load_scales(n):
             scale_rows = innov_scales[:, :, 512 * n : 512 * (n + 1)].rearrange("g (q j) n -> j q g n", j=4)
@@ -88,52 +94,18 @@ def tile_factored_gain_correction_e3_kernel(tc, innov_words, innov_scales, obs_m
             for g in range(lo, hi):
                 g_words[g, n] = tile[:, g - lo, :]
 
-        def load_v(q):
+        def load_v(q, second=None):
             if q not in BY_VECTOR:
                 nc.sync.dma_start(out=v_raw[q][:], in_=v_rows[q])
-            else:
-                quarters = state_modes[256 * q : 256 * (q + 1), :].rearrange("(j x) (r c w) -> c j (x r) w", x=8, r=2, c=4)
-                for c in range(4):
-                    rows = v_raw[q][32 * c : 32 * (c + 1)].rearrange("p i (y w) -> p (i y) w", w=128)
-                    nc.sync.dma_start(out=rows, in_=quarters[c])
-
-        for g in range(KG):
-            load_u(g)
-            load_w(g, g + 1, 0)
-            if g == 0:
-                load_scales(0)
-                nc.sync.dma_start(out=ratio_rows[0:2, :].bitcast(BF16), in_=mode_ratio.rearrange("(r c) -> r c", r=2))
-        load_scales(1)
-        load_w(0, 2, 1)
-        load_w(2, 4, 1)
-        for q in range(SP):
-            load_v(q)
-
-        ratio_bank = psum.tile([P, 512], F32, name="ratio_bank", tag="bank7")
-        for u in range(2):
-            nc.tensor.transpose(ratio_bank[:, P * u : P * (u + 1)], ratio_rows[:, u:256:2], ident[:])
-        ratio_turned = ratio_bank[:, : 2 * P].bitcast(BF16).rearrange("p (u k e) -> p k u e", u=2, e=2)[:, 0:2]
-        gain_steps = [
-            lambda: nc.vector.tensor_copy(out=ratio32[:].rearrange("p (r u e) -> p r u e", r=2, u=2), in_=ratio_turned),
-            lambda: nc.vector.tensor_tensor(out=square[:], in0=ratio32[:], in1=ratio32[:], op=MULT),
-            lambda: nc.vector.tensor_scalar_add(square[:], square[:], 1.0),
-            lambda: nc.vector.reciprocal(square[:], square[:]),
-            lambda: nc.vector.tensor_tensor(out=gain[:], in0=ratio32[:], in1=square[:], op=MULT),
-        ]
-
-        def copy(engine, out, in_):
-            if engine == "s":
-                nc.scalar.copy(out=out, in_=in_)
-            else:
-                nc.vector.tensor_copy(out=out, in_=in_)
+                return
+            quarters = state_modes[256 * q : 256 * (q + 1), :].rearrange("(j x) (r c w) -> c j (x r) w", x=8, r=2, c=4)
+            for c in range(4):
+                rows = v_raw[q][32 * c : 32 * (c + 1)].rearrange("p i (y w) -> p (i y) w", w=128)
+                nc.sync.dma_start(out=rows, in_=quarters[c])
 
         v_words = {}
         v_group = {}
         v_bank = {}
-
-        def words_tile(q):
-            v_words[q] = work.tile([P, 1024], F32, name="v_words", tag="v_words", bufs=WORD_BUFS, align_bytes=256)
-            return v_words[q]
 
         def group_tile(q):
             if q not in v_group:
@@ -144,9 +116,8 @@ def tile_factored_gain_correction_e3_kernel(tc, innov_words, innov_scales, obs_m
             return v_raw[q][:].rearrange("p i r -> p (i r)").bitcast(F32)
 
         def order_v(q, engine="v"):
-            run = 32 if q in BY_VECTOR else P
-            src = raw_words(q).rearrange("p (x m u) -> p x u m", m=run, u=2)
-            copy(engine, words_tile(q)[:].rearrange("p (x u m) -> p x u m", m=run, u=2), src)
+            v_words[q] = work.tile([P, 1024], F32, name="v_words", tag="v_words", bufs=WORD_BUFS, align_bytes=256)
+            order_words(engine, v_words[q][:], raw_words(q), L // 4 if q in BY_VECTOR else L)
 
         def transpose_v(a):
             v_bank[a] = next_bank()
@@ -161,22 +132,22 @@ def tile_factored_gain_correction_e3_kernel(tc, innov_words, innov_scales, obs_m
         def turn_blocks(q):
             nc.vector.transpose(raw_words(q), v_words[q][:])
 
-        def group_blocks(q, half):
+        def group_blocks(q, half, engine="v"):
             dst = group_tile(q)[:].bitcast(F32).rearrange("p (y j b u) -> p y j b u", y=4, b=4, u=2)
             src = raw_words(q).rearrange("p (b y u j) -> p y j b u", b=4, y=4, u=2)
-            copy("v", dst[:, :, :, 2 * half : 2 * half + 2], src[:, :, :, 2 * half : 2 * half + 2])
+            copy(engine, dst[:, :, :, 2 * half : 2 * half + 2], src[:, :, :, 2 * half : 2 * half + 2])
 
         def quantize_v(q):
             nc.vector.quantize_mx(out=v_codes[q][:].bitcast(E4), scales=v_scales[q][:], in_=v_group[q][:])
 
         u_group = {}
 
-        def group_u(g, r, engine, lo, hi):
+        def group_u(g, r, u, engine, lo=0, hi=L):
             if (g, r) not in u_group:
                 u_group[g, r] = work.tile([P, 4, P, 4], BF16, name="u_group", tag="u_group", bufs=4, align_bytes=256)
-            src = u_raw[g, r].rearrange("p j (m t) -> p m j t", t=4)
-            dst = u_group[g, r][:].rearrange("p t m j -> p m j t")
-            copy(engine, dst[:, lo:hi], src[:, lo:hi])
+            src = u_raw[g, r].rearrange("p k (l u h j e) -> p u l h k j e", u=2, h=2, j=2, e=2)
+            dst = u_group[g, r][:].rearrange("p (u e) (l h j) k -> p u l h k j e", u=2, h=2, j=2)
+            copy(engine, dst[:, u, lo:hi], src[:, u, lo:hi])
 
         def quantize_u(g, r, lo=0, hi=4):
             cols = slice(128 * lo, 128 * hi)
@@ -188,75 +159,48 @@ def tile_factored_gain_correction_e3_kernel(tc, innov_words, innov_scales, obs_m
 
         z = {}
 
-        def stage1(out_ap, g, r, n, t, members, start, stop):
-            m = slice(128 * t, 128 * (t + 1))
-            nc.tensor.matmul_mx(
-                out=out_ap,
-                lhsT=u_codes[g, r][:, m].bitcast(E4),
-                lhsT_scale=u_scales[g, r][:, m],
-                rhs=g_words[g, n][:, members].bitcast(E5),
-                rhs_scale=g_scales[n][:, g, members],
-                start=start,
-                stop=stop,
-            )
+        def stage1(g, r, n, slots):
+            for t in slots:
+                if g == 0:
+                    z[r, n, t] = next_bank()
+                m = slice(128 * t, 128 * (t + 1))
+                nc.tensor.matmul_mx(
+                    out=z[r, n, t][:],
+                    lhsT=u_codes[g, r][:, m].bitcast(E4),
+                    lhsT_scale=u_scales[g, r][:, m],
+                    rhs=g_words[g, n].bitcast(E5),
+                    rhs_scale=g_scales[n][:, g, :],
+                    start=(g == 0),
+                    stop=(g == KG - 1),
+                )
 
-        def wide_pass(g, r, n, t):
-            if g == 0:
-                z[r, n, t] = next_bank()
-            stage1(z[r, n, t][:], g, r, n, t, slice(0, 512), g == 0, g == KG - 1)
-
-        def narrow_pass(g, r, n, t, b):
-            if g == 0 and t == 0:
-                z[r, n, b] = next_bank()
-            stage1(z[r, n, b][:, P * t : P * (t + 1)], g, r, n, t, slice(P * b, P * (b + 1)), g == 0 and t == 0, g == KG - 1 and t == 3)
-
-        def passes(g, r, n):
-            for t in range(4):
-                if (r, n) in NARROW:
-                    for b in range(4):
-                        narrow_pass(g, r, n, t, b)
-                else:
-                    wide_pass(g, r, n, t)
-
-        def sweep_bank(r, n, b):
+        def sweep_bank(r, n, t):
             for g in range(KG):
-                if (r, n) in NARROW:
-                    for t in range(4):
-                        narrow_pass(g, r, n, t, b)
-                else:
-                    wide_pass(g, r, n, b)
+                stage1(g, r, n, (t,))
 
         h_rows = {}
         h_group = {}
 
-        def h_tile(r, n):
-            if (r, n) not in h_group:
-                h_group[r, n] = work.tile([P, 512, 4], BF16, name="h_group", tag="h_group", bufs=H_BUFS, align_bytes=256)
-            return h_group[r, n]
-
-        def empty_z(r, n, b, engine="v"):
-            if (r, n) in NARROW:
-                gains = gain[:, 4 * r : 4 * r + 4].rearrange("p (o t) -> p o t", o=1).to_broadcast([P, P, 4])
-                sums = z[r, n, b][:].rearrange("p (t c) -> p c t", t=4)
-                nc.vector.tensor_tensor(out=h_tile(r, n)[:, P * b : P * (b + 1), :], in0=sums, in1=gains, op=MULT)
-                return
+        def empty_z(r, n, t, engine):
             if (r, n) not in h_rows:
                 h_rows[r, n] = work.tile([P, 4, 512], BF16, name="h_rows", tag="h_rows", bufs=ROW_BUFS, align_bytes=256)
-            scale = gain[:, 4 * r + b : 4 * r + b + 1]
+            scale = gain[:, 4 * r + t : 4 * r + t + 1]
             if engine == "s":
-                nc.scalar.activation(out=h_rows[r, n][:, b, :], in_=z[r, n, b][:], func=COPY, scale=scale)
+                nc.scalar.activation(out=h_rows[r, n][:, t, :], in_=z[r, n, t][:], func=COPY, scale=scale)
             else:
-                nc.vector.tensor_scalar_mul(h_rows[r, n][:, b, :], z[r, n, b][:], scale)
+                nc.vector.tensor_scalar_mul(h_rows[r, n][:, t, :], z[r, n, t][:], scale)
 
         def group_h(r, n, engine="v", lo=0, hi=P):
+            if (r, n) not in h_group:
+                h_group[r, n] = work.tile([P, 512, 4], BF16, name="h_group", tag="h_group", bufs=H_BUFS, align_bytes=256)
             src = h_rows[r, n][:].rearrange("p t (c i) -> p c t i", i=4)
-            copy(engine, h_tile(r, n)[:].rearrange("p (c i) t -> p c t i", i=4)[:, lo:hi], src[:, lo:hi])
+            copy(engine, h_group[r, n][:].rearrange("p (c i) t -> p c t i", i=4)[:, lo:hi], src[:, lo:hi])
 
-        def quantize_h(r, n, lo=0, hi=512):
+        def quantize_h(r, n):
             nc.vector.quantize_mx(
-                out=h_codes[r, n][:, lo:hi].bitcast(E5),
-                scales=h_scales[r, n][:, lo:hi],
-                in_=h_group[r, n][:, lo:hi].rearrange("p n t -> p (n t)"),
+                out=h_codes[r, n][:].bitcast(E5),
+                scales=h_scales[r, n][:],
+                in_=h_group[r, n][:].rearrange("p n t -> p (n t)"),
             )
 
         acc = {}
@@ -287,28 +231,66 @@ def tile_factored_gain_correction_e3_kernel(tc, innov_words, innov_scales, obs_m
         def store(a, lo=0, hi=N):
             nc.sync.dma_start(out=out_rows[a // 2][:, a % 2 : a % 2 + 1, lo:hi], in_=results[a // 2][:, a % 2 : a % 2 + 1, lo:hi])
 
+        def finish(a, engines):
+            for n in range(2):
+                stage2(a, n)
+                empty_out(a, n, engines[n])
+            store(a)
+
+        nc.sync.dma_start(out=ratio_rows[:].bitcast(BF16), in_=mode_ratio.rearrange("(r c) -> r c", r=2))
+        nc.vector.memset(ratio_runs[:], 0.0)
+        for n in range(2):
+            nc.vector.memset(g_scales[n][:].rearrange("p g n -> p (g n)").bitcast(I32), 0)
+        make_identity(nc, ident[:])
+        for g in range(KG):
+            load_u(g)
+            load_w(g, g + 1, 0)
+            if g == 0:
+                load_scales(0)
+        load_scales(1)
+        load_w(0, 2, 1)
+        load_w(2, 4, 1)
+        for q in range(SP):
+            load_v(q)
+
+        order_words("v", ratio_runs[0:2], ratio_rows[:], L)
+        ratio_bank = psum.tile([P, 512], F32, name="ratio_bank", tag="bank7")
+        for u in range(2):
+            nc.tensor.transpose(ratio_bank[:, P * u : P * (u + 1)], ratio_runs[:, P * u : P * (u + 1)], ident[:])
+        ratio_turned = ratio_bank[:, : 2 * P].bitcast(BF16).rearrange("p (u k e) -> p k u e", u=2, e=2)[:, 0:2]
+        nc.vector.tensor_copy(out=ratio32[:].rearrange("p (r u e) -> p r u e", r=2, u=2), in_=ratio_turned)
+        nc.vector.tensor_tensor(out=square[:], in0=ratio32[:], in1=ratio32[:], op=MULT)
+        nc.vector.tensor_scalar_add(square[:], square[:], 1.0)
+        nc.vector.reciprocal(square[:], square[:])
+        nc.vector.tensor_tensor(out=gain[:], in0=ratio32[:], in1=square[:], op=MULT)
 
         for g in range(KG - 1):
-            group_u(g, 1, "s", U_CUT, P)
-            group_u(g, 0, "v", 0, P)
-            group_u(g, 1, "v", 0, U_CUT)
-            for r in range(2):
-                quantize_u(g, r)
-                if gain_steps:
-                    gain_steps.pop(0)()
-                passes(g, r, 0)
+            group_u(g, 0, 1, "s")
+            group_u(g, 1, 1, "s", U_CUT, L)
+            group_u(g, 0, 0, "v")
+            group_u(g, 1, 1, "v", 0, U_CUT)
+            quantize_u(g, 0, 0, 2)
+            group_u(g, 1, 0, "v")
+            quantize_u(g, 0, 2, 4)
+            stage1(g, 0, 0, range(4))
+            quantize_u(g, 1)
+            stage1(g, 1, 0, range(4))
         g = KG - 1
-        group_u(g, 0, "v", 0, 88)
-        group_u(g, 0, "s", 88, P)
-        group_u(g, 1, "s", 64, P)
-        group_u(g, 1, "v", 0, 24)
+        group_u(g, 0, 0, "s", FIRST_CUT, L)
+        group_u(g, 0, 1, "s", L // 2, L)
+        group_u(g, 1, 0, "s", L // 2, L)
+        group_u(g, 1, 1, "s", LAST_CUT, L)
+        group_u(g, 0, 0, "v", 0, FIRST_CUT)
+        group_u(g, 0, 1, "v", 0, L // 2)
         quantize_u(g, 0, 0, 2)
+        group_u(g, 1, 0, "v", 0, L // 2)
         quantize_u(g, 0, 2, 4)
-        group_u(g, 1, "v", 24, 64)
-        passes(g, 0, 0)
+        stage1(g, 0, 0, range(4))
+        group_u(g, 1, 1, "v", 0, LAST_CUT)
         quantize_u(g, 1, 0, 2)
-        quantize_u(g, 1, 2, 4)
-        passes(g, 1, 0)
+        quantize_u(g, 1, 2, 3)
+        quantize_u(g, 1, 3, 4)
+        stage1(g, 1, 0, range(4))
 
         for r in range(2):
             for t in range(4):
@@ -359,13 +341,6 @@ def tile_factored_gain_correction_e3_kernel(tc, innov_words, innov_scales, obs_m
             stage2(a, 1, (1,) if a < 2 else (0, 1))
             empty_out(a, 1, "s")
             store(a, 512, N)
-
-        def finish(a, engines):
-            for n in range(2):
-                stage2(a, n)
-                empty_out(a, n, engines[n])
-            store(a)
-
 
         turn_blocks(5)
         quantize_v(4)

@@ -21,7 +21,8 @@ KG = K // 512
 ST = S // P
 SP = ST // 2
 L = 32
-BY_VECTOR = (4, 5, 6)
+BY_VECTOR = (4, 5, 6, 7)
+TWO_QUEUES = (5, 6, 7)
 WIDE_BUFS = 7
 WORD_BUFS = 4
 GROUP_BUFS = 3
@@ -94,14 +95,22 @@ def tile_factored_gain_correction_e3_kernel(tc, innov_words, innov_scales, obs_m
             for g in range(lo, hi):
                 g_words[g, n] = tile[:, g - lo, :]
 
-        def load_v(q, second=None):
+        def load_quadrants(q, quadrants, queue):
+            quarters = state_modes[256 * q : 256 * (q + 1), :].rearrange("(j x) (r c w) -> c j (x r) w", x=8, r=2, c=4)
+            for c in quadrants:
+                rows = v_raw[q][32 * c : 32 * (c + 1)].rearrange("p i (y w) -> p (i y) w", w=128)
+                queue.dma_start(out=rows, in_=quarters[c])
+
+        def load_v(q):
             if q not in BY_VECTOR:
                 nc.sync.dma_start(out=v_raw[q][:], in_=v_rows[q])
-                return
-            quarters = state_modes[256 * q : 256 * (q + 1), :].rearrange("(j x) (r c w) -> c j (x r) w", x=8, r=2, c=4)
-            for c in range(4):
-                rows = v_raw[q][32 * c : 32 * (c + 1)].rearrange("p i (y w) -> p (i y) w", w=128)
-                nc.sync.dma_start(out=rows, in_=quarters[c])
+            else:
+                load_quadrants(q, (0, 1) if q in TWO_QUEUES else (2, 3, 0, 1), nc.sync)
+
+        def load_halves(q):
+            load_quadrants(q, (2, 3), nc.scalar)
+            if q + 1 < SP:
+                load_v(q + 1)
 
         v_words = {}
         v_group = {}
@@ -129,13 +138,14 @@ def tile_factored_gain_correction_e3_kernel(tc, innov_words, innov_scales, obs_m
             dst = group_tile(a // 2)[:, 1024 * (a % 2) : 1024 * (a % 2 + 1)].bitcast(F32).rearrange("p (g s u) -> p g s u", g=2, u=2)
             copy(engine, dst, v_bank[a][:].rearrange("p (g u s) -> p g s u", g=2, u=2))
 
-        def turn_blocks(q):
-            nc.vector.transpose(raw_words(q), v_words[q][:])
+        def turn_blocks(q, lo=0, hi=1024):
+            nc.vector.transpose(raw_words(q)[:, lo:hi], v_words[q][:, lo:hi])
 
-        def group_blocks(q, half, engine="v"):
+        def group_blocks(q):
             dst = group_tile(q)[:].bitcast(F32).rearrange("p (y j b u) -> p y j b u", y=4, b=4, u=2)
             src = raw_words(q).rearrange("p (b y u j) -> p y j b u", b=4, y=4, u=2)
-            copy(engine, dst[:, :, :, 2 * half : 2 * half + 2], src[:, :, :, 2 * half : 2 * half + 2])
+            for lo in (0, 2):
+                nc.vector.tensor_copy(out=dst[:, :, :, lo : lo + 2], in_=src[:, :, :, lo : lo + 2])
 
         def quantize_v(q):
             nc.vector.quantize_mx(out=v_codes[q][:].bitcast(E4), scales=v_scales[q][:], in_=v_group[q][:])
@@ -250,7 +260,7 @@ def tile_factored_gain_correction_e3_kernel(tc, innov_words, innov_scales, obs_m
         load_scales(1)
         load_w(0, 2, 1)
         load_w(2, 4, 1)
-        for q in range(SP):
+        for q in range(TWO_QUEUES[0] + 1):
             load_v(q)
 
         order_words("v", ratio_runs[0:2], ratio_rows[:], L)
@@ -304,64 +314,56 @@ def tile_factored_gain_correction_e3_kernel(tc, innov_words, innov_scales, obs_m
             empty_z(0, 1, t, "s")
             if t < 2:
                 group_h(1, 0, "s", 32 * t, 32 * (t + 1))
-        group_h(1, 0, "v", 64, P)
         order_v(2)
-        quantize_h(1, 0)
-        order_v(3)
-        for a in range(4):
+        group_h(1, 0, "v", 64, P)
+        for a in range(6):
             transpose_v(a)
-            empty_v(a, "vsvs"[a])
+            empty_v(a, "vsvsss"[a])
+            if a == 0:
+                quantize_h(1, 0)
+            if a == 1:
+                load_halves(5)
+        load_halves(6)
         group_h(0, 1)
         quantize_v(0)
         quantize_h(0, 1)
         quantize_v(1)
+        order_v(3)
+        quantize_v(2)
         for t in range(4):
             sweep_bank(1, 1, t)
             empty_z(1, 1, t, "s")
             if t == 0:
                 order_v(4, "s")
-        turn_blocks(4)
+                load_halves(7)
+        turn_blocks(4, 0, 512)
         group_h(1, 1)
-        for a in range(4):
+        turn_blocks(4, 512, 1024)
+        quantize_h(1, 1)
+        for a in range(6):
             stage2(a, 0)
             empty_out(a, 0, "s")
             store(a, 0, 512)
-        group_blocks(4, 0)
-        quantize_h(1, 1)
-        for a in range(4, 8):
-            transpose_v(a)
-            empty_v(a, "svss"[a % 4])
-        group_blocks(4, 1)
-        quantize_v(2)
         order_v(5)
-        quantize_v(3)
-        for a in range(2):
-            stage2(a, 1, (0,))
-        for a in range(4):
-            stage2(a, 1, (1,) if a < 2 else (0, 1))
-            empty_out(a, 1, "s")
-            store(a, 512, N)
-
-        turn_blocks(5)
-        quantize_v(4)
-        for q in (5, 6):
-            group_blocks(q, 0)
-            group_blocks(q, 1)
-            if q == 5:
-                order_v(6)
-            finish(2 * q - 6, "ss")
-            quantize_v(q)
-            if q == 5:
-                turn_blocks(6)
-                order_v(7)
-            finish(2 * q - 5, "ss")
-        finish(8, "ss")
-        finish(9, "sv")
-        finish(10, "sv")
-        for a in (14, 15):
+        for a in range(6, 8):
             transpose_v(a)
             empty_v(a, "vs"[a % 2])
-        finish(11, "sv")
+        group_blocks(4)
+        quantize_v(3)
+        turn_blocks(5)
+        quantize_v(4)
+        for a in range(6):
+            stage2(a, 1)
+            empty_out(a, 1, "s")
+            store(a, 512, N)
+        for q in (5, 6):
+            order_v(q + 1)
+            group_blocks(q)
+            turn_blocks(q + 1)
+            quantize_v(q)
+            finish(2 * q - 4, "ss")
+            finish(2 * q - 3, "ss")
+        group_blocks(7)
         quantize_v(7)
-        for a in range(12, ST):
-            finish(a, "sv")
+        for a in range(10, ST):
+            finish(a, "ss" if a < 12 else "sv")

@@ -31,6 +31,7 @@ ROW_BUFS = 3
 U_CUT = 8
 FIRST_CUT = 22
 LAST_CUT = 12
+HALF = 512
 
 
 def tile_factored_gain_correction_e3_kernel(tc, innov_words, innov_scales, obs_modes, mode_ratio, state_modes, out):
@@ -188,6 +189,22 @@ def tile_factored_gain_correction_e3_kernel(tc, innov_words, innov_scales, obs_m
             for g in range(KG):
                 stage1(g, r, n, (t,))
 
+        def sweep_pair(r, n, m, u):
+            z[r, n, m, u] = next_bank()
+            members = slice(256 * m, 256 * (m + 1))
+            for e in range(2):
+                cols = slice(128 * (2 * u + e), 128 * (2 * u + e + 1))
+                for g in range(KG):
+                    nc.tensor.matmul_mx(
+                        out=z[r, n, m, u][:, 256 * e : 256 * (e + 1)],
+                        lhsT=u_codes[g, r][:, cols].bitcast(E4),
+                        lhsT_scale=u_scales[g, r][:, cols],
+                        rhs=g_words[g, n][:, members].bitcast(E5),
+                        rhs_scale=g_scales[n][:, g, members],
+                        start=(g == 0),
+                        stop=(g == KG - 1),
+                    )
+
         h_rows = {}
         h_group = {}
 
@@ -200,17 +217,30 @@ def tile_factored_gain_correction_e3_kernel(tc, innov_words, innov_scales, obs_m
             else:
                 nc.vector.tensor_scalar_mul(h_rows[r, n][:, t, :], z[r, n, t][:], scale)
 
+        def empty_pair(r, n, m, u):
+            if (r, n) not in h_rows:
+                h_rows[r, n] = work.tile([P, 4, 512], BF16, name="h_rows", tag="h_rows", bufs=ROW_BUFS, align_bytes=256)
+            gains = gain[:, 4 * r + 2 * u : 4 * r + 2 * u + 2].rearrange("p (o e) -> p o e", o=1).to_broadcast([P, 256, 2])
+            pairs = h_rows[r, n][:, 2 * m + u, :].rearrange("p (c e) -> p c e", e=2)
+            nc.vector.tensor_tensor(out=pairs, in0=z[r, n, m, u][:].rearrange("p (e c) -> p c e", e=2), in1=gains, op=MULT)
+
+        def group_pairs(r, n, m, engine):
+            if (r, n) not in h_group:
+                h_group[r, n] = work.tile([P, 512, 4], BF16, name="h_group", tag="h_group", bufs=H_BUFS, align_bytes=256)
+            dst = h_group[r, n][:, 256 * m : 256 * (m + 1), :].bitcast(F32)
+            copy(engine, dst, h_rows[r, n][:, 2 * m : 2 * m + 2, :].bitcast(F32).rearrange("p u c -> p c u"))
+
         def group_h(r, n, engine="v", lo=0, hi=P):
             if (r, n) not in h_group:
                 h_group[r, n] = work.tile([P, 512, 4], BF16, name="h_group", tag="h_group", bufs=H_BUFS, align_bytes=256)
             src = h_rows[r, n][:].rearrange("p t (c i) -> p c t i", i=4)
             copy(engine, h_group[r, n][:].rearrange("p (c i) t -> p c t i", i=4)[:, lo:hi], src[:, lo:hi])
 
-        def quantize_h(r, n):
+        def quantize_h(r, n, lo=0, hi=512):
             nc.vector.quantize_mx(
-                out=h_codes[r, n][:].bitcast(E5),
-                scales=h_scales[r, n][:],
-                in_=h_group[r, n][:].rearrange("p n t -> p (n t)"),
+                out=h_codes[r, n][:, lo:hi].bitcast(E5),
+                scales=h_scales[r, n][:, lo:hi],
+                in_=h_group[r, n][:, lo:hi].rearrange("p n t -> p (n t)"),
             )
 
         acc = {}
@@ -258,8 +288,8 @@ def tile_factored_gain_correction_e3_kernel(tc, innov_words, innov_scales, obs_m
             if g == 0:
                 load_scales(0)
         load_scales(1)
-        load_w(0, 2, 1)
-        load_w(2, 4, 1)
+        for g in range(KG):
+            load_w(g, g + 1, 1)
         for q in range(TWO_QUEUES[0] + 1):
             load_v(q)
 
@@ -283,7 +313,8 @@ def tile_factored_gain_correction_e3_kernel(tc, innov_words, innov_scales, obs_m
             group_u(g, 1, 0, "v")
             quantize_u(g, 0, 2, 4)
             stage1(g, 0, 0, range(4))
-            quantize_u(g, 1)
+            quantize_u(g, 1, 0, 2)
+            quantize_u(g, 1, 2, 4)
             stage1(g, 1, 0, range(4))
         g = KG - 1
         group_u(g, 0, 0, "s", FIRST_CUT, L)
@@ -304,66 +335,73 @@ def tile_factored_gain_correction_e3_kernel(tc, innov_words, innov_scales, obs_m
 
         for r in range(2):
             for t in range(4):
-                empty_z(r, 0, t, "ssvs"[t] if r == 0 else "vsvs"[t])
+                empty_z(r, 0, t, "ssvv"[t] if r == 0 else "s")
+        for b in range(4):
+            sweep_pair(0, 1, b // 2, b % 2)
         group_h(0, 0)
-        order_v(0)
+        empty_pair(0, 1, 0, 0)
         quantize_h(0, 0)
-        order_v(1)
-        for t in range(4):
-            sweep_bank(0, 1, t)
-            empty_z(0, 1, t, "s")
-            if t < 2:
-                group_h(1, 0, "s", 32 * t, 32 * (t + 1))
+        empty_pair(0, 1, 0, 1)
+        order_v(0, "s")
+        order_v(1, "s")
         order_v(2)
-        group_h(1, 0, "v", 64, P)
+        empty_pair(0, 1, 1, 0)
+        group_h(1, 0, "s", 0, 32)
+        group_h(1, 0, "v", 32, P)
+        empty_pair(0, 1, 1, 1)
         for a in range(6):
             transpose_v(a)
-            empty_v(a, "vsvsss"[a])
-            if a == 0:
-                quantize_h(1, 0)
+            empty_v(a, "s")
             if a == 1:
                 load_halves(5)
         load_halves(6)
-        group_h(0, 1)
+        group_pairs(0, 1, 0, "v")
+        quantize_h(1, 0)
+        group_pairs(0, 1, 1, "v")
         quantize_v(0)
+        sweep_pair(1, 1, 0, 0)
+        empty_pair(1, 1, 0, 0)
         quantize_h(0, 1)
+        order_v(4, "s")
+        load_halves(7)
+        order_v(3, "s")
+        sweep_pair(1, 1, 0, 1)
+        empty_pair(1, 1, 0, 1)
         quantize_v(1)
-        order_v(3)
+        sweep_pair(1, 1, 1, 0)
+        empty_pair(1, 1, 1, 0)
+        group_pairs(1, 1, 0, "s")
         quantize_v(2)
-        for t in range(4):
-            sweep_bank(1, 1, t)
-            empty_z(1, 1, t, "s")
-            if t == 0:
-                order_v(4, "s")
-                load_halves(7)
-        turn_blocks(4, 0, 512)
-        group_h(1, 1)
-        turn_blocks(4, 512, 1024)
-        quantize_h(1, 1)
+        sweep_pair(1, 1, 1, 1)
+        empty_pair(1, 1, 1, 1)
+        quantize_h(1, 1, 0, 256)
+        group_pairs(1, 1, 1, "v")
+        turn_blocks(4, 0, HALF)
+        quantize_h(1, 1, 256, 512)
+        turn_blocks(4, HALF, 2 * HALF)
+        order_v(5)
         for a in range(6):
             stage2(a, 0)
             empty_out(a, 0, "s")
             store(a, 0, 512)
-        order_v(5)
         for a in range(6, 8):
             transpose_v(a)
             empty_v(a, "vs"[a % 2])
         group_blocks(4)
         quantize_v(3)
-        turn_blocks(5)
-        quantize_v(4)
         for a in range(6):
             stage2(a, 1)
             empty_out(a, 1, "s")
             store(a, 512, N)
-        for q in (5, 6):
-            order_v(q + 1)
-            group_blocks(q)
-            turn_blocks(q + 1)
+        for q in (4, 5, 6):
+            turn_blocks(q + 1, 0, HALF)
             quantize_v(q)
-            finish(2 * q - 4, "ss")
-            finish(2 * q - 3, "ss")
-        group_blocks(7)
+            turn_blocks(q + 1, HALF, 2 * HALF)
+            if q < 6:
+                order_v(q + 2)
+            group_blocks(q + 1)
+            finish(2 * q - 2, "ss")
+            finish(2 * q - 1, "ss")
         quantize_v(7)
-        for a in range(10, ST):
-            finish(a, "ss" if a < 12 else "sv")
+        for a in range(12, ST):
+            finish(a, "sv")

@@ -32,6 +32,8 @@ U_CUT = 8
 FIRST_CUT = 22
 LAST_CUT = 12
 HALF = 512
+LATE_PAIR = 3
+H_CUT = 64
 
 
 def tile_factored_gain_correction_e3_kernel(tc, innov_words, innov_scales, obs_modes, mode_ratio, state_modes, out):
@@ -110,8 +112,7 @@ def tile_factored_gain_correction_e3_kernel(tc, innov_words, innov_scales, obs_m
 
         def load_halves(q):
             load_quadrants(q, (2, 3), nc.scalar)
-            if q + 1 < SP:
-                load_v(q + 1)
+            load_v(q + 1 if q + 1 < SP else LATE_PAIR)
 
         v_words = {}
         v_group = {}
@@ -125,9 +126,10 @@ def tile_factored_gain_correction_e3_kernel(tc, innov_words, innov_scales, obs_m
         def raw_words(q):
             return v_raw[q][:].rearrange("p i r -> p (i r)").bitcast(F32)
 
-        def order_v(q, engine="v"):
-            v_words[q] = work.tile([P, 1024], F32, name="v_words", tag="v_words", bufs=WORD_BUFS, align_bytes=256)
-            order_words(engine, v_words[q][:], raw_words(q), L // 4 if q in BY_VECTOR else L)
+        def order_v(q, engine="v", lo=0, hi=1024):
+            if q not in v_words:
+                v_words[q] = work.tile([P, 1024], F32, name="v_words", tag="v_words", bufs=WORD_BUFS, align_bytes=256)
+            order_words(engine, v_words[q][:, lo:hi], raw_words(q)[:, lo:hi], L // 4 if q in BY_VECTOR else L)
 
         def transpose_v(a):
             v_bank[a] = next_bank()
@@ -142,14 +144,14 @@ def tile_factored_gain_correction_e3_kernel(tc, innov_words, innov_scales, obs_m
         def turn_blocks(q, lo=0, hi=1024):
             nc.vector.transpose(raw_words(q)[:, lo:hi], v_words[q][:, lo:hi])
 
-        def group_blocks(q):
+        def group_blocks(q, starts=(0, 2)):
             dst = group_tile(q)[:].bitcast(F32).rearrange("p (y j b u) -> p y j b u", y=4, b=4, u=2)
             src = raw_words(q).rearrange("p (b y u j) -> p y j b u", b=4, y=4, u=2)
-            for lo in (0, 2):
+            for lo in starts:
                 nc.vector.tensor_copy(out=dst[:, :, :, lo : lo + 2], in_=src[:, :, :, lo : lo + 2])
 
-        def quantize_v(q):
-            nc.vector.quantize_mx(out=v_codes[q][:].bitcast(E4), scales=v_scales[q][:], in_=v_group[q][:])
+        def quantize_v(q, lo=0, hi=512):
+            nc.vector.quantize_mx(out=v_codes[q][:, lo:hi].bitcast(E4), scales=v_scales[q][:, lo:hi], in_=v_group[q][:, 4 * lo : 4 * hi])
 
         u_group = {}
 
@@ -189,21 +191,23 @@ def tile_factored_gain_correction_e3_kernel(tc, innov_words, innov_scales, obs_m
             for g in range(KG):
                 stage1(g, r, n, (t,))
 
-        def sweep_pair(r, n, m, u):
-            z[r, n, m, u] = next_bank()
+        def sweep_pairs(r, n, m, halves):
             members = slice(256 * m, 256 * (m + 1))
+            for u in halves:
+                z[r, n, m, u] = next_bank()
             for e in range(2):
-                cols = slice(128 * (2 * u + e), 128 * (2 * u + e + 1))
                 for g in range(KG):
-                    nc.tensor.matmul_mx(
-                        out=z[r, n, m, u][:, 256 * e : 256 * (e + 1)],
-                        lhsT=u_codes[g, r][:, cols].bitcast(E4),
-                        lhsT_scale=u_scales[g, r][:, cols],
-                        rhs=g_words[g, n][:, members].bitcast(E5),
-                        rhs_scale=g_scales[n][:, g, members],
-                        start=(g == 0),
-                        stop=(g == KG - 1),
-                    )
+                    for u in halves:
+                        cols = slice(128 * (2 * u + e), 128 * (2 * u + e + 1))
+                        nc.tensor.matmul_mx(
+                            out=z[r, n, m, u][:, 256 * e : 256 * (e + 1)],
+                            lhsT=u_codes[g, r][:, cols].bitcast(E4),
+                            lhsT_scale=u_scales[g, r][:, cols],
+                            rhs=g_words[g, n][:, members].bitcast(E5),
+                            rhs_scale=g_scales[n][:, g, members],
+                            start=(g == 0),
+                            stop=(g == KG - 1),
+                        )
 
         h_rows = {}
         h_group = {}
@@ -291,7 +295,8 @@ def tile_factored_gain_correction_e3_kernel(tc, innov_words, innov_scales, obs_m
         for g in range(KG):
             load_w(g, g + 1, 1)
         for q in range(TWO_QUEUES[0] + 1):
-            load_v(q)
+            if q != LATE_PAIR:
+                load_v(q)
 
         order_words("v", ratio_runs[0:2], ratio_rows[:], L)
         ratio_bank = psum.tile([P, 512], F32, name="ratio_bank", tag="bank7")
@@ -335,73 +340,73 @@ def tile_factored_gain_correction_e3_kernel(tc, innov_words, innov_scales, obs_m
 
         for r in range(2):
             for t in range(4):
-                empty_z(r, 0, t, "ssvv"[t] if r == 0 else "s")
-        for b in range(4):
-            sweep_pair(0, 1, b // 2, b % 2)
+                empty_z(r, 0, t, "ssvv"[t] if r == 0 else "vsss"[t])
         group_h(0, 0)
-        empty_pair(0, 1, 0, 0)
+        order_v(0)
         quantize_h(0, 0)
-        empty_pair(0, 1, 0, 1)
-        order_v(0, "s")
-        order_v(1, "s")
+        order_v(1)
+        for t in range(4):
+            sweep_bank(0, 1, t)
+            empty_z(0, 1, t, "s")
+            if t == 0:
+                group_h(1, 0, "s", 0, H_CUT)
         order_v(2)
-        empty_pair(0, 1, 1, 0)
-        group_h(1, 0, "s", 0, 32)
-        group_h(1, 0, "v", 32, P)
-        empty_pair(0, 1, 1, 1)
+        group_h(1, 0, "v", H_CUT, P)
         for a in range(6):
             transpose_v(a)
             empty_v(a, "s")
             if a == 1:
                 load_halves(5)
-        load_halves(6)
-        group_pairs(0, 1, 0, "v")
+            if a == 3:
+                load_halves(6)
+        order_v(4, "s")
+        group_h(0, 1, "v", 0, P // 2)
         quantize_h(1, 0)
-        group_pairs(0, 1, 1, "v")
+        group_h(0, 1, "v", P // 2, P)
         quantize_v(0)
-        sweep_pair(1, 1, 0, 0)
+        sweep_pairs(1, 1, 0, (0,))
         empty_pair(1, 1, 0, 0)
         quantize_h(0, 1)
-        order_v(4, "s")
         load_halves(7)
-        order_v(3, "s")
-        sweep_pair(1, 1, 0, 1)
+        sweep_pairs(1, 1, 0, (1,))
         empty_pair(1, 1, 0, 1)
         quantize_v(1)
-        sweep_pair(1, 1, 1, 0)
+        sweep_pairs(1, 1, 1, (0,))
         empty_pair(1, 1, 1, 0)
         group_pairs(1, 1, 0, "s")
+        order_v(5, "s")
         quantize_v(2)
-        sweep_pair(1, 1, 1, 1)
+        sweep_pairs(1, 1, 1, (1,))
         empty_pair(1, 1, 1, 1)
-        quantize_h(1, 1, 0, 256)
-        group_pairs(1, 1, 1, "v")
         turn_blocks(4, 0, HALF)
+        group_pairs(1, 1, 1, "v")
+        quantize_h(1, 1, 0, 256)
         quantize_h(1, 1, 256, 512)
         turn_blocks(4, HALF, 2 * HALF)
-        order_v(5)
-        for a in range(6):
-            stage2(a, 0)
-            empty_out(a, 0, "s")
-            store(a, 0, 512)
-        for a in range(6, 8):
-            transpose_v(a)
-            empty_v(a, "vs"[a % 2])
-        group_blocks(4)
-        quantize_v(3)
-        for a in range(6):
-            stage2(a, 1)
-            empty_out(a, 1, "s")
-            store(a, 512, N)
-        for q in (4, 5, 6):
-            turn_blocks(q + 1, 0, HALF)
+        for n in range(2):
+            for a in range(6):
+                stage2(a, n)
+                empty_out(a, n, "s")
+                store(a, 512 * n, 512 * (n + 1))
+        for q, filler in ((4, 6), (5, 3), (6, 7)):
+            order_v(filler, "v", 0, HALF)
+            group_blocks(q)
+            order_v(filler, "v", HALF, 2 * HALF)
             quantize_v(q)
-            turn_blocks(q + 1, HALF, 2 * HALF)
             if q < 6:
-                order_v(q + 2)
-            group_blocks(q + 1)
-            finish(2 * q - 2, "ss")
-            finish(2 * q - 1, "ss")
+                turn_blocks(q + 1)
+            else:
+                turn_blocks(7, 0, HALF)
+                for a in range(6, 8):
+                    transpose_v(a)
+                    empty_v(a, "vs"[a % 2])
+                turn_blocks(7, HALF, 2 * HALF)
+                quantize_v(3, 0, 256)
+                group_blocks(7, (0,))
+                quantize_v(3, 256, 512)
+                group_blocks(7, (2,))
+            finish(2 * q, "ss")
+            finish(2 * q + 1, "ss")
         quantize_v(7)
-        for a in range(12, ST):
+        for a in (6, 7, 14, 15):
             finish(a, "sv")

@@ -22,7 +22,6 @@ ST = S // P
 SP = ST // 2
 L = 32
 BY_VECTOR = (4, 5, 6, 7)
-TWO_QUEUES = (5, 6, 7)
 WIDE_BUFS = 7
 WORD_BUFS = 4
 GROUP_BUFS = 3
@@ -33,7 +32,7 @@ FIRST_CUT = 22
 LAST_CUT = 12
 HALF = 512
 LATE_PAIR = 3
-H_CUT = 64
+H_CUT = 32
 
 
 def tile_factored_gain_correction_e3_kernel(tc, innov_words, innov_scales, obs_modes, mode_ratio, state_modes, out):
@@ -108,11 +107,15 @@ def tile_factored_gain_correction_e3_kernel(tc, innov_words, innov_scales, obs_m
             if q not in BY_VECTOR:
                 nc.sync.dma_start(out=v_raw[q][:], in_=v_rows[q])
             else:
-                load_quadrants(q, (0, 1) if q in TWO_QUEUES else (2, 3, 0, 1), nc.sync)
+                load_quadrants(q, (0, 1), nc.sync)
 
-        def load_halves(q):
-            load_quadrants(q, (2, 3), nc.scalar)
-            load_v(q + 1 if q + 1 < SP else LATE_PAIR)
+        upper = [(q, c) for q in BY_VECTOR for c in (2, 3)]
+
+        def load_upper():
+            q, c = upper.pop(0)
+            load_quadrants(q, (c,), nc.scalar)
+            if c == 3:
+                load_v(q + 1 if q + 1 < SP else LATE_PAIR)
 
         v_words = {}
         v_group = {}
@@ -272,14 +275,26 @@ def tile_factored_gain_correction_e3_kernel(tc, innov_words, innov_scales, obs_m
                 results[a // 2] = work.tile([P, 2, N], F32, name="result", tag="wide", bufs=WIDE_BUFS, align_bytes=256)
             copy(engine, results[a // 2][:, a % 2, 512 * n : 512 * (n + 1)], acc[a, n][:])
 
-        def store(a, lo=0, hi=N):
-            nc.sync.dma_start(out=out_rows[a // 2][:, a % 2 : a % 2 + 1, lo:hi], in_=results[a // 2][:, a % 2 : a % 2 + 1, lo:hi])
+        def store(a, lo=0, hi=N, tiles=1):
+            rows = slice(a % 2, a % 2 + tiles)
+            nc.sync.dma_start(out=out_rows[a // 2][:, rows, lo:hi], in_=results[a // 2][:, rows, lo:hi])
 
-        def finish(a, engines):
+        def finish(a, engines, stored=True):
             for n in range(2):
                 stage2(a, n)
                 empty_out(a, n, engines[n])
-            store(a)
+            if stored:
+                store(a)
+
+        def half_tile(a, n, mode_halves=(0, 1)):
+            stage2(a, n, mode_halves)
+            empty_out(a, n, "s")
+            store(a, 512 * n, 512 * (n + 1))
+
+        def finish_pair(q, engines):
+            for a in (2 * q, 2 * q + 1):
+                finish(a, engines, False)
+            store(2 * q, 0, N, 2)
 
         nc.sync.dma_start(out=ratio_rows[:].bitcast(BF16), in_=mode_ratio.rearrange("(r c) -> r c", r=2))
         nc.vector.memset(ratio_runs[:], 0.0)
@@ -294,9 +309,8 @@ def tile_factored_gain_correction_e3_kernel(tc, innov_words, innov_scales, obs_m
         load_scales(1)
         for g in range(KG):
             load_w(g, g + 1, 1)
-        for q in range(TWO_QUEUES[0] + 1):
-            if q != LATE_PAIR:
-                load_v(q)
+        for q in (0, 1, 2, 4):
+            load_v(q)
 
         order_words("v", ratio_runs[0:2], ratio_rows[:], L)
         ratio_bank = psum.tile([P, 512], F32, name="ratio_bank", tag="bank7")
@@ -348,34 +362,30 @@ def tile_factored_gain_correction_e3_kernel(tc, innov_words, innov_scales, obs_m
         for t in range(4):
             sweep_bank(0, 1, t)
             empty_z(0, 1, t, "s")
+            load_upper()
             if t == 0:
                 group_h(1, 0, "s", 0, H_CUT)
-        order_v(2)
         group_h(1, 0, "v", H_CUT, P)
-        for a in range(6):
+        order_v(2)
+        for a in range(4):
             transpose_v(a)
             empty_v(a, "s")
-            if a == 1:
-                load_halves(5)
-            if a == 3:
-                load_halves(6)
+            load_upper()
         order_v(4, "s")
+        order_v(5, "s")
         group_h(0, 1, "v", 0, P // 2)
         quantize_h(1, 0)
         group_h(0, 1, "v", P // 2, P)
-        quantize_v(0)
         sweep_pairs(1, 1, 0, (0,))
         empty_pair(1, 1, 0, 0)
-        quantize_h(0, 1)
-        load_halves(7)
+        quantize_v(0)
         sweep_pairs(1, 1, 0, (1,))
         empty_pair(1, 1, 0, 1)
         quantize_v(1)
+        group_pairs(1, 1, 0, "s")
         sweep_pairs(1, 1, 1, (0,))
         empty_pair(1, 1, 1, 0)
-        group_pairs(1, 1, 0, "s")
-        order_v(5, "s")
-        quantize_v(2)
+        quantize_h(0, 1)
         sweep_pairs(1, 1, 1, (1,))
         empty_pair(1, 1, 1, 1)
         turn_blocks(4, 0, HALF)
@@ -383,14 +393,23 @@ def tile_factored_gain_correction_e3_kernel(tc, innov_words, innov_scales, obs_m
         quantize_h(1, 1, 0, 256)
         quantize_h(1, 1, 256, 512)
         turn_blocks(4, HALF, 2 * HALF)
-        for n in range(2):
-            for a in range(6):
-                stage2(a, n)
-                empty_out(a, n, "s")
-                store(a, 512 * n, 512 * (n + 1))
+        for a in range(4):
+            half_tile(a, 0)
+        for a in (4, 5):
+            transpose_v(a)
+            empty_v(a, "vs"[a % 2])
+        group_blocks(4, (0,))
+        quantize_v(2, 0, 256)
+        group_blocks(4, (2,))
+        quantize_v(2, 256, 512)
+        for a in range(4):
+            half_tile(a, 1)
+        finish(4, "ss")
+        finish(5, "ss")
         for q, filler in ((4, 6), (5, 3), (6, 7)):
             order_v(filler, "v", 0, HALF)
-            group_blocks(q)
+            if q > 4:
+                group_blocks(q)
             order_v(filler, "v", HALF, 2 * HALF)
             quantize_v(q)
             if q < 6:

@@ -22,6 +22,7 @@ ST = S // P
 SP = ST // 2
 L = 32
 BY_VECTOR = (4, 5, 6, 7)
+TWO_QUEUES = (5, 6, 7)
 WIDE_BUFS = 7
 WORD_BUFS = 4
 GROUP_BUFS = 3
@@ -107,15 +108,11 @@ def tile_factored_gain_correction_e3_kernel(tc, innov_words, innov_scales, obs_m
             if q not in BY_VECTOR:
                 nc.sync.dma_start(out=v_raw[q][:], in_=v_rows[q])
             else:
-                load_quadrants(q, (0, 1), nc.sync)
+                load_quadrants(q, (0, 1) if q in TWO_QUEUES else (2, 3, 0, 1), nc.sync)
 
-        upper = [(q, c) for q in BY_VECTOR for c in (2, 3)]
-
-        def load_upper():
-            q, c = upper.pop(0)
-            load_quadrants(q, (c,), nc.scalar)
-            if c == 3:
-                load_v(q + 1 if q + 1 < SP else LATE_PAIR)
+        def load_halves(q):
+            load_quadrants(q, (2, 3), nc.scalar)
+            load_v(q + 1 if q + 1 < SP else LATE_PAIR)
 
         v_words = {}
         v_group = {}
@@ -309,8 +306,9 @@ def tile_factored_gain_correction_e3_kernel(tc, innov_words, innov_scales, obs_m
         load_scales(1)
         for g in range(KG):
             load_w(g, g + 1, 1)
-        for q in (0, 1, 2, 4):
-            load_v(q)
+        for q in range(TWO_QUEUES[0] + 1):
+            if q != LATE_PAIR:
+                load_v(q)
 
         order_words("v", ratio_runs[0:2], ratio_rows[:], L)
         ratio_bank = psum.tile([P, 512], F32, name="ratio_bank", tag="bank7")
@@ -362,7 +360,6 @@ def tile_factored_gain_correction_e3_kernel(tc, innov_words, innov_scales, obs_m
         for t in range(4):
             sweep_bank(0, 1, t)
             empty_z(0, 1, t, "s")
-            load_upper()
             if t == 0:
                 group_h(1, 0, "s", 0, H_CUT)
         group_h(1, 0, "v", H_CUT, P)
@@ -370,9 +367,9 @@ def tile_factored_gain_correction_e3_kernel(tc, innov_words, innov_scales, obs_m
         for a in range(4):
             transpose_v(a)
             empty_v(a, "s")
-            load_upper()
+            if a % 2 == 1:
+                load_halves(5 + a // 2)
         order_v(4, "s")
-        order_v(5, "s")
         group_h(0, 1, "v", 0, P // 2)
         quantize_h(1, 0)
         group_h(0, 1, "v", P // 2, P)
@@ -383,6 +380,8 @@ def tile_factored_gain_correction_e3_kernel(tc, innov_words, innov_scales, obs_m
         empty_pair(1, 1, 0, 1)
         quantize_v(1)
         group_pairs(1, 1, 0, "s")
+        load_halves(7)
+        order_v(5, "s")
         sweep_pairs(1, 1, 1, (0,))
         empty_pair(1, 1, 1, 0)
         quantize_h(0, 1)

@@ -33,7 +33,7 @@ FIRST_CUT = 22
 LAST_CUT = 12
 HALF = 512
 LATE_PAIR = 3
-H_CUT = 32
+H_CUT = 64
 
 
 def tile_factored_gain_correction_e3_kernel(tc, innov_words, innov_scales, obs_modes, mode_ratio, state_modes, out):
@@ -272,26 +272,30 @@ def tile_factored_gain_correction_e3_kernel(tc, innov_words, innov_scales, obs_m
                 results[a // 2] = work.tile([P, 2, N], F32, name="result", tag="wide", bufs=WIDE_BUFS, align_bytes=256)
             copy(engine, results[a // 2][:, a % 2, 512 * n : 512 * (n + 1)], acc[a, n][:])
 
-        def store(a, lo=0, hi=N, tiles=1):
-            rows = slice(a % 2, a % 2 + tiles)
-            nc.sync.dma_start(out=out_rows[a // 2][:, rows, lo:hi], in_=results[a // 2][:, rows, lo:hi])
+        def store(a, lo=0, hi=N, queue=nc.sync):
+            rows = slice(a % 2, a % 2 + 1)
+            queue.dma_start(out=out_rows[a // 2][:, rows, lo:hi], in_=results[a // 2][:, rows, lo:hi])
 
-        def finish(a, engines, stored=True):
+        held = []
+
+        def release():
+            if held:
+                store(held.pop(), 0, N, nc.scalar)
+
+        def finish(a, engines, second_queue=False):
             for n in range(2):
                 stage2(a, n)
                 empty_out(a, n, engines[n])
-            if stored:
+                release()
+            if second_queue:
+                held.append(a)
+            else:
                 store(a)
 
         def half_tile(a, n, mode_halves=(0, 1)):
             stage2(a, n, mode_halves)
             empty_out(a, n, "s")
             store(a, 512 * n, 512 * (n + 1))
-
-        def finish_pair(q, engines):
-            for a in (2 * q, 2 * q + 1):
-                finish(a, engines, False)
-            store(2 * q, 0, N, 2)
 
         nc.sync.dma_start(out=ratio_rows[:].bitcast(BF16), in_=mode_ratio.rearrange("(r c) -> r c", r=2))
         nc.vector.memset(ratio_runs[:], 0.0)
@@ -364,26 +368,25 @@ def tile_factored_gain_correction_e3_kernel(tc, innov_words, innov_scales, obs_m
                 group_h(1, 0, "s", 0, H_CUT)
         group_h(1, 0, "v", H_CUT, P)
         order_v(2)
+        quantize_h(1, 0)
         for a in range(4):
             transpose_v(a)
             empty_v(a, "s")
             if a % 2 == 1:
                 load_halves(5 + a // 2)
         order_v(4, "s")
-        group_h(0, 1, "v", 0, P // 2)
-        quantize_h(1, 0)
-        group_h(0, 1, "v", P // 2, P)
+        group_h(0, 1)
         sweep_pairs(1, 1, 0, (0,))
         empty_pair(1, 1, 0, 0)
         quantize_v(0)
         sweep_pairs(1, 1, 0, (1,))
         empty_pair(1, 1, 0, 1)
         quantize_v(1)
-        group_pairs(1, 1, 0, "s")
         load_halves(7)
         order_v(5, "s")
         sweep_pairs(1, 1, 1, (0,))
         empty_pair(1, 1, 1, 0)
+        group_pairs(1, 1, 0, "v")
         quantize_h(0, 1)
         sweep_pairs(1, 1, 1, (1,))
         empty_pair(1, 1, 1, 1)
@@ -417,14 +420,16 @@ def tile_factored_gain_correction_e3_kernel(tc, innov_words, innov_scales, obs_m
                 turn_blocks(7, 0, HALF)
                 for a in range(6, 8):
                     transpose_v(a)
-                    empty_v(a, "vs"[a % 2])
+                    empty_v(a, "sv"[a % 2])
+                    release()
                 turn_blocks(7, HALF, 2 * HALF)
                 quantize_v(3, 0, 256)
                 group_blocks(7, (0,))
                 quantize_v(3, 256, 512)
                 group_blocks(7, (2,))
             finish(2 * q, "ss")
-            finish(2 * q + 1, "ss")
+            finish(2 * q + 1, "ss", True)
         quantize_v(7)
         for a in (6, 7, 14, 15):
-            finish(a, "sv")
+            finish(a, "sv" if a == 6 else "vs", a % 2 == 1)
+            release()

@@ -22,7 +22,7 @@ ST = S // P
 SP = ST // 2
 L = 32
 BY_VECTOR = (4, 5, 6, 7)
-TWO_QUEUES = (5, 6, 7)
+TWO_QUEUES = (6, 7)
 WIDE_BUFS = 7
 WORD_BUFS = 4
 GROUP_BUFS = 3
@@ -372,8 +372,7 @@ def tile_factored_gain_correction_e3_kernel(tc, innov_words, innov_scales, obs_m
         for a in range(4):
             transpose_v(a)
             empty_v(a, "s")
-            if a % 2 == 1:
-                load_halves(5 + a // 2)
+        load_halves(6)
         order_v(4, "s")
         group_h(0, 1)
         sweep_pairs(1, 1, 0, (0,))
@@ -384,9 +383,9 @@ def tile_factored_gain_correction_e3_kernel(tc, innov_words, innov_scales, obs_m
         quantize_v(1)
         load_halves(7)
         order_v(5, "s")
+        group_pairs(1, 1, 0, "s")
         sweep_pairs(1, 1, 1, (0,))
         empty_pair(1, 1, 1, 0)
-        group_pairs(1, 1, 0, "v")
         quantize_h(0, 1)
         sweep_pairs(1, 1, 1, (1,))
         empty_pair(1, 1, 1, 1)

@@ -22,7 +22,6 @@ ST = S // P
 SP = ST // 2
 L = 32
 BY_VECTOR = (4, 5, 6, 7)
-TWO_QUEUES = (6, 7)
 WIDE_BUFS = 7
 WORD_BUFS = 4
 GROUP_BUFS = 3
@@ -98,21 +97,14 @@ def tile_factored_gain_correction_e3_kernel(tc, innov_words, innov_scales, obs_m
             for g in range(lo, hi):
                 g_words[g, n] = tile[:, g - lo, :]
 
-        def load_quadrants(q, quadrants, queue):
-            quarters = state_modes[256 * q : 256 * (q + 1), :].rearrange("(j x) (r c w) -> c j (x r) w", x=8, r=2, c=4)
-            for c in quadrants:
-                rows = v_raw[q][32 * c : 32 * (c + 1)].rearrange("p i (y w) -> p (i y) w", w=128)
-                queue.dma_start(out=rows, in_=quarters[c])
-
         def load_v(q):
             if q not in BY_VECTOR:
                 nc.sync.dma_start(out=v_raw[q][:], in_=v_rows[q])
-            else:
-                load_quadrants(q, (0, 1) if q in TWO_QUEUES else (2, 3, 0, 1), nc.sync)
-
-        def load_halves(q):
-            load_quadrants(q, (2, 3), nc.scalar)
-            load_v(q + 1 if q + 1 < SP else LATE_PAIR)
+                return
+            quarters = state_modes[256 * q : 256 * (q + 1), :].rearrange("(j x) (r c w) -> c j (x r) w", x=8, r=2, c=4)
+            for c in (0, 2, 1, 3):
+                rows = v_raw[q][32 * c : 32 * (c + 1)].rearrange("p i (y w) -> p (i y) w", w=128)
+                nc.sync.dma_start(out=rows, in_=quarters[c])
 
         v_words = {}
         v_group = {}
@@ -310,9 +302,10 @@ def tile_factored_gain_correction_e3_kernel(tc, innov_words, innov_scales, obs_m
         load_scales(1)
         for g in range(KG):
             load_w(g, g + 1, 1)
-        for q in range(TWO_QUEUES[0] + 1):
+        for q in range(SP):
             if q != LATE_PAIR:
                 load_v(q)
+        load_v(LATE_PAIR)
 
         order_words("v", ratio_runs[0:2], ratio_rows[:], L)
         ratio_bank = psum.tile([P, 512], F32, name="ratio_bank", tag="bank7")
@@ -372,7 +365,6 @@ def tile_factored_gain_correction_e3_kernel(tc, innov_words, innov_scales, obs_m
         for a in range(4):
             transpose_v(a)
             empty_v(a, "s")
-        load_halves(6)
         order_v(4, "s")
         group_h(0, 1)
         sweep_pairs(1, 1, 0, (0,))
@@ -381,7 +373,6 @@ def tile_factored_gain_correction_e3_kernel(tc, innov_words, innov_scales, obs_m
         sweep_pairs(1, 1, 0, (1,))
         empty_pair(1, 1, 0, 1)
         quantize_v(1)
-        load_halves(7)
         order_v(5, "s")
         group_pairs(1, 1, 0, "s")
         sweep_pairs(1, 1, 1, (0,))

@@ -20,16 +20,16 @@ P = 128
 KG = K // 512
 ST = S // P
 SP = ST // 2
-L = 32
+L = 16
 BY_VECTOR = (4, 5, 6, 7)
 WIDE_BUFS = 7
 WORD_BUFS = 4
 GROUP_BUFS = 3
 H_BUFS = 2
 ROW_BUFS = 3
-U_CUT = 8
-FIRST_CUT = 22
-LAST_CUT = 12
+U_CUT = 4
+FIRST_CUT = 11
+LAST_CUT = 6
 HALF = 512
 LATE_PAIR = 3
 H_CUT = 64
@@ -54,8 +54,8 @@ def tile_factored_gain_correction_e3_kernel(tc, innov_words, innov_scales, obs_m
             return psum.tile([P, 512], F32, name="bank%d" % b, tag="bank%d" % b)
 
         ident = keep.tile([P, P], F32, name="ident", align_bytes=256)
-        ratio_rows = keep.tile([2, 256], F32, name="ratio_rows", align_bytes=256)
-        ratio_runs = keep.tile([P, 256], F32, name="ratio_runs", align_bytes=256)
+        ratio_rows = work.tile([1, 512], F32, name="ratio_rows", tag="v_words", bufs=WORD_BUFS, align_bytes=256)
+        ratio_runs = work.tile([P, 512], F32, name="ratio_runs", tag="v_words", bufs=WORD_BUFS, align_bytes=256)
         ratio32 = keep.tile([P, 8], F32, name="ratio32")
         square = keep.tile([P, 8], F32, name="square")
         gain = keep.tile([P, 8], F32, name="gain")
@@ -77,7 +77,7 @@ def tile_factored_gain_correction_e3_kernel(tc, innov_words, innov_scales, obs_m
                 nc.vector.tensor_copy(out=out, in_=in_)
 
         def order_words(engine, dst, src, runs):
-            copy(engine, dst.rearrange("p (x u l w) -> p x u l w", u=2, l=runs, w=4), src.rearrange("p (x l u w) -> p x u l w", u=2, l=runs, w=4))
+            copy(engine, dst.rearrange("p (x t q w) -> p x t q w", t=4, q=runs, w=8), src.rearrange("p (x q t w) -> p x t q w", t=4, q=runs, w=8))
 
         def load_scales(n):
             scale_rows = innov_scales[:, :, 512 * n : 512 * (n + 1)].rearrange("g (q j) n -> j q g n", j=4)
@@ -87,8 +87,7 @@ def tile_factored_gain_correction_e3_kernel(tc, innov_words, innov_scales, obs_m
         def load_u(g):
             raw = work.tile([P, 4, R], BF16, name="u_raw", tag="wide", bufs=WIDE_BUFS, align_bytes=256)
             nc.sync.dma_start(out=raw[:], in_=obs_modes[512 * g : 512 * (g + 1), :].rearrange("(p j) w -> p j w", j=4))
-            for r in range(2):
-                u_raw[g, r] = raw[:, :, 512 * r : 512 * (r + 1)]
+            u_raw[g] = raw
 
         def load_w(lo, hi, n):
             tile = keep.tile([P, hi - lo, 512], U32, name="g_words%d_%d" % (lo, n), align_bytes=256)
@@ -101,9 +100,9 @@ def tile_factored_gain_correction_e3_kernel(tc, innov_words, innov_scales, obs_m
             if q not in BY_VECTOR:
                 nc.sync.dma_start(out=v_raw[q][:], in_=v_rows[q])
                 return
-            quarters = state_modes[256 * q : 256 * (q + 1), :].rearrange("(j x) (r c w) -> c j (x r) w", x=8, r=2, c=4)
+            quarters = state_modes[256 * q : 256 * (q + 1), :].rearrange("(j x) (c w) -> c j x w", x=8, c=4)
             for c in (0, 2, 1, 3):
-                rows = v_raw[q][32 * c : 32 * (c + 1)].rearrange("p i (y w) -> p (i y) w", w=128)
+                rows = v_raw[q][32 * c : 32 * (c + 1)].rearrange("p i (y w) -> p (i y) w", w=256)
                 nc.sync.dma_start(out=rows, in_=quarters[c])
 
         v_words = {}
@@ -150,9 +149,9 @@ def tile_factored_gain_correction_e3_kernel(tc, innov_words, innov_scales, obs_m
         def group_u(g, r, u, engine, lo=0, hi=L):
             if (g, r) not in u_group:
                 u_group[g, r] = work.tile([P, 4, P, 4], BF16, name="u_group", tag="u_group", bufs=4, align_bytes=256)
-            src = u_raw[g, r].rearrange("p k (l u h j e) -> p u l h k j e", u=2, h=2, j=2, e=2)
-            dst = u_group[g, r][:].rearrange("p (u e) (l h j) k -> p u l h k j e", u=2, h=2, j=2)
-            copy(engine, dst[:, u, lo:hi], src[:, u, lo:hi])
+            src = u_raw[g][:].rearrange("p k (q r u h j e) -> p r u q h k j e", r=2, u=2, h=4, j=2, e=2)
+            dst = u_group[g, r][:].rearrange("p (u e) (q h j) k -> p u q h k j e", u=2, h=4, j=2)
+            copy(engine, dst[:, u, lo:hi], src[:, r, u, lo:hi])
 
         def quantize_u(g, r, lo=0, hi=4):
             cols = slice(128 * lo, 128 * hi)
@@ -289,7 +288,7 @@ def tile_factored_gain_correction_e3_kernel(tc, innov_words, innov_scales, obs_m
             empty_out(a, n, "s")
             store(a, 512 * n, 512 * (n + 1))
 
-        nc.sync.dma_start(out=ratio_rows[:].bitcast(BF16), in_=mode_ratio.rearrange("(r c) -> r c", r=2))
+        nc.sync.dma_start(out=ratio_rows[:].bitcast(BF16), in_=mode_ratio.rearrange("(o c) -> o c", o=1))
         nc.vector.memset(ratio_runs[:], 0.0)
         for n in range(2):
             nc.vector.memset(g_scales[n][:].rearrange("p g n -> p (g n)").bitcast(I32), 0)
@@ -307,12 +306,12 @@ def tile_factored_gain_correction_e3_kernel(tc, innov_words, innov_scales, obs_m
                 load_v(q)
         load_v(LATE_PAIR)
 
-        order_words("v", ratio_runs[0:2], ratio_rows[:], L)
+        order_words("v", ratio_runs[0:1], ratio_rows[:], L)
         ratio_bank = psum.tile([P, 512], F32, name="ratio_bank", tag="bank7")
-        for u in range(2):
-            nc.tensor.transpose(ratio_bank[:, P * u : P * (u + 1)], ratio_runs[:, P * u : P * (u + 1)], ident[:])
-        ratio_turned = ratio_bank[:, : 2 * P].bitcast(BF16).rearrange("p (u k e) -> p k u e", u=2, e=2)[:, 0:2]
-        nc.vector.tensor_copy(out=ratio32[:].rearrange("p (r u e) -> p r u e", r=2, u=2), in_=ratio_turned)
+        for t in range(4):
+            nc.tensor.transpose(ratio_bank[:, P * t : P * (t + 1)], ratio_runs[:, P * t : P * (t + 1)], ident[:])
+        ratio_turned = ratio_bank[:].bitcast(BF16).rearrange("p (t k e) -> p k t e", t=4, e=2)[:, 0]
+        nc.vector.tensor_copy(out=ratio32[:].rearrange("p (t e) -> p t e", t=4), in_=ratio_turned)
         nc.vector.tensor_tensor(out=square[:], in0=ratio32[:], in1=ratio32[:], op=MULT)
         nc.vector.tensor_scalar_add(square[:], square[:], 1.0)
         nc.vector.reciprocal(square[:], square[:])

@@ -14,25 +14,20 @@ U8 = mybir.dt.uint8
 E4 = mybir.dt.float8_e4m3fn_x4
 E5 = mybir.dt.float8_e5m2_x4
 COPY = mybir.ActivationFunctionType.Copy
-MULT = mybir.AluOpType.mult
+ADD = mybir.AluOpType.add
 
 P = 128
 KG = K // 512
-ST = S // P
-SP = ST // 2
-L = 16
-BY_VECTOR = (4, 5, 6, 7)
+PAIRS = S // (2 * P)
+OCTETS = P // 8
+BY_VECTOR = (3, 4, 5, 6)
+U_SHARES = (10, 8, 10, 8)
 WIDE_BUFS = 7
 WORD_BUFS = 4
 GROUP_BUFS = 3
 H_BUFS = 2
 ROW_BUFS = 3
-U_CUT = 4
-FIRST_CUT = 11
-LAST_CUT = 6
-HALF = 512
-LATE_PAIR = 3
-H_CUT = 64
+U_BUFS = 4
 
 
 def tile_factored_gain_correction_e3_kernel(tc, innov_words, innov_scales, obs_modes, mode_ratio, state_modes, out):
@@ -53,20 +48,20 @@ def tile_factored_gain_correction_e3_kernel(tc, innov_words, innov_scales, obs_m
             turn[0] = (b + 1) % 8
             return psum.tile([P, 512], F32, name="bank%d" % b, tag="bank%d" % b)
 
+        def word_tile(rows, name):
+            return work.tile([rows, 1024], F32, name=name, tag="words", bufs=WORD_BUFS, align_bytes=256)
+
         ident = keep.tile([P, P], F32, name="ident", align_bytes=256)
-        ratio_rows = work.tile([1, 512], F32, name="ratio_rows", tag="v_words", bufs=WORD_BUFS, align_bytes=256)
-        ratio_runs = work.tile([P, 512], F32, name="ratio_runs", tag="v_words", bufs=WORD_BUFS, align_bytes=256)
-        ratio32 = keep.tile([P, 8], F32, name="ratio32")
-        square = keep.tile([P, 8], F32, name="square")
-        gain = keep.tile([P, 8], F32, name="gain")
-        g_words = {}
+        inverse = keep.tile([P, 4, 2], F32, name="inverse")
+        total = keep.tile([P, 4, 2], F32, name="total")
+        gain = keep.tile([P, 4, 2], F32, name="gain")
+        g_words = {(g, n): keep.tile([P, 512], U32, name="g_words%d_%d" % (g, n), align_bytes=256) for g in range(KG) for n in range(2)}
         g_scales = [keep.tile([P, KG, 512], U8, name="g_scales%d" % n, align_bytes=256) for n in range(2)]
-        u_raw = {}
         u_codes = {(g, r): keep.tile([P, 512], U32, name="u_codes%d_%d" % (g, r), align_bytes=256) for g in range(KG) for r in range(2)}
         u_scales = {k: keep.tile([P, 512], U8, name="u_scales%d_%d" % k, align_bytes=256) for k in u_codes}
-        v_raw = [keep.tile([P, 2, R], BF16, name="v_raw%d" % q, align_bytes=256) for q in range(SP)]
-        v_codes = [keep.tile([P, 512], U32, name="v_codes%d" % q, align_bytes=256) for q in range(SP)]
-        v_scales = [keep.tile([P, 512], U8, name="v_scales%d" % q, align_bytes=256) for q in range(SP)]
+        v_raw = [keep.tile([P, 1024], F32, name="v_raw%d" % q, align_bytes=256) for q in range(PAIRS)]
+        v_codes = [keep.tile([P, 512], U32, name="v_codes%d" % q, align_bytes=256) for q in range(PAIRS)]
+        v_scales = [keep.tile([P, 512], U8, name="v_scales%d" % q, align_bytes=256) for q in range(PAIRS)]
         h_codes = {(r, n): keep.tile([P, 512], U32, name="h_codes%d_%d" % (r, n), align_bytes=256) for r in range(2) for n in range(2)}
         h_scales = {k: keep.tile([P, 512], U8, name="h_scales%d_%d" % k, align_bytes=256) for k in h_codes}
 
@@ -76,129 +71,69 @@ def tile_factored_gain_correction_e3_kernel(tc, innov_words, innov_scales, obs_m
             else:
                 nc.vector.tensor_copy(out=out, in_=in_)
 
-        def order_words(engine, dst, src, runs):
-            copy(engine, dst.rearrange("p (x t q w) -> p x t q w", t=4, q=runs, w=8), src.rearrange("p (x q t w) -> p x t q w", t=4, q=runs, w=8))
+        def order_words(engine, dst, src, octets):
+            copy(engine, dst.rearrange("p (x t q j) -> p x t q j", t=4, q=octets, j=8), src.rearrange("p (x q t j) -> p x t q j", t=4, q=octets, j=8))
+
+        u_raw = {}
+
+        def load_u(g):
+            u_raw[g] = work.tile([P, 4, R], BF16, name="u_raw", tag="wide", bufs=WIDE_BUFS, align_bytes=256)
+            nc.sync.dma_start(out=u_raw[g][:], in_=obs_modes[512 * g : 512 * (g + 1), :].rearrange("(p k) w -> p k w", k=4))
+
+        def load_words(g, n):
+            words = innov_words[g, :, 512 * n : 512 * (n + 1), :].rearrange("p n t -> p (n t)")
+            nc.sync.dma_start(out=g_words[g, n][:].bitcast(I32), in_=words.bitcast(I32))
 
         def load_scales(n):
-            scale_rows = innov_scales[:, :, 512 * n : 512 * (n + 1)].rearrange("g (q j) n -> j q g n", j=4)
+            scale_rows = innov_scales[:, :, 512 * n : 512 * (n + 1)].rearrange("g (c j) n -> j c g n", j=4)
             for j in range(4):
                 nc.sync.dma_start(out=g_scales[n][j:P:32, :, :].bitcast(I32), in_=scale_rows[j].bitcast(I32))
 
-        def load_u(g):
-            raw = work.tile([P, 4, R], BF16, name="u_raw", tag="wide", bufs=WIDE_BUFS, align_bytes=256)
-            nc.sync.dma_start(out=raw[:], in_=obs_modes[512 * g : 512 * (g + 1), :].rearrange("(p j) w -> p j w", j=4))
-            u_raw[g] = raw
-
-        def load_w(lo, hi, n):
-            tile = keep.tile([P, hi - lo, 512], U32, name="g_words%d_%d" % (lo, n), align_bytes=256)
-            words = innov_words[lo:hi, :, 512 * n : 512 * (n + 1), :].rearrange("g p n t -> p g (n t)")
-            nc.sync.dma_start(out=tile[:].bitcast(I32), in_=words.bitcast(I32))
-            for g in range(lo, hi):
-                g_words[g, n] = tile[:, g - lo, :]
-
         def load_v(q):
+            raw = v_raw[q][:].bitcast(BF16)
             if q not in BY_VECTOR:
-                nc.sync.dma_start(out=v_raw[q][:], in_=v_rows[q])
+                nc.sync.dma_start(out=raw.rearrange("p (i r) -> p i r", i=2), in_=v_rows[q])
                 return
             quarters = state_modes[256 * q : 256 * (q + 1), :].rearrange("(j x) (c w) -> c j x w", x=8, c=4)
             for c in (0, 2, 1, 3):
-                rows = v_raw[q][32 * c : 32 * (c + 1)].rearrange("p i (y w) -> p (i y) w", w=256)
-                nc.sync.dma_start(out=rows, in_=quarters[c])
-
-        v_words = {}
-        v_group = {}
-        v_bank = {}
-
-        def group_tile(q):
-            if q not in v_group:
-                v_group[q] = work.tile([P, 2048], BF16, name="v_group", tag="v_group", bufs=GROUP_BUFS, align_bytes=256)
-            return v_group[q]
-
-        def raw_words(q):
-            return v_raw[q][:].rearrange("p i r -> p (i r)").bitcast(F32)
-
-        def order_v(q, engine="v", lo=0, hi=1024):
-            if q not in v_words:
-                v_words[q] = work.tile([P, 1024], F32, name="v_words", tag="v_words", bufs=WORD_BUFS, align_bytes=256)
-            order_words(engine, v_words[q][:, lo:hi], raw_words(q)[:, lo:hi], L // 4 if q in BY_VECTOR else L)
-
-        def transpose_v(a):
-            v_bank[a] = next_bank()
-            for c in range(4):
-                first = 512 * (a % 2) + P * c
-                nc.tensor.transpose(v_bank[a][:, P * c : P * (c + 1)], v_words[a // 2][:, first : first + P], ident[:])
-
-        def empty_v(a, engine):
-            dst = group_tile(a // 2)[:, 1024 * (a % 2) : 1024 * (a % 2 + 1)].bitcast(F32).rearrange("p (g s u) -> p g s u", g=2, u=2)
-            copy(engine, dst, v_bank[a][:].rearrange("p (g u s) -> p g s u", g=2, u=2))
-
-        def turn_blocks(q, lo=0, hi=1024):
-            nc.vector.transpose(raw_words(q)[:, lo:hi], v_words[q][:, lo:hi])
-
-        def group_blocks(q, starts=(0, 2)):
-            dst = group_tile(q)[:].bitcast(F32).rearrange("p (y j b u) -> p y j b u", y=4, b=4, u=2)
-            src = raw_words(q).rearrange("p (b y u j) -> p y j b u", b=4, y=4, u=2)
-            for lo in starts:
-                nc.vector.tensor_copy(out=dst[:, :, :, lo : lo + 2], in_=src[:, :, :, lo : lo + 2])
-
-        def quantize_v(q, lo=0, hi=512):
-            nc.vector.quantize_mx(out=v_codes[q][:, lo:hi].bitcast(E4), scales=v_scales[q][:, lo:hi], in_=v_group[q][:, 4 * lo : 4 * hi])
+                nc.sync.dma_start(out=raw[32 * c : 32 * (c + 1)].rearrange("p (x w) -> p x w", x=8), in_=quarters[c])
 
         u_group = {}
 
-        def group_u(g, r, u, engine, lo=0, hi=L):
+        def group_u(g, r, u, engine, lo, hi):
             if (g, r) not in u_group:
-                u_group[g, r] = work.tile([P, 4, P, 4], BF16, name="u_group", tag="u_group", bufs=4, align_bytes=256)
+                u_group[g, r] = work.tile([P, 4, P, 4], BF16, name="u_group", tag="u_group", bufs=U_BUFS, align_bytes=256)
             src = u_raw[g][:].rearrange("p k (q r u h j e) -> p r u q h k j e", r=2, u=2, h=4, j=2, e=2)
             dst = u_group[g, r][:].rearrange("p (u e) (q h j) k -> p u q h k j e", u=2, h=4, j=2)
             copy(engine, dst[:, u, lo:hi], src[:, r, u, lo:hi])
 
-        def quantize_u(g, r, lo=0, hi=4):
-            cols = slice(128 * lo, 128 * hi)
+        def quantize_u(g, r, lo, hi):
+            cols = slice(P * lo, P * hi)
             nc.vector.quantize_mx(
                 out=u_codes[g, r][:, cols].bitcast(E4),
                 scales=u_scales[g, r][:, cols],
-                in_=u_group[g, r][:, lo:hi].rearrange("p t m j -> p (t m j)"),
+                in_=u_group[g, r][:, lo:hi].rearrange("p t m k -> p (t m k)"),
             )
 
         z = {}
 
-        def stage1(g, r, n, slots):
-            for t in slots:
-                if g == 0:
-                    z[r, n, t] = next_bank()
-                m = slice(128 * t, 128 * (t + 1))
-                nc.tensor.matmul_mx(
-                    out=z[r, n, t][:],
-                    lhsT=u_codes[g, r][:, m].bitcast(E4),
-                    lhsT_scale=u_scales[g, r][:, m],
-                    rhs=g_words[g, n].bitcast(E5),
-                    rhs_scale=g_scales[n][:, g, :],
-                    start=(g == 0),
-                    stop=(g == KG - 1),
-                )
+        def stage1(g, r, n, t):
+            if g == 0:
+                z[r, n, t] = next_bank()
+            cols = slice(P * t, P * (t + 1))
+            nc.tensor.matmul_mx(
+                out=z[r, n, t][:],
+                lhsT=u_codes[g, r][:, cols].bitcast(E4),
+                lhsT_scale=u_scales[g, r][:, cols],
+                rhs=g_words[g, n][:].bitcast(E5),
+                rhs_scale=g_scales[n][:, g, :],
+                start=(g == 0),
+                stop=(g == KG - 1),
+            )
 
         def sweep_bank(r, n, t):
             for g in range(KG):
-                stage1(g, r, n, (t,))
-
-        def sweep_pairs(r, n, m, halves):
-            members = slice(256 * m, 256 * (m + 1))
-            for u in halves:
-                z[r, n, m, u] = next_bank()
-            for e in range(2):
-                for g in range(KG):
-                    for u in halves:
-                        cols = slice(128 * (2 * u + e), 128 * (2 * u + e + 1))
-                        nc.tensor.matmul_mx(
-                            out=z[r, n, m, u][:, 256 * e : 256 * (e + 1)],
-                            lhsT=u_codes[g, r][:, cols].bitcast(E4),
-                            lhsT_scale=u_scales[g, r][:, cols],
-                            rhs=g_words[g, n][:, members].bitcast(E5),
-                            rhs_scale=g_scales[n][:, g, members],
-                            start=(g == 0),
-                            stop=(g == KG - 1),
-                        )
+                stage1(g, r, n, t)
 
         h_rows = {}
         h_group = {}
@@ -206,30 +141,17 @@ def tile_factored_gain_correction_e3_kernel(tc, innov_words, innov_scales, obs_m
         def empty_z(r, n, t, engine):
             if (r, n) not in h_rows:
                 h_rows[r, n] = work.tile([P, 4, 512], BF16, name="h_rows", tag="h_rows", bufs=ROW_BUFS, align_bytes=256)
-            scale = gain[:, 4 * r + t : 4 * r + t + 1]
+            scale = gain[:, 2 * r + t // 2, t % 2 : t % 2 + 1]
             if engine == "s":
                 nc.scalar.activation(out=h_rows[r, n][:, t, :], in_=z[r, n, t][:], func=COPY, scale=scale)
             else:
                 nc.vector.tensor_scalar_mul(h_rows[r, n][:, t, :], z[r, n, t][:], scale)
 
-        def empty_pair(r, n, m, u):
-            if (r, n) not in h_rows:
-                h_rows[r, n] = work.tile([P, 4, 512], BF16, name="h_rows", tag="h_rows", bufs=ROW_BUFS, align_bytes=256)
-            gains = gain[:, 4 * r + 2 * u : 4 * r + 2 * u + 2].rearrange("p (o e) -> p o e", o=1).to_broadcast([P, 256, 2])
-            pairs = h_rows[r, n][:, 2 * m + u, :].rearrange("p (c e) -> p c e", e=2)
-            nc.vector.tensor_tensor(out=pairs, in0=z[r, n, m, u][:].rearrange("p (e c) -> p c e", e=2), in1=gains, op=MULT)
-
-        def group_pairs(r, n, m, engine):
+        def group_h(r, n, lo=0, hi=512):
             if (r, n) not in h_group:
                 h_group[r, n] = work.tile([P, 512, 4], BF16, name="h_group", tag="h_group", bufs=H_BUFS, align_bytes=256)
-            dst = h_group[r, n][:, 256 * m : 256 * (m + 1), :].bitcast(F32)
-            copy(engine, dst, h_rows[r, n][:, 2 * m : 2 * m + 2, :].bitcast(F32).rearrange("p u c -> p c u"))
-
-        def group_h(r, n, engine="v", lo=0, hi=P):
-            if (r, n) not in h_group:
-                h_group[r, n] = work.tile([P, 512, 4], BF16, name="h_group", tag="h_group", bufs=H_BUFS, align_bytes=256)
-            src = h_rows[r, n][:].rearrange("p t (c i) -> p c t i", i=4)
-            copy(engine, h_group[r, n][:].rearrange("p (c i) t -> p c t i", i=4)[:, lo:hi], src[:, lo:hi])
+            src = h_rows[r, n][:, :, lo:hi].rearrange("p t (c i) -> p c t i", i=4)
+            nc.vector.tensor_copy(out=h_group[r, n][:, lo:hi].rearrange("p (c i) t -> p c t i", i=4), in_=src)
 
         def quantize_h(r, n, lo=0, hi=512):
             nc.vector.quantize_mx(
@@ -238,187 +160,191 @@ def tile_factored_gain_correction_e3_kernel(tc, innov_words, innov_scales, obs_m
                 in_=h_group[r, n][:, lo:hi].rearrange("p n t -> p (n t)"),
             )
 
-        acc = {}
+        v_words = {}
+        v_group = {}
+        v_bank = {}
 
-        def stage2(a, n, mode_halves=(0, 1)):
+        def group_tile(q):
+            if q not in v_group:
+                v_group[q] = work.tile([P, 1024], F32, name="v_group", tag="v_group", bufs=GROUP_BUFS, align_bytes=256)
+            return v_group[q]
+
+        def order_v(q, engine, halves=(0, 1)):
+            if q not in v_words:
+                v_words[q] = word_tile(P, "v_words")
+            cols = slice(512 * halves[0], 512 * (halves[-1] + 1))
+            order_words(engine, v_words[q][:, cols], v_raw[q][:, cols], OCTETS // 4 if q in BY_VECTOR else OCTETS)
+
+        def transpose_v(a):
+            v_bank[a] = next_bank()
+            for t in range(4):
+                first = 512 * (a % 2) + P * t
+                nc.tensor.transpose(v_bank[a][:, P * t : P * (t + 1)], v_words[a // 2][:, first : first + P], ident[:])
+
+        def empty_v(a, engine):
+            dst = group_tile(a // 2)[:, 512 * (a % 2) : 512 * (a % 2 + 1)].rearrange("p (r s u) -> p r s u", r=2, u=2)
+            copy(engine, dst, v_bank[a][:].rearrange("p (r u s) -> p r s u", r=2, u=2))
+
+        def turn_blocks(q, halves=(0, 1)):
+            cols = slice(512 * halves[0], 512 * (halves[-1] + 1))
+            nc.vector.transpose(v_raw[q][:, cols], v_words[q][:, cols])
+
+        def group_blocks(q, half):
+            dst = group_tile(q)[:].rearrange("p (y j b u) -> p y j b u", y=4, b=4, u=2)
+            src = v_raw[q][:].rearrange("p (b y u j) -> p y j b u", b=4, y=4, u=2)
+            nc.vector.tensor_copy(out=dst[:, :, :, 2 * half : 2 * half + 2], in_=src[:, :, :, 2 * half : 2 * half + 2])
+
+        def quantize_v(q, halves=(0, 1)):
+            lo, hi = 256 * halves[0], 256 * (halves[-1] + 1)
+            nc.vector.quantize_mx(out=v_codes[q][:, lo:hi].bitcast(E4), scales=v_scales[q][:, lo:hi], in_=v_group[q][:, 2 * lo : 2 * hi].bitcast(BF16))
+
+        results = {}
+
+        def result_bank(a, n, engine):
             q, i = a // 2, a % 2
-            if (a, n) not in acc:
-                acc[a, n] = next_bank()
-            for r in mode_halves:
-                m = slice(256 * i + 128 * r, 256 * i + 128 * (r + 1))
+            acc = next_bank()
+            for r in range(2):
+                cols = slice(256 * i + P * r, 256 * i + P * (r + 1))
                 nc.tensor.matmul_mx(
-                    out=acc[a, n][:],
-                    lhsT=v_codes[q][:, m].bitcast(E4),
-                    lhsT_scale=v_scales[q][:, m],
+                    out=acc[:],
+                    lhsT=v_codes[q][:, cols].bitcast(E4),
+                    lhsT_scale=v_scales[q][:, cols],
                     rhs=h_codes[r, n][:].bitcast(E5),
                     rhs_scale=h_scales[r, n][:],
                     start=(r == 0),
                     stop=(r == 1),
                 )
+            if q not in results:
+                results[q] = work.tile([P, 2, N], F32, name="result", tag="wide", bufs=WIDE_BUFS, align_bytes=256)
+            copy(engine, results[q][:, i, 512 * n : 512 * (n + 1)], acc[:])
 
-        results = {}
+        def store(a, lo, hi):
+            nc.sync.dma_start(out=out_rows[a // 2][:, a % 2, lo:hi], in_=results[a // 2][:, a % 2, lo:hi])
 
-        def empty_out(a, n, engine):
-            if a // 2 not in results:
-                results[a // 2] = work.tile([P, 2, N], F32, name="result", tag="wide", bufs=WIDE_BUFS, align_bytes=256)
-            copy(engine, results[a // 2][:, a % 2, 512 * n : 512 * (n + 1)], acc[a, n][:])
-
-        def store(a, lo=0, hi=N, queue=nc.sync):
-            rows = slice(a % 2, a % 2 + 1)
-            queue.dma_start(out=out_rows[a // 2][:, rows, lo:hi], in_=results[a // 2][:, rows, lo:hi])
-
-        held = []
-
-        def release():
-            if held:
-                store(held.pop(), 0, N, nc.scalar)
-
-        def finish(a, engines, second_queue=False):
-            for n in range(2):
-                stage2(a, n)
-                empty_out(a, n, engines[n])
-                release()
-            if second_queue:
-                held.append(a)
-            else:
-                store(a)
-
-        def half_tile(a, n, mode_halves=(0, 1)):
-            stage2(a, n, mode_halves)
-            empty_out(a, n, "s")
+        def half_tile(a, n, engine="s"):
+            result_bank(a, n, engine)
             store(a, 512 * n, 512 * (n + 1))
 
-        nc.sync.dma_start(out=ratio_rows[:].bitcast(BF16), in_=mode_ratio.rearrange("(o c) -> o c", o=1))
-        nc.vector.memset(ratio_runs[:], 0.0)
-        for n in range(2):
-            nc.vector.memset(g_scales[n][:].rearrange("p g n -> p (g n)").bitcast(I32), 0)
+        def whole_tile(a, engines="ss"):
+            for n in range(2):
+                result_bank(a, n, engines[n])
+            store(a, 0, N)
+
+        ratio_row = word_tile(1, "ratio_row")
+        ratio_runs = word_tile(P, "ratio_runs")
+        nc.sync.dma_start(out=ratio_row[:, :512].bitcast(BF16), in_=mode_ratio.rearrange("(o c) -> o c", o=1))
+        nc.vector.memset(ratio_runs[:, :512], 0.0)
         make_identity(nc, ident[:])
         for g in range(KG):
             load_u(g)
-            load_w(g, g + 1, 0)
+            load_words(g, 0)
             if g == 0:
                 load_scales(0)
         load_scales(1)
         for g in range(KG):
-            load_w(g, g + 1, 1)
-        for q in range(SP):
-            if q != LATE_PAIR:
-                load_v(q)
-        load_v(LATE_PAIR)
+            load_words(g, 1)
+        for q in range(PAIRS):
+            load_v(q)
 
-        order_words("v", ratio_runs[0:1], ratio_rows[:], L)
+        order_words("v", ratio_runs[0:1, :512], ratio_row[:, :512], OCTETS)
         ratio_bank = psum.tile([P, 512], F32, name="ratio_bank", tag="bank7")
         for t in range(4):
             nc.tensor.transpose(ratio_bank[:, P * t : P * (t + 1)], ratio_runs[:, P * t : P * (t + 1)], ident[:])
-        ratio_turned = ratio_bank[:].bitcast(BF16).rearrange("p (t k e) -> p k t e", t=4, e=2)[:, 0]
-        nc.vector.tensor_copy(out=ratio32[:].rearrange("p (t e) -> p t e", t=4), in_=ratio_turned)
-        nc.vector.tensor_tensor(out=square[:], in0=ratio32[:], in1=ratio32[:], op=MULT)
-        nc.vector.tensor_scalar_add(square[:], square[:], 1.0)
-        nc.vector.reciprocal(square[:], square[:])
-        nc.vector.tensor_tensor(out=gain[:], in0=ratio32[:], in1=square[:], op=MULT)
+        ratio = ratio_bank[:].bitcast(BF16).rearrange("p (t s e) -> p s t e", t=4, e=2)[:, 0]
+        nc.vector.reciprocal(inverse[:], ratio)
+        nc.vector.tensor_tensor(out=total[:], in0=ratio, in1=inverse[:], op=ADD)
+        nc.vector.reciprocal(gain[:], total[:])
 
-        for g in range(KG - 1):
-            group_u(g, 0, 1, "s")
-            group_u(g, 1, 1, "s", U_CUT, L)
-            group_u(g, 0, 0, "v")
-            group_u(g, 1, 1, "v", 0, U_CUT)
-            quantize_u(g, 0, 0, 2)
-            group_u(g, 1, 0, "v")
-            quantize_u(g, 0, 2, 4)
-            stage1(g, 0, 0, range(4))
-            quantize_u(g, 1, 0, 2)
-            quantize_u(g, 1, 2, 4)
-            stage1(g, 1, 0, range(4))
-        g = KG - 1
-        group_u(g, 0, 0, "s", FIRST_CUT, L)
-        group_u(g, 0, 1, "s", L // 2, L)
-        group_u(g, 1, 0, "s", L // 2, L)
-        group_u(g, 1, 1, "s", LAST_CUT, L)
-        group_u(g, 0, 0, "v", 0, FIRST_CUT)
-        group_u(g, 0, 1, "v", 0, L // 2)
-        quantize_u(g, 0, 0, 2)
-        group_u(g, 1, 0, "v", 0, L // 2)
-        quantize_u(g, 0, 2, 4)
-        stage1(g, 0, 0, range(4))
-        group_u(g, 1, 1, "v", 0, LAST_CUT)
-        quantize_u(g, 1, 0, 2)
-        quantize_u(g, 1, 2, 3)
-        quantize_u(g, 1, 3, 4)
-        stage1(g, 1, 0, range(4))
+        for g in range(KG):
+            last = g == KG - 1
+            for x in range(4):
+                group_u(g, x // 2, x % 2, "s", U_SHARES[x], OCTETS)
+            group_u(g, 0, 0, "v", 0, U_SHARES[0])
+            for tile in range(8):
+                r, t = tile // 4, tile % 4
+                if tile in ((0, 2, 5) if last else (0, 2, 4)):
+                    x = tile // 2 + 1
+                    group_u(g, x // 2, x % 2, "v", 0, U_SHARES[x])
+                if last:
+                    quantize_u(g, r, t, t + 1)
+                elif t % 2 == 0:
+                    quantize_u(g, r, t, t + 2)
+                stage1(g, r, 0, t)
 
-        for r in range(2):
-            for t in range(4):
-                empty_z(r, 0, t, "ssvv"[t] if r == 0 else "vsss"[t])
+        for t in range(4):
+            empty_z(0, 0, t, "ssvv"[t])
+        for t in range(4):
+            empty_z(1, 0, t, "s")
         group_h(0, 0)
-        order_v(0)
+        order_v(0, "v")
         quantize_h(0, 0)
-        order_v(1)
         for t in range(4):
             sweep_bank(0, 1, t)
             empty_z(0, 1, t, "s")
-            if t == 0:
-                group_h(1, 0, "s", 0, H_CUT)
-        group_h(1, 0, "v", H_CUT, P)
-        order_v(2)
+            if t in (1, 2):
+                order_v(1, "s", (t - 1,))
+        group_h(1, 0)
+        order_v(2, "v")
         quantize_h(1, 0)
         for a in range(4):
             transpose_v(a)
             empty_v(a, "s")
-        order_v(4, "s")
         group_h(0, 1)
-        sweep_pairs(1, 1, 0, (0,))
-        empty_pair(1, 1, 0, 0)
         quantize_v(0)
-        sweep_pairs(1, 1, 0, (1,))
-        empty_pair(1, 1, 0, 1)
+        order_v(3, "v")
         quantize_v(1)
-        order_v(5, "s")
-        group_pairs(1, 1, 0, "s")
-        sweep_pairs(1, 1, 1, (0,))
-        empty_pair(1, 1, 1, 0)
+        turn_blocks(3)
         quantize_h(0, 1)
-        sweep_pairs(1, 1, 1, (1,))
-        empty_pair(1, 1, 1, 1)
-        turn_blocks(4, 0, HALF)
-        group_pairs(1, 1, 1, "v")
+        group_blocks(3, 0)
+        group_blocks(3, 1)
+        for t in range(4):
+            sweep_bank(1, 1, t)
+            empty_z(1, 1, t, "s")
+            if t < 2:
+                order_v(4, "s", (t,))
+            if t == 2:
+                order_v(5, "s", (0,))
+        group_h(1, 1, 0, 256)
+        group_h(1, 1, 256, 512)
         quantize_h(1, 1, 0, 256)
         quantize_h(1, 1, 256, 512)
-        turn_blocks(4, HALF, 2 * HALF)
+
         for a in range(4):
             half_tile(a, 0)
         for a in (4, 5):
             transpose_v(a)
             empty_v(a, "vs"[a % 2])
-        group_blocks(4, (0,))
-        quantize_v(2, 0, 256)
-        group_blocks(4, (2,))
-        quantize_v(2, 256, 512)
+        quantize_v(3)
+        quantize_v(2)
         for a in range(4):
             half_tile(a, 1)
-        finish(4, "ss")
-        finish(5, "ss")
-        for q, filler in ((4, 6), (5, 3), (6, 7)):
-            order_v(filler, "v", 0, HALF)
-            if q > 4:
-                group_blocks(q)
-            order_v(filler, "v", HALF, 2 * HALF)
-            quantize_v(q)
-            if q < 6:
-                turn_blocks(q + 1)
-            else:
-                turn_blocks(7, 0, HALF)
-                for a in range(6, 8):
-                    transpose_v(a)
-                    empty_v(a, "sv"[a % 2])
-                    release()
-                turn_blocks(7, HALF, 2 * HALF)
-                quantize_v(3, 0, 256)
-                group_blocks(7, (0,))
-                quantize_v(3, 256, 512)
-                group_blocks(7, (2,))
-            finish(2 * q, "ss")
-            finish(2 * q + 1, "ss", True)
-        quantize_v(7)
-        for a in (6, 7, 14, 15):
-            finish(a, "sv" if a == 6 else "vs", a % 2 == 1)
-            release()
+        turn_blocks(4)
+        order_v(5, "v", (1,))
+        group_blocks(4, 0)
+        group_blocks(4, 1)
+        order_v(6, "v")
+        quantize_v(4)
+        turn_blocks(5)
+        order_v(7, "v", (0,))
+        group_blocks(5, 0)
+        group_blocks(5, 1)
+        order_v(7, "v", (1,))
+        quantize_v(5)
+        turn_blocks(6, (0,))
+        turn_blocks(6, (1,))
+        for a in range(4, 12):
+            whole_tile(a)
+        for a in (14, 15):
+            transpose_v(a)
+        group_blocks(6, 0)
+        group_blocks(6, 1)
+        quantize_v(6)
+        empty_v(14, "v")
+        empty_v(15, "v")
+        for a in (12, 13):
+            for n in range(2):
+                half_tile(a, n)
+            quantize_v(7, (a % 2,))
+        for a in (14, 15):
+            for n in range(2):
+                half_tile(a, n, "vs"[n])

@@ -20,14 +20,12 @@ P = 128
 KG = K // 512
 PAIRS = S // (2 * P)
 OCTETS = P // 8
-BY_VECTOR = (3, 4, 5, 6)
+BY_VECTOR = (3, 4, 5, 7)
 U_SHARES = (10, 8, 10, 8)
 WIDE_BUFS = 7
 WORD_BUFS = 4
 GROUP_BUFS = 3
-H_BUFS = 2
-ROW_BUFS = 3
-U_BUFS = 4
+QUAD_BUFS = 9
 
 
 def tile_factored_gain_correction_e3_kernel(tc, innov_words, innov_scales, obs_modes, mode_ratio, state_modes, out):
@@ -102,7 +100,7 @@ def tile_factored_gain_correction_e3_kernel(tc, innov_words, innov_scales, obs_m
 
         def group_u(g, r, u, engine, lo, hi):
             if (g, r) not in u_group:
-                u_group[g, r] = work.tile([P, 4, P, 4], BF16, name="u_group", tag="u_group", bufs=U_BUFS, align_bytes=256)
+                u_group[g, r] = work.tile([P, 4, P, 4], BF16, name="u_group", tag="quad", bufs=QUAD_BUFS, align_bytes=256)
             src = u_raw[g][:].rearrange("p k (q r u h j e) -> p r u q h k j e", r=2, u=2, h=4, j=2, e=2)
             dst = u_group[g, r][:].rearrange("p (u e) (q h j) k -> p u q h k j e", u=2, h=4, j=2)
             copy(engine, dst[:, u, lo:hi], src[:, r, u, lo:hi])
@@ -140,7 +138,7 @@ def tile_factored_gain_correction_e3_kernel(tc, innov_words, innov_scales, obs_m
 
         def empty_z(r, n, t, engine):
             if (r, n) not in h_rows:
-                h_rows[r, n] = work.tile([P, 4, 512], BF16, name="h_rows", tag="h_rows", bufs=ROW_BUFS, align_bytes=256)
+                h_rows[r, n] = work.tile([P, 4, 512], BF16, name="h_rows", tag="quad", bufs=QUAD_BUFS, align_bytes=256)
             scale = gain[:, 2 * r + t // 2, t % 2 : t % 2 + 1]
             if engine == "s":
                 nc.scalar.activation(out=h_rows[r, n][:, t, :], in_=z[r, n, t][:], func=COPY, scale=scale)
@@ -149,7 +147,7 @@ def tile_factored_gain_correction_e3_kernel(tc, innov_words, innov_scales, obs_m
 
         def group_h(r, n, lo=0, hi=512):
             if (r, n) not in h_group:
-                h_group[r, n] = work.tile([P, 512, 4], BF16, name="h_group", tag="h_group", bufs=H_BUFS, align_bytes=256)
+                h_group[r, n] = work.tile([P, 512, 4], BF16, name="h_group", tag="quad", bufs=QUAD_BUFS, align_bytes=256)
             src = h_rows[r, n][:, :, lo:hi].rearrange("p t (c i) -> p c t i", i=4)
             nc.vector.tensor_copy(out=h_group[r, n][:, lo:hi].rearrange("p (c i) t -> p c t i", i=4), in_=src)
 
@@ -200,13 +198,15 @@ def tile_factored_gain_correction_e3_kernel(tc, innov_words, innov_scales, obs_m
 
         results = {}
 
-        def result_bank(a, n, engine):
+        sums = {}
+
+        def stage2(a, n):
             q, i = a // 2, a % 2
-            acc = next_bank()
+            sums[a, n] = next_bank()
             for r in range(2):
                 cols = slice(256 * i + P * r, 256 * i + P * (r + 1))
                 nc.tensor.matmul_mx(
-                    out=acc[:],
+                    out=sums[a, n][:],
                     lhsT=v_codes[q][:, cols].bitcast(E4),
                     lhsT_scale=v_scales[q][:, cols],
                     rhs=h_codes[r, n][:].bitcast(E5),
@@ -214,20 +214,26 @@ def tile_factored_gain_correction_e3_kernel(tc, innov_words, innov_scales, obs_m
                     start=(r == 0),
                     stop=(r == 1),
                 )
+
+        def empty_sum(a, n, engine):
+            q, i = a // 2, a % 2
             if q not in results:
                 results[q] = work.tile([P, 2, N], F32, name="result", tag="wide", bufs=WIDE_BUFS, align_bytes=256)
-            copy(engine, results[q][:, i, 512 * n : 512 * (n + 1)], acc[:])
+            copy(engine, results[q][:, i, 512 * n : 512 * (n + 1)], sums[a, n][:])
 
         def store(a, lo, hi):
             nc.sync.dma_start(out=out_rows[a // 2][:, a % 2, lo:hi], in_=results[a // 2][:, a % 2, lo:hi])
 
         def half_tile(a, n, engine="s"):
-            result_bank(a, n, engine)
+            stage2(a, n)
+            empty_sum(a, n, engine)
             store(a, 512 * n, 512 * (n + 1))
 
-        def whole_tile(a, engines="ss"):
+        def whole_tile(a, engines="ss", order=(0, 1)):
             for n in range(2):
-                result_bank(a, n, engines[n])
+                stage2(a, n)
+            for n in order:
+                empty_sum(a, n, engines[n])
             store(a, 0, N)
 
         ratio_row = word_tile(1, "ratio_row")
@@ -243,7 +249,7 @@ def tile_factored_gain_correction_e3_kernel(tc, innov_words, innov_scales, obs_m
         load_scales(1)
         for g in range(KG):
             load_words(g, 1)
-        for q in range(PAIRS):
+        for q in (0, 1, 2, 3, 4, 5, 7, 6):
             load_v(q)
 
         order_words("v", ratio_runs[0:1, :512], ratio_row[:, :512], OCTETS)
@@ -271,23 +277,25 @@ def tile_factored_gain_correction_e3_kernel(tc, innov_words, innov_scales, obs_m
                     quantize_u(g, r, t, t + 2)
                 stage1(g, r, 0, t)
 
-        for t in range(4):
+        for t in (1, 0, 2, 3):
             empty_z(0, 0, t, "ssvv"[t])
-        for t in range(4):
-            empty_z(1, 0, t, "s")
+        for t in (0, 3, 2, 1):
+            empty_z(1, 0, t, "vsss"[t])
         group_h(0, 0)
         order_v(0, "v")
         quantize_h(0, 0)
+        order_v(1, "v", (0,))
         for t in range(4):
             sweep_bank(0, 1, t)
             empty_z(0, 1, t, "s")
-            if t in (1, 2):
-                order_v(1, "s", (t - 1,))
+            if t == 0:
+                order_v(1, "s", (1,))
         group_h(1, 0)
         order_v(2, "v")
         quantize_h(1, 0)
         for a in range(4):
             transpose_v(a)
+        for a in (1, 0, 3, 2):
             empty_v(a, "s")
         group_h(0, 1)
         quantize_v(0)
@@ -296,18 +304,16 @@ def tile_factored_gain_correction_e3_kernel(tc, innov_words, innov_scales, obs_m
         turn_blocks(3)
         quantize_h(0, 1)
         group_blocks(3, 0)
-        group_blocks(3, 1)
         for t in range(4):
             sweep_bank(1, 1, t)
             empty_z(1, 1, t, "s")
             if t < 2:
                 order_v(4, "s", (t,))
-            if t == 2:
-                order_v(5, "s", (0,))
         group_h(1, 1, 0, 256)
         group_h(1, 1, 256, 512)
         quantize_h(1, 1, 0, 256)
         quantize_h(1, 1, 256, 512)
+        group_blocks(3, 1)
 
         for a in range(4):
             half_tile(a, 0)
@@ -319,32 +325,34 @@ def tile_factored_gain_correction_e3_kernel(tc, innov_words, innov_scales, obs_m
         for a in range(4):
             half_tile(a, 1)
         turn_blocks(4)
-        order_v(5, "v", (1,))
+        order_v(5, "v", (0,))
         group_blocks(4, 0)
         group_blocks(4, 1)
-        order_v(6, "v")
+        order_v(5, "v", (1,))
         quantize_v(4)
         turn_blocks(5)
-        order_v(7, "v", (0,))
+        order_v(6, "v", (0,))
         group_blocks(5, 0)
         group_blocks(5, 1)
-        order_v(7, "v", (1,))
+        order_v(6, "v", (1,))
         quantize_v(5)
-        turn_blocks(6, (0,))
-        turn_blocks(6, (1,))
-        for a in range(4, 12):
-            whole_tile(a)
-        for a in (14, 15):
-            transpose_v(a)
-        group_blocks(6, 0)
-        group_blocks(6, 1)
-        quantize_v(6)
-        empty_v(14, "v")
-        empty_v(15, "v")
+        order_v(7, "v", (0,))
+        order_v(7, "v", (1,))
+        turn_blocks(7, (0,))
+        for a in range(4, 10):
+            whole_tile(a, "ss", (1, 0))
         for a in (12, 13):
-            for n in range(2):
-                half_tile(a, n)
-            quantize_v(7, (a % 2,))
-        for a in (14, 15):
-            for n in range(2):
-                half_tile(a, n, "vs"[n])
+            transpose_v(a)
+            empty_v(a, "v")
+        quantize_v(6, (0,))
+        turn_blocks(7, (1,))
+        quantize_v(6, (1,))
+        group_blocks(7, 0)
+        group_blocks(7, 1)
+        for a in (10, 11):
+            whole_tile(a)
+        whole_tile(12, "vs")
+        quantize_v(7, (0,))
+        quantize_v(7, (1,))
+        for a in (13, 14, 15):
+            whole_tile(a, "vs")

@@ -15,6 +15,7 @@ E4 = mybir.dt.float8_e4m3fn_x4
 E5 = mybir.dt.float8_e5m2_x4
 COPY = mybir.ActivationFunctionType.Copy
 ADD = mybir.AluOpType.add
+MULT = mybir.AluOpType.mult
 
 P = 128
 KG = K // 512
@@ -133,8 +134,37 @@ def tile_factored_gain_correction_e3_kernel(tc, innov_words, innov_scales, obs_m
             for g in range(KG):
                 stage1(g, r, n, t)
 
+        def sweep_pair(m, u):
+            members = slice(256 * m, 256 * (m + 1))
+            z[m, u] = next_bank()
+            for e in range(2):
+                cols = slice(P * (2 * u + e), P * (2 * u + e + 1))
+                for g in range(KG):
+                    nc.tensor.matmul_mx(
+                        out=z[m, u][:, 256 * e : 256 * (e + 1)],
+                        lhsT=u_codes[g, 1][:, cols].bitcast(E4),
+                        lhsT_scale=u_scales[g, 1][:, cols],
+                        rhs=g_words[g, 1][:, members].bitcast(E5),
+                        rhs_scale=g_scales[1][:, g, members],
+                        start=(g == 0),
+                        stop=(g == KG - 1),
+                    )
+
         h_rows = {}
         h_group = {}
+
+        def empty_pair(m, u):
+            if (1, 1) not in h_rows:
+                h_rows[1, 1] = work.tile([P, 4, 512], BF16, name="h_pairs", tag="quad", bufs=QUAD_BUFS, align_bytes=256)
+            gains = gain[:, 2 + u : 3 + u, :].to_broadcast([P, 256, 2])
+            pairs = h_rows[1, 1][:, 2 * m + u, :].rearrange("p (c e) -> p c e", e=2)
+            nc.vector.tensor_tensor(out=pairs, in0=z[m, u][:].rearrange("p (e c) -> p c e", e=2), in1=gains, op=MULT)
+
+        def group_pairs(m, engine):
+            if (1, 1) not in h_group:
+                h_group[1, 1] = work.tile([P, 512, 4], BF16, name="h_group", tag="quad", bufs=QUAD_BUFS, align_bytes=256)
+            dst = h_group[1, 1][:, 256 * m : 256 * (m + 1), :].bitcast(F32)
+            copy(engine, dst, h_rows[1, 1][:, 2 * m : 2 * m + 2, :].bitcast(F32).rearrange("p u c -> p c u"))
 
         def empty_z(r, n, t, engine):
             if (r, n) not in h_rows:
@@ -183,9 +213,8 @@ def tile_factored_gain_correction_e3_kernel(tc, innov_words, innov_scales, obs_m
             dst = group_tile(a // 2)[:, 512 * (a % 2) : 512 * (a % 2 + 1)].rearrange("p (r s u) -> p r s u", r=2, u=2)
             copy(engine, dst, v_bank[a][:].rearrange("p (r u s) -> p r s u", r=2, u=2))
 
-        def turn_blocks(q, halves=(0, 1)):
-            cols = slice(512 * halves[0], 512 * (halves[-1] + 1))
-            nc.vector.transpose(v_raw[q][:, cols], v_words[q][:, cols])
+        def turn_blocks(q, lo=0, hi=1024):
+            nc.vector.transpose(v_raw[q][:, lo:hi], v_words[q][:, lo:hi])
 
         def group_blocks(q, half):
             dst = group_tile(q)[:].rearrange("p (y j b u) -> p y j b u", y=4, b=4, u=2)
@@ -249,7 +278,7 @@ def tile_factored_gain_correction_e3_kernel(tc, innov_words, innov_scales, obs_m
         load_scales(1)
         for g in range(KG):
             load_words(g, 1)
-        for q in (0, 1, 2, 3, 4, 5, 7, 6):
+        for q in (0, 1, 2, 3, 4, 6, 5, 7):
             load_v(q)
 
         order_words("v", ratio_runs[0:1, :512], ratio_row[:, :512], OCTETS)
@@ -297,61 +326,67 @@ def tile_factored_gain_correction_e3_kernel(tc, innov_words, innov_scales, obs_m
             transpose_v(a)
         for a in (1, 0, 3, 2):
             empty_v(a, "s")
+        order_v(3, "s")
+        order_v(4, "s")
         group_h(0, 1)
+        sweep_pair(0, 0)
+        empty_pair(0, 0)
         quantize_v(0)
-        order_v(3, "v")
+        sweep_pair(0, 1)
+        empty_pair(0, 1)
         quantize_v(1)
-        turn_blocks(3)
+        group_pairs(0, "s")
+        order_v(6, "s", (0,))
+        sweep_pair(1, 0)
+        empty_pair(1, 0)
         quantize_h(0, 1)
-        group_blocks(3, 0)
-        for t in range(4):
-            sweep_bank(1, 1, t)
-            empty_z(1, 1, t, "s")
-            if t < 2:
-                order_v(4, "s", (t,))
-        group_h(1, 1, 0, 256)
-        group_h(1, 1, 256, 512)
+        sweep_pair(1, 1)
+        empty_pair(1, 1)
         quantize_h(1, 1, 0, 256)
+        group_pairs(1, "v")
+        turn_blocks(3, 0, 256)
         quantize_h(1, 1, 256, 512)
-        group_blocks(3, 1)
+        turn_blocks(3, 256, 1024)
 
         for a in range(4):
             half_tile(a, 0)
         for a in (4, 5):
             transpose_v(a)
             empty_v(a, "vs"[a % 2])
+        group_blocks(3, 0)
+        quantize_v(2, (0,))
+        group_blocks(3, 1)
+        quantize_v(2, (1,))
+        order_v(5, "v", (0,))
         quantize_v(3)
-        quantize_v(2)
         for a in range(4):
             half_tile(a, 1)
         turn_blocks(4)
-        order_v(5, "v", (0,))
+        order_v(5, "v", (1,))
         group_blocks(4, 0)
         group_blocks(4, 1)
-        order_v(5, "v", (1,))
+        order_v(6, "v", (1,))
         quantize_v(4)
         turn_blocks(5)
-        order_v(6, "v", (0,))
+        order_v(7, "v", (0,))
         group_blocks(5, 0)
         group_blocks(5, 1)
-        order_v(6, "v", (1,))
-        quantize_v(5)
-        order_v(7, "v", (0,))
         order_v(7, "v", (1,))
-        turn_blocks(7, (0,))
+        quantize_v(5)
         for a in range(4, 10):
             whole_tile(a, "ss", (1, 0))
         for a in (12, 13):
             transpose_v(a)
             empty_v(a, "v")
+        turn_blocks(7, 0, 256)
         quantize_v(6, (0,))
-        turn_blocks(7, (1,))
+        turn_blocks(7, 256, 1024)
         quantize_v(6, (1,))
         group_blocks(7, 0)
         group_blocks(7, 1)
         for a in (10, 11):
             whole_tile(a)
-        whole_tile(12, "vs")
+        whole_tile(12)
         quantize_v(7, (0,))
         quantize_v(7, (1,))
         for a in (13, 14, 15):

@@ -21,8 +21,9 @@ P = 128
 KG = K // 512
 PAIRS = S // (2 * P)
 OCTETS = P // 8
-BY_VECTOR = (3, 4, 5, 7)
+BY_VECTOR = (3, 4, 5, 6, 7)
 U_SHARES = (10, 8, 10, 8)
+H_CUT = 352
 WIDE_BUFS = 7
 WORD_BUFS = 4
 GROUP_BUFS = 3
@@ -175,11 +176,11 @@ def tile_factored_gain_correction_e3_kernel(tc, innov_words, innov_scales, obs_m
             else:
                 nc.vector.tensor_scalar_mul(h_rows[r, n][:, t, :], z[r, n, t][:], scale)
 
-        def group_h(r, n, lo=0, hi=512):
+        def group_h(r, n, lo=0, hi=512, engine="v"):
             if (r, n) not in h_group:
                 h_group[r, n] = work.tile([P, 512, 4], BF16, name="h_group", tag="quad", bufs=QUAD_BUFS, align_bytes=256)
             src = h_rows[r, n][:, :, lo:hi].rearrange("p t (c i) -> p c t i", i=4)
-            nc.vector.tensor_copy(out=h_group[r, n][:, lo:hi].rearrange("p (c i) t -> p c t i", i=4), in_=src)
+            copy(engine, h_group[r, n][:, lo:hi].rearrange("p (c i) t -> p c t i", i=4), src)
 
         def quantize_h(r, n, lo=0, hi=512):
             nc.vector.quantize_mx(
@@ -216,10 +217,11 @@ def tile_factored_gain_correction_e3_kernel(tc, innov_words, innov_scales, obs_m
         def turn_blocks(q, lo=0, hi=1024):
             nc.vector.transpose(v_raw[q][:, lo:hi], v_words[q][:, lo:hi])
 
-        def group_blocks(q, half):
+        def group_blocks(q, half, tiles=(0, 1)):
             dst = group_tile(q)[:].rearrange("p (y j b u) -> p y j b u", y=4, b=4, u=2)
             src = v_raw[q][:].rearrange("p (b y u j) -> p y j b u", b=4, y=4, u=2)
-            nc.vector.tensor_copy(out=dst[:, :, :, 2 * half : 2 * half + 2], in_=src[:, :, :, 2 * half : 2 * half + 2])
+            y = slice(2 * tiles[0], 2 * tiles[-1] + 2)
+            nc.vector.tensor_copy(out=dst[:, y, :, 2 * half : 2 * half + 2], in_=src[:, y, :, 2 * half : 2 * half + 2])
 
         def quantize_v(q, halves=(0, 1)):
             lo, hi = 256 * halves[0], 256 * (halves[-1] + 1)
@@ -253,15 +255,14 @@ def tile_factored_gain_correction_e3_kernel(tc, innov_words, innov_scales, obs_m
         def store(a, lo, hi):
             nc.sync.dma_start(out=out_rows[a // 2][:, a % 2, lo:hi], in_=results[a // 2][:, a % 2, lo:hi])
 
-        def half_tile(a, n, engine="s"):
+        def half_tile(a, n):
             stage2(a, n)
-            empty_sum(a, n, engine)
+            empty_sum(a, n, "s")
             store(a, 512 * n, 512 * (n + 1))
 
-        def whole_tile(a, engines="ss", order=(0, 1)):
+        def whole_tile(a, engines="ss"):
             for n in range(2):
                 stage2(a, n)
-            for n in order:
                 empty_sum(a, n, engines[n])
             store(a, 0, N)
 
@@ -278,7 +279,7 @@ def tile_factored_gain_correction_e3_kernel(tc, innov_words, innov_scales, obs_m
         load_scales(1)
         for g in range(KG):
             load_words(g, 1)
-        for q in (0, 1, 2, 3, 4, 6, 5, 7):
+        for q in range(PAIRS):
             load_v(q)
 
         order_words("v", ratio_runs[0:1, :512], ratio_row[:, :512], OCTETS)
@@ -306,88 +307,73 @@ def tile_factored_gain_correction_e3_kernel(tc, innov_words, innov_scales, obs_m
                     quantize_u(g, r, t, t + 2)
                 stage1(g, r, 0, t)
 
-        for t in (1, 0, 2, 3):
+        for t in range(4):
             empty_z(0, 0, t, "ssvv"[t])
-        for t in (0, 3, 2, 1):
-            empty_z(1, 0, t, "vsss"[t])
+        for t in range(4):
+            empty_z(1, 0, t, "s")
         group_h(0, 0)
         order_v(0, "v")
         quantize_h(0, 0)
-        order_v(1, "v", (0,))
         for t in range(4):
             sweep_bank(0, 1, t)
             empty_z(0, 1, t, "s")
-            if t == 0:
-                order_v(1, "s", (1,))
+            if t in (1, 2):
+                order_v(1, "s", (t - 1,))
         group_h(1, 0)
         order_v(2, "v")
         quantize_h(1, 0)
         for a in range(4):
             transpose_v(a)
-        for a in (1, 0, 3, 2):
             empty_v(a, "s")
+            if a == 0:
+                group_h(0, 1, H_CUT, 512, "s")
         order_v(3, "s")
         order_v(4, "s")
-        group_h(0, 1)
+        group_h(0, 1, 0, H_CUT)
+        quantize_v(0, (0,))
+        quantize_h(0, 1)
         sweep_pair(0, 0)
         empty_pair(0, 0)
-        quantize_v(0)
+        quantize_v(0, (1,))
         sweep_pair(0, 1)
         empty_pair(0, 1)
         quantize_v(1)
         group_pairs(0, "s")
-        order_v(6, "s", (0,))
         sweep_pair(1, 0)
         empty_pair(1, 0)
-        quantize_h(0, 1)
+        turn_blocks(3, 0, 512)
         sweep_pair(1, 1)
         empty_pair(1, 1)
         quantize_h(1, 1, 0, 256)
         group_pairs(1, "v")
-        turn_blocks(3, 0, 256)
+        turn_blocks(3, 512, 1024)
         quantize_h(1, 1, 256, 512)
-        turn_blocks(3, 256, 1024)
 
         for a in range(4):
             half_tile(a, 0)
+        group_blocks(3, 0)
+        group_blocks(3, 1)
         for a in (4, 5):
             transpose_v(a)
             empty_v(a, "vs"[a % 2])
-        group_blocks(3, 0)
-        quantize_v(2, (0,))
-        group_blocks(3, 1)
-        quantize_v(2, (1,))
-        order_v(5, "v", (0,))
         quantize_v(3)
+        quantize_v(2)
         for a in range(4):
             half_tile(a, 1)
-        turn_blocks(4)
-        order_v(5, "v", (1,))
-        group_blocks(4, 0)
-        group_blocks(4, 1)
-        order_v(6, "v", (1,))
-        quantize_v(4)
-        turn_blocks(5)
-        order_v(7, "v", (0,))
-        group_blocks(5, 0)
-        group_blocks(5, 1)
-        order_v(7, "v", (1,))
-        quantize_v(5)
-        for a in range(4, 10):
-            whole_tile(a, "ss", (1, 0))
-        for a in (12, 13):
-            transpose_v(a)
-            empty_v(a, "v")
-        turn_blocks(7, 0, 256)
-        quantize_v(6, (0,))
-        turn_blocks(7, 256, 1024)
-        quantize_v(6, (1,))
-        group_blocks(7, 0)
-        group_blocks(7, 1)
-        for a in (10, 11):
-            whole_tile(a)
-        whole_tile(12)
-        quantize_v(7, (0,))
-        quantize_v(7, (1,))
-        for a in (13, 14, 15):
-            whole_tile(a, "vs")
+        for q in range(4, PAIRS - 1):
+            turn_blocks(q)
+            order_v(q + 1, "v", (0,))
+            group_blocks(q, 0)
+            group_blocks(q, 1)
+            order_v(q + 1, "v", (1,))
+            quantize_v(q)
+        q = PAIRS - 1
+        turn_blocks(q, 0, 512)
+        turn_blocks(q, 512, 1024)
+        group_blocks(q, 0)
+        group_blocks(q, 1, (0,))
+        group_blocks(q, 1, (1,))
+        quantize_v(q, (0,))
+        quantize_v(q, (1,))
+        for a in range(4, 2 * PAIRS):
+            whole_tile(a, "ss" if a < 14 else "vs")

@@ -94,9 +94,11 @@ def tile_factored_gain_correction_e3_kernel(tc, innov_words, innov_scales, obs_m
             if q not in BY_VECTOR:
                 nc.sync.dma_start(out=raw.rearrange("p (i r) -> p i r", i=2), in_=v_rows[q])
                 return
-            quarters = state_modes[256 * q : 256 * (q + 1), :].rearrange("(j x) (c w) -> c j x w", x=8, c=4)
-            for c in (0, 2, 1, 3):
-                nc.sync.dma_start(out=raw[32 * c : 32 * (c + 1)].rearrange("p (x w) -> p x w", x=8), in_=quarters[c])
+            quarters = state_modes[256 * q : 256 * (q + 1), :].rearrange("(j y x) (c w) -> y c j x w", y=2, x=4, c=4)
+            for y in range(2):
+                for c in (0, 2, 1, 3):
+                    rows = raw[32 * c : 32 * (c + 1), 1024 * y : 1024 * (y + 1)].rearrange("p (x w) -> p x w", x=4)
+                    nc.sync.dma_start(out=rows, in_=quarters[y, c])
 
         u_group = {}
 

@@ -22,6 +22,7 @@ KG = K // 512
 PAIRS = S // (2 * P)
 OCTETS = P // 8
 BY_VECTOR = (3, 4, 5, 6, 7)
+MIXED = 2
 U_SHARES = (10, 8, 10, 8)
 H_CUT = 352
 WIDE_BUFS = 7
@@ -88,6 +89,13 @@ def tile_factored_gain_correction_e3_kernel(tc, innov_words, innov_scales, obs_m
             scale_rows = innov_scales[:, :, 512 * n : 512 * (n + 1)].rearrange("g (c j) n -> j c g n", j=4)
             for j in range(4):
                 nc.sync.dma_start(out=g_scales[n][j:P:32, :, :].bitcast(I32), in_=scale_rows[j].bitcast(I32))
+
+        def load_mixed():
+            raw = v_raw[MIXED][:].bitcast(BF16)
+            nc.sync.dma_start(out=raw[:, :R], in_=v_rows[MIXED][:, 0, :])
+            quarters = state_modes[256 * MIXED : 256 * (MIXED + 1), :].rearrange("(j b i) (c w) -> i c j b w", b=4, i=2, c=4)
+            for c in (0, 2, 1, 3):
+                nc.sync.dma_start(out=raw[32 * c : 32 * (c + 1), R:].rearrange("p (b w) -> p b w", b=4), in_=quarters[1, c])
 
         def load_v(q):
             raw = v_raw[q][:].bitcast(BF16)
@@ -204,7 +212,7 @@ def tile_factored_gain_correction_e3_kernel(tc, innov_words, innov_scales, obs_m
             if q not in v_words:
                 v_words[q] = word_tile(P, "v_words")
             cols = slice(512 * halves[0], 512 * (halves[-1] + 1))
-            order_words(engine, v_words[q][:, cols], v_raw[q][:, cols], OCTETS // 4 if q in BY_VECTOR else OCTETS)
+            order_words(engine, v_words[q][:, cols], v_raw[q][:, cols], OCTETS // 4 if q in BY_VECTOR or (q, halves) == (MIXED, (1,)) else OCTETS)
 
         def transpose_v(a):
             v_bank[a] = next_bank()
@@ -224,6 +232,11 @@ def tile_factored_gain_correction_e3_kernel(tc, innov_words, innov_scales, obs_m
             src = v_raw[q][:].rearrange("p (b y u j) -> p y j b u", b=4, y=4, u=2)
             y = slice(2 * tiles[0], 2 * tiles[-1] + 2)
             nc.vector.tensor_copy(out=dst[:, y, :, 2 * half : 2 * half + 2], in_=src[:, y, :, 2 * half : 2 * half + 2])
+
+        def group_mixed(half):
+            dst = group_tile(MIXED)[:, 512:].rearrange("p (r j b u) -> p r j b u", r=2, b=4, u=2)
+            src = v_raw[MIXED][:, 512:].rearrange("p (b r u j) -> p r j b u", b=4, r=2, u=2)
+            nc.vector.tensor_copy(out=dst[:, :, :, 2 * half : 2 * half + 2], in_=src[:, :, :, 2 * half : 2 * half + 2])
 
         def quantize_v(q, halves=(0, 1)):
             lo, hi = 256 * halves[0], 256 * (halves[-1] + 1)
@@ -282,7 +295,10 @@ def tile_factored_gain_correction_e3_kernel(tc, innov_words, innov_scales, obs_m
         for g in range(KG):
             load_words(g, 1)
         for q in range(PAIRS):
-            load_v(q)
+            if q == MIXED:
+                load_mixed()
+            else:
+                load_v(q)
 
         order_words("v", ratio_runs[0:1, :512], ratio_row[:, :512], OCTETS)
         ratio_bank = psum.tile([P, 512], F32, name="ratio_bank", tag="bank7")
@@ -322,7 +338,8 @@ def tile_factored_gain_correction_e3_kernel(tc, innov_words, innov_scales, obs_m
             if t in (1, 2):
                 order_v(1, "s", (t - 1,))
         group_h(1, 0)
-        order_v(2, "v")
+        order_v(MIXED, "v", (0,))
+        order_v(MIXED, "v", (1,))
         quantize_h(1, 0)
         for a in range(4):
             transpose_v(a)
@@ -334,9 +351,12 @@ def tile_factored_gain_correction_e3_kernel(tc, innov_words, innov_scales, obs_m
         group_h(0, 1, 0, H_CUT)
         quantize_v(0, (0,))
         quantize_h(0, 1)
+        turn_blocks(MIXED, 512, 1024)
         sweep_pair(0, 0)
         empty_pair(0, 0)
         quantize_v(0, (1,))
+        group_mixed(0)
+        group_mixed(1)
         sweep_pair(0, 1)
         empty_pair(0, 1)
         quantize_v(1)
@@ -355,11 +375,11 @@ def tile_factored_gain_correction_e3_kernel(tc, innov_words, innov_scales, obs_m
             half_tile(a, 0)
         group_blocks(3, 0)
         group_blocks(3, 1)
-        for a in (4, 5):
-            transpose_v(a)
-            empty_v(a, "vs"[a % 2])
+        transpose_v(2 * MIXED)
+        empty_v(2 * MIXED, "s")
+        quantize_v(MIXED, (1,))
         quantize_v(3)
-        quantize_v(2)
+        quantize_v(MIXED, (0,))
         for a in range(4):
             half_tile(a, 1)
         for q in range(4, PAIRS - 1):
@@ -377,5 +397,5 @@ def tile_factored_gain_correction_e3_kernel(tc, innov_words, innov_scales, obs_m
         group_blocks(q, 1, (1,))
         quantize_v(q, (0,))
         quantize_v(q, (1,))
-        for a in range(4, 2 * PAIRS):
+        for a in (2 * MIXED + 1, 2 * MIXED, *range(6, 2 * PAIRS)):
             whole_tile(a, "ss" if a < 14 else "vs")

from contextlib import ExitStack

import concourse.mybir as mybir
from concourse.masks import make_identity

K, N, R, S = 2048, 1024, 1024, 2048
FLOPS = 2 * K * R * N + 2 * S * R * N

F32 = mybir.dt.float32
BF16 = mybir.dt.bfloat16
U32 = mybir.dt.uint32
I32 = mybir.dt.int32
U8 = mybir.dt.uint8
E4 = mybir.dt.float8_e4m3fn_x4
E5 = mybir.dt.float8_e5m2_x4
COPY = mybir.ActivationFunctionType.Copy
ADD = mybir.AluOpType.add
MULT = mybir.AluOpType.mult

P = 128
KG = K // 512
PAIRS = S // (2 * P)
OCTETS = P // 8
BY_VECTOR = (3, 4, 5, 6, 7)
MIXED = 2
U_SHARES = (10, 8, 10, 8)
H_CUT = 352
WIDE_BUFS = 7
WORD_BUFS = 4
GROUP_BUFS = 3
QUAD_BUFS = 9


def tile_factored_gain_correction_e3_kernel(tc, innov_words, innov_scales, obs_modes, mode_ratio, state_modes, out):
    nc = tc.nc
    v_rows = state_modes.rearrange("(q p i) r -> q p i r", p=P, i=2)
    out_rows = out.rearrange("(q p i) n -> q p i n", p=P, i=2)

    with ExitStack() as ctx:
        keep = ctx.enter_context(tc.tile_pool(name="keep", bufs=1))
        work = ctx.enter_context(tc.tile_pool(name="work", bufs=2))
        psum = ctx.enter_context(tc.psum_pool(name="psum", bufs=1))
        ctx.enter_context(tc.manual_schedule())

        turn = [0]

        def next_bank():
            b = turn[0]
            turn[0] = (b + 1) % 8
            return psum.tile([P, 512], F32, name="bank%d" % b, tag="bank%d" % b)

        def word_tile(rows, name):
            return work.tile([rows, 1024], F32, name=name, tag="words", bufs=WORD_BUFS, align_bytes=256)

        ident = keep.tile([P, P], F32, name="ident", align_bytes=256)
        inverse = keep.tile([P, 4, 2], F32, name="inverse")
        total = keep.tile([P, 4, 2], F32, name="total")
        gain = keep.tile([P, 4, 2], F32, name="gain")
        g_words = {(g, n): keep.tile([P, 512], U32, name="g_words%d_%d" % (g, n), align_bytes=256) for g in range(KG) for n in range(2)}
        g_scales = [keep.tile([P, KG, 512], U8, name="g_scales%d" % n, align_bytes=256) for n in range(2)]
        u_codes = {(g, r): keep.tile([P, 512], U32, name="u_codes%d_%d" % (g, r), align_bytes=256) for g in range(KG) for r in range(2)}
        u_scales = {k: keep.tile([P, 512], U8, name="u_scales%d_%d" % k, align_bytes=256) for k in u_codes}
        v_raw = [keep.tile([P, 1024], F32, name="v_raw%d" % q, align_bytes=256) for q in range(PAIRS)]
        v_codes = [keep.tile([P, 512], U32, name="v_codes%d" % q, align_bytes=256) for q in range(PAIRS)]
        v_scales = [keep.tile([P, 512], U8, name="v_scales%d" % q, align_bytes=256) for q in range(PAIRS)]
        h_codes = {(r, n): keep.tile([P, 512], U32, name="h_codes%d_%d" % (r, n), align_bytes=256) for r in range(2) for n in range(2)}
        h_scales = {k: keep.tile([P, 512], U8, name="h_scales%d_%d" % k, align_bytes=256) for k in h_codes}

        def copy(engine, out, in_):
            if engine == "s":
                nc.scalar.copy(out=out, in_=in_)
            else:
                nc.vector.tensor_copy(out=out, in_=in_)

        def order_words(engine, dst, src, octets):
            copy(engine, dst.rearrange("p (x t q j) -> p x t q j", t=4, q=octets, j=8), src.rearrange("p (x q t j) -> p x t q j", t=4, q=octets, j=8))

        u_raw = {}

        def load_u(g):
            u_raw[g] = work.tile([P, 4, R], BF16, name="u_raw", tag="wide", bufs=WIDE_BUFS, align_bytes=256)
            nc.sync.dma_start(out=u_raw[g][:], in_=obs_modes[512 * g : 512 * (g + 1), :].rearrange("(p k) w -> p k w", k=4))

        def load_words(g, n):
            words = innov_words[g, :, 512 * n : 512 * (n + 1), :].rearrange("p n t -> p (n t)")
            nc.sync.dma_start(out=g_words[g, n][:].bitcast(I32), in_=words.bitcast(I32))

        def load_scales(n):
            scale_rows = innov_scales[:, :, 512 * n : 512 * (n + 1)].rearrange("g (c j) n -> j c g n", j=4)
            for j in range(4):
                nc.sync.dma_start(out=g_scales[n][j:P:32, :, :].bitcast(I32), in_=scale_rows[j].bitcast(I32))

        def load_mixed():
            raw = v_raw[MIXED][:].bitcast(BF16)
            nc.sync.dma_start(out=raw[:, :R], in_=v_rows[MIXED][:, 0, :])
            quarters = state_modes[256 * MIXED : 256 * (MIXED + 1), :].rearrange("(j b i) (c w) -> i c j b w", b=4, i=2, c=4)
            for c in (0, 2, 1, 3):
                nc.sync.dma_start(out=raw[32 * c : 32 * (c + 1), R:].rearrange("p (b w) -> p b w", b=4), in_=quarters[1, c])

        def load_v(q):
            raw = v_raw[q][:].bitcast(BF16)
            if q not in BY_VECTOR:
                nc.sync.dma_start(out=raw.rearrange("p (i r) -> p i r", i=2), in_=v_rows[q])
                return
            quarters = state_modes[256 * q : 256 * (q + 1), :].rearrange("(j y x) (c w) -> y c j x w", y=2, x=4, c=4)
            for y in range(2):
                for c in (0, 2, 1, 3):
                    rows = raw[32 * c : 32 * (c + 1), 1024 * y : 1024 * (y + 1)].rearrange("p (x w) -> p x w", x=4)
                    nc.sync.dma_start(out=rows, in_=quarters[y, c])

        u_group = {}

        def group_u(g, r, u, engine, lo, hi):
            if (g, r) not in u_group:
                u_group[g, r] = work.tile([P, 4, P, 4], BF16, name="u_group", tag="quad", bufs=QUAD_BUFS, align_bytes=256)
            src = u_raw[g][:].rearrange("p k (q r u h j e) -> p r u q h k j e", r=2, u=2, h=4, j=2, e=2)
            dst = u_group[g, r][:].rearrange("p (u e) (q h j) k -> p u q h k j e", u=2, h=4, j=2)
            copy(engine, dst[:, u, lo:hi], src[:, r, u, lo:hi])

        def quantize_u(g, r, lo, hi):
            cols = slice(P * lo, P * hi)
            nc.vector.quantize_mx(
                out=u_codes[g, r][:, cols].bitcast(E4),
                scales=u_scales[g, r][:, cols],
                in_=u_group[g, r][:, lo:hi].rearrange("p t m k -> p (t m k)"),
            )

        z = {}

        def stage1(g, r, n, t):
            if g == 0:
                z[r, n, t] = next_bank()
            cols = slice(P * t, P * (t + 1))
            nc.tensor.matmul_mx(
                out=z[r, n, t][:],
                lhsT=u_codes[g, r][:, cols].bitcast(E4),
                lhsT_scale=u_scales[g, r][:, cols],
                rhs=g_words[g, n][:].bitcast(E5),
                rhs_scale=g_scales[n][:, g, :],
                start=(g == 0),
                stop=(g == KG - 1),
            )

        def sweep_bank(r, n, t):
            for g in range(KG):
                stage1(g, r, n, t)

        def sweep_pair(m, u):
            members = slice(256 * m, 256 * (m + 1))
            z[m, u] = next_bank()
            for e in range(2):
                cols = slice(P * (2 * u + e), P * (2 * u + e + 1))
                for g in range(KG):
                    nc.tensor.matmul_mx(
                        out=z[m, u][:, 256 * e : 256 * (e + 1)],
                        lhsT=u_codes[g, 1][:, cols].bitcast(E4),
                        lhsT_scale=u_scales[g, 1][:, cols],
                        rhs=g_words[g, 1][:, members].bitcast(E5),
                        rhs_scale=g_scales[1][:, g, members],
                        start=(g == 0),
                        stop=(g == KG - 1),
                    )

        h_rows = {}
        h_group = {}

        def empty_pair(m, u):
            if (1, 1) not in h_rows:
                h_rows[1, 1] = work.tile([P, 4, 512], BF16, name="h_pairs", tag="quad", bufs=QUAD_BUFS, align_bytes=256)
            gains = gain[:, 2 + u : 3 + u, :].to_broadcast([P, 256, 2])
            pairs = h_rows[1, 1][:, 2 * m + u, :].rearrange("p (c e) -> p c e", e=2)
            nc.vector.tensor_tensor(out=pairs, in0=z[m, u][:].rearrange("p (e c) -> p c e", e=2), in1=gains, op=MULT)

        def group_pairs(m, engine):
            if (1, 1) not in h_group:
                h_group[1, 1] = work.tile([P, 512, 4], BF16, name="h_group", tag="quad", bufs=QUAD_BUFS, align_bytes=256)
            dst = h_group[1, 1][:, 256 * m : 256 * (m + 1), :].bitcast(F32)
            copy(engine, dst, h_rows[1, 1][:, 2 * m : 2 * m + 2, :].bitcast(F32).rearrange("p u c -> p c u"))

        def empty_z(r, n, t, engine):
            if (r, n) not in h_rows:
                h_rows[r, n] = work.tile([P, 4, 512], BF16, name="h_rows", tag="quad", bufs=QUAD_BUFS, align_bytes=256)
            scale = gain[:, 2 * r + t // 2, t % 2 : t % 2 + 1]
            if engine == "s":
                nc.scalar.activation(out=h_rows[r, n][:, t, :], in_=z[r, n, t][:], func=COPY, scale=scale)
            else:
                nc.vector.tensor_scalar_mul(h_rows[r, n][:, t, :], z[r, n, t][:], scale)

        def group_h(r, n, lo=0, hi=512, engine="v"):
            if (r, n) not in h_group:
                h_group[r, n] = work.tile([P, 512, 4], BF16, name="h_group", tag="quad", bufs=QUAD_BUFS, align_bytes=256)
            src = h_rows[r, n][:, :, lo:hi].rearrange("p t (c i) -> p c t i", i=4)
            copy(engine, h_group[r, n][:, lo:hi].rearrange("p (c i) t -> p c t i", i=4), src)

        def quantize_h(r, n, lo=0, hi=512):
            nc.vector.quantize_mx(
                out=h_codes[r, n][:, lo:hi].bitcast(E5),
                scales=h_scales[r, n][:, lo:hi],
                in_=h_group[r, n][:, lo:hi].rearrange("p n t -> p (n t)"),
            )

        v_words = {}
        v_group = {}
        v_bank = {}

        def group_tile(q):
            if q not in v_group:
                v_group[q] = work.tile([P, 1024], F32, name="v_group", tag="v_group", bufs=GROUP_BUFS, align_bytes=256)
            return v_group[q]

        def order_v(q, engine, halves=(0, 1)):
            if q not in v_words:
                v_words[q] = word_tile(P, "v_words")
            cols = slice(512 * halves[0], 512 * (halves[-1] + 1))
            order_words(engine, v_words[q][:, cols], v_raw[q][:, cols], OCTETS // 4 if q in BY_VECTOR or (q, halves) == (MIXED, (1,)) else OCTETS)

        def transpose_v(a):
            v_bank[a] = next_bank()
            for t in range(4):
                first = 512 * (a % 2) + P * t
                nc.tensor.transpose(v_bank[a][:, P * t : P * (t + 1)], v_words[a // 2][:, first : first + P], ident[:])

        def empty_v(a, engine):
            dst = group_tile(a // 2)[:, 512 * (a % 2) : 512 * (a % 2 + 1)].rearrange("p (r s u) -> p r s u", r=2, u=2)
            copy(engine, dst, v_bank[a][:].rearrange("p (r u s) -> p r s u", r=2, u=2))

        def turn_blocks(q, lo=0, hi=1024):
            nc.vector.transpose(v_raw[q][:, lo:hi], v_words[q][:, lo:hi])

        def group_blocks(q, half, tiles=(0, 1)):
            dst = group_tile(q)[:].rearrange("p (y j b u) -> p y j b u", y=4, b=4, u=2)
            src = v_raw[q][:].rearrange("p (b y u j) -> p y j b u", b=4, y=4, u=2)
            y = slice(2 * tiles[0], 2 * tiles[-1] + 2)
            nc.vector.tensor_copy(out=dst[:, y, :, 2 * half : 2 * half + 2], in_=src[:, y, :, 2 * half : 2 * half + 2])

        def group_mixed(half):
            dst = group_tile(MIXED)[:, 512:].rearrange("p (r j b u) -> p r j b u", r=2, b=4, u=2)
            src = v_raw[MIXED][:, 512:].rearrange("p (b r u j) -> p r j b u", b=4, r=2, u=2)
            nc.vector.tensor_copy(out=dst[:, :, :, 2 * half : 2 * half + 2], in_=src[:, :, :, 2 * half : 2 * half + 2])

        def quantize_v(q, halves=(0, 1)):
            lo, hi = 256 * halves[0], 256 * (halves[-1] + 1)
            nc.vector.quantize_mx(out=v_codes[q][:, lo:hi].bitcast(E4), scales=v_scales[q][:, lo:hi], in_=v_group[q][:, 2 * lo : 2 * hi].bitcast(BF16))

        results = {}

        sums = {}

        def stage2(a, n):
            q, i = a // 2, a % 2
            sums[a, n] = next_bank()
            for r in range(2):
                cols = slice(256 * i + P * r, 256 * i + P * (r + 1))
                nc.tensor.matmul_mx(
                    out=sums[a, n][:],
                    lhsT=v_codes[q][:, cols].bitcast(E4),
                    lhsT_scale=v_scales[q][:, cols],
                    rhs=h_codes[r, n][:].bitcast(E5),
                    rhs_scale=h_scales[r, n][:],
                    start=(r == 0),
                    stop=(r == 1),
                )

        def empty_sum(a, n, engine):
            q, i = a // 2, a % 2
            if q not in results:
                results[q] = work.tile([P, 2, N], F32, name="result", tag="wide", bufs=WIDE_BUFS, align_bytes=256)
            copy(engine, results[q][:, i, 512 * n : 512 * (n + 1)], sums[a, n][:])

        def store(a, lo, hi):
            nc.sync.dma_start(out=out_rows[a // 2][:, a % 2, lo:hi], in_=results[a // 2][:, a % 2, lo:hi])

        def half_tile(a, n):
            stage2(a, n)
            empty_sum(a, n, "s")
            store(a, 512 * n, 512 * (n + 1))

        def whole_tile(a, engines="ss"):
            for n in range(2):
                stage2(a, n)
                empty_sum(a, n, engines[n])
            store(a, 0, N)

        ratio_row = word_tile(1, "ratio_row")
        ratio_runs = word_tile(P, "ratio_runs")
        nc.sync.dma_start(out=ratio_row[:, :512].bitcast(BF16), in_=mode_ratio.rearrange("(o c) -> o c", o=1))
        nc.vector.memset(ratio_runs[:, :512], 0.0)
        make_identity(nc, ident[:])
        for g in range(KG):
            load_u(g)
            load_words(g, 0)
            if g == 0:
                load_scales(0)
        load_scales(1)
        for g in range(KG):
            load_words(g, 1)
        for q in range(PAIRS):
            if q == MIXED:
                load_mixed()
            else:
                load_v(q)

        order_words("v", ratio_runs[0:1, :512], ratio_row[:, :512], OCTETS)
        ratio_bank = psum.tile([P, 512], F32, name="ratio_bank", tag="bank7")
        for t in range(4):
            nc.tensor.transpose(ratio_bank[:, P * t : P * (t + 1)], ratio_runs[:, P * t : P * (t + 1)], ident[:])
        ratio = ratio_bank[:].bitcast(BF16).rearrange("p (t s e) -> p s t e", t=4, e=2)[:, 0]
        nc.vector.reciprocal(inverse[:], ratio)
        nc.vector.tensor_tensor(out=total[:], in0=ratio, in1=inverse[:], op=ADD)
        nc.vector.reciprocal(gain[:], total[:])

        for g in range(KG):
            last = g == KG - 1
            for x in range(4):
                group_u(g, x // 2, x % 2, "s", U_SHARES[x], OCTETS)
            group_u(g, 0, 0, "v", 0, U_SHARES[0])
            for tile in range(8):
                r, t = tile // 4, tile % 4
                if tile in ((0, 2, 5) if last else (0, 2, 4)):
                    x = tile // 2 + 1
                    group_u(g, x // 2, x % 2, "v", 0, U_SHARES[x])
                if last:
                    quantize_u(g, r, t, t + 1)
                elif t % 2 == 0:
                    quantize_u(g, r, t, t + 2)
                stage1(g, r, 0, t)

        for t in range(4):
            empty_z(0, 0, t, "ssvv"[t])
        for t in range(4):
            empty_z(1, 0, t, "s")
        group_h(0, 0)
        order_v(0, "v")
        quantize_h(0, 0)
        for t in range(4):
            sweep_bank(0, 1, t)
            empty_z(0, 1, t, "s")
            if t in (1, 2):
                order_v(1, "s", (t - 1,))
        group_h(1, 0)
        order_v(MIXED, "v", (0,))
        order_v(MIXED, "v", (1,))
        quantize_h(1, 0)
        for a in range(4):
            transpose_v(a)
            empty_v(a, "s")
            if a == 0:
                group_h(0, 1, H_CUT, 512, "s")
        order_v(3, "s")
        order_v(4, "s")
        group_h(0, 1, 0, H_CUT)
        quantize_v(0, (0,))
        quantize_h(0, 1)
        turn_blocks(MIXED, 512, 1024)
        sweep_pair(0, 0)
        empty_pair(0, 0)
        quantize_v(0, (1,))
        group_mixed(0)
        group_mixed(1)
        sweep_pair(0, 1)
        empty_pair(0, 1)
        quantize_v(1)
        group_pairs(0, "s")
        sweep_pair(1, 0)
        empty_pair(1, 0)
        turn_blocks(3, 0, 512)
        sweep_pair(1, 1)
        empty_pair(1, 1)
        quantize_h(1, 1, 0, 256)
        group_pairs(1, "v")
        turn_blocks(3, 512, 1024)
        quantize_h(1, 1, 256, 512)

        for a in range(4):
            half_tile(a, 0)
        group_blocks(3, 0)
        group_blocks(3, 1)
        transpose_v(2 * MIXED)
        empty_v(2 * MIXED, "s")
        quantize_v(MIXED, (1,))
        quantize_v(3)
        quantize_v(MIXED, (0,))
        for a in range(4):
            half_tile(a, 1)
        for q in range(4, PAIRS - 1):
            turn_blocks(q)
            order_v(q + 1, "v", (0,))
            group_blocks(q, 0)
            group_blocks(q, 1)
            order_v(q + 1, "v", (1,))
            quantize_v(q)
        q = PAIRS - 1
        turn_blocks(q, 0, 512)
        turn_blocks(q, 512, 1024)
        group_blocks(q, 0)
        group_blocks(q, 1, (0,))
        group_blocks(q, 1, (1,))
        quantize_v(q, (0,))
        quantize_v(q, (1,))
        for a in (2 * MIXED + 1, 2 * MIXED, *range(6, 2 * PAIRS)):
            whole_tile(a, "ss" if a < 14 else "vs")
